import numpy as np, ml_dtypes
CORES = [3,11,19,27,35,43,51,59]
N = 8
import mx_ref
BF = ml_dtypes.bfloat16
def gentries(a):
    return np.ascontiguousarray(a.reshape(8, 16, -1).transpose(0, 2, 1)).reshape(8, -1)
def gtable(e):
    e = np.asarray(e); return np.ascontiguousarray(e.reshape(8, -1, 16).transpose(0, 2, 1)).reshape(128, -1).astype(np.int32)
def gcols(t, e):
    v = np.concatenate([t.reshape(8, 16, -1, 4), np.zeros((8, 16, 1, 4), BF)], axis=2)
    return np.ascontiguousarray(np.stack([v[g][:, e[g]] for g in range(8)])).reshape(128, -1)
def tile(rs):
    return np.stack(rs, axis=2).reshape(128, -1).astype(BF)
def cut(t, i, w=512):
    return t[:, w * i:w * i + w]
def pick(q, e):
    c = np.concatenate([q[0].reshape(128, -1, 4), np.zeros((128, 1, 4), np.uint8)], axis=1); s = np.concatenate([q[1], np.ones((16, 1), np.uint8)], axis=1)
    return (np.ascontiguousarray(c[:, e].reshape(128, -1)), np.ascontiguousarray(s[:, e]))
def join(*qs):
    return (np.concatenate([q[0] for q in qs], axis=1), np.concatenate([q[1] for q in qs], axis=1))
def put(q, e, v):
    c, s = q[0].reshape(128, -1, 4).copy(), q[1].copy(); c[:, e] = v[0].reshape(128, -1, 4); s[:, e] = v[1]
    return (c.reshape(128, -1), s)
def pk(c, s):
    return (np.ascontiguousarray(c), mx_ref.live(s))
def emit(q):
    return q[0], q[1]
def packed(v, rng):
    q = [mx_ref.quantize(np.ascontiguousarray(v[r])) for r in range(N)]
    return np.stack([a for a, b in q]), np.stack([mx_ref.plane(b, rng) for a, b in q])
def values_of_codes():
    e, c = np.zeros((128, 128, 4), np.float32), np.zeros((128, 2, 4), np.uint8)
    e[np.arange(128), np.arange(128), 0] = 1
    c[:127, :, 0] = np.arange(256).reshape(2, 128).T[:127]
    return mx_ref.matmul(mx_ref.quantize(e.reshape(128, 512).astype(BF)), (c.reshape(128, 8), np.full((16, 2), 127, np.uint8))).T.reshape(-1).astype(np.float64)
CODE_VALUE, SCALE_VALUE = values_of_codes(), 2.0 ** (np.arange(256) - 127.0)
def decode(q):
    return (CODE_VALUE[q[0]].reshape(16, 8, -1, 4) * SCALE_VALUE[q[1]][:, None, :, None] + 0.0).reshape(128, -1).astype(np.float32)
def f(rng, *shape):
    return mx_ref.flush((rng.standard_normal(shape, dtype=np.float32) * np.exp2(rng.integers(-2, 3, shape[:-1] + (1,)))).astype(BF))
def wide(rng, *shape, cols=0):
    v = rng.standard_normal(shape, dtype=np.float32) * np.exp2(rng.integers(-12, 13, shape)).astype(np.float32)
    if cols: v *= np.repeat(np.exp2(rng.integers(-cols, cols + 1, shape[:-2] + (1, shape[-1] // 4))) * (rng.random(shape[:-2] + (1, shape[-1] // 4)) > 0.0625), 4, axis=-1).astype(np.float32)
    return mx_ref.flush(v.astype(BF))
C, A, R, T = 224, 96, 3, 7
STEP = [1, 2, 4]
def turn(p, s):
    at = np.argmax((s + np.float32(0.0)).reshape(8, T, 32), axis=2) + 32 * np.arange(T)
    back, on, new, way = at, np.ones((8, T), bool), p.copy(), np.full((8, T, 32), -1)
    for i in range(32):
        way[:, :, i] = np.where(on, at, -1)
        np.put_along_axis(new, at, back, axis=1)
        up = np.take_along_axis(p, at, axis=1)
        back = np.where(up == at, back, at)
        on = on & (up != at)
        at = up
    slot, home = np.full((8, A), -1), np.full((8, C), -1)
    for g in range(8):
        n = 0
        for k in range(T):
            w = way[g, k][way[g, k] >= 0][:A - n]
            slot[g, n:n + len(w)] = w
            home[g, w] = n + len(w) - 1 - np.arange(len(w))
            n += len(w)
    return new, slot, home
def numbers_of(rng):
    return {"x": np.array(f(rng, N, 128, 4 * C)), "u": np.array(f(rng, N, 128, 512)), "v": np.array(f(rng, N, 128, 512))}
def packing(rng, w):
    c, p = packed(w, rng)
    return {"wc": c, "ws": p}
def weights(rng, off=None, deaf=False):
    w = np.array(f(rng, N, 128, 2048)).reshape(N, 128, 4, 128, 4)
    if off is not None:
        w[:, :, :, off] = 0
        if deaf: w[:, off] = 0
    return packing(rng, w.reshape(N, 128, 2048))
def forest(rng):
    o = np.argsort(rng.random((N, 8, T, 32)), axis=3)
    i = np.arange(32)
    n = rng.choice([1, 2, 3, 32], (N, 8, T, 1))
    b = np.minimum(1 + rng.integers(0, n, o.shape), i)
    p = np.zeros_like(o)
    np.put_along_axis(p, o, np.take_along_axis(o, i - b, axis=3), axis=3)
    return p
def stored(p):
    return np.stack([gtable((p[r] + 32 * np.arange(T)[:, None]).reshape(8, C)) for r in range(N)])
def signs(rng):
    return np.stack([rng.permutation(8) % 2 * 2.0 - 1.0 for r in range(N)])
def setup_inputs(rng):
    return {**numbers_of(rng), "par": stored(forest(rng)), **weights(rng)}
def setup_inputs_ties(rng):
    d = numbers_of(rng)
    e = rng.permutation(N)
    x = d["x"].reshape(N, 8, 16, C, 4)
    for r in range(N):
        k = rng.permutation(C) % 3
        if e[r] == 0: k[:] = 0
        a = x[r][:, :8, :3].copy()
        a[:, :, 2] = 0
        if e[r] == 1: a[:] = 0
        x[r][:, :8] = a[:, :, k]
    u = d["u"].reshape(N, 8, 16, 128, 4)
    for t in range(R): u[:, :, 8:, t::16] = 0
    return {"x": x.reshape(N, 128, 4 * C), "u": u.reshape(N, 128, 512), "v": d["v"], "par": stored(forest(rng)), **weights(rng, np.arange(128) % 16 < 8)}
def setup_inputs_near(rng):
    d = numbers_of(rng)
    x = d["x"].astype(np.float32).reshape(N, 8, 16, C, 4)
    s = np.argsort(rng.random((N, 8, R, T, 32)), axis=4) // 2
    up = (np.arange(N)[:, None, None] + np.arange(8)[:, None] + np.arange(R)) % 2 == int(rng.integers(2))
    s = np.where(up[..., None, None], np.arange(32) // 2, s).reshape(N, 8, R, C)
    x[:, :, 0] = 0
    x[:, :, 0, :, 0] = signs(rng)[:, :, None]
    x[:, :, 8:8 + R] = ((s[..., None] >> np.arange(4)) & 1) * np.exp2(np.arange(4) - 23.0)
    x[:, :, 8 + R:] = rng.integers(4, 8, (N, 8, 8 - R, C, 4)) * rng.choice([-1.0, 1.0], (N, 8, 8 - R, C, 4)) * 2.0 ** -20
    for g in rng.permutation(8)[:4]:
        x[:, int(g), 0, 32 * np.arange(T) + rng.integers(0, 32, T), 0] = -2.0 ** 30
    k = np.where(rng.permutation(N) < N // 2, 2.0 ** -30, 1.0).astype(np.float32).astype(BF)
    u = d["u"].reshape(N, 128, 128, 4)
    for t in range(R):
        u[:, :, t::16] = 0
        for h in range(0, 128, 16):
            u[:, h, h + t, 0] = k
            u[:, h + 8 + t, h + t] = k[:, None]
    i = np.arange(128) % 16
    return {"x": x.reshape(N, 128, 4 * C).astype(BF), "u": u.reshape(N, 128, 512), "v": d["v"], "par": stored(forest(rng)), **weights(rng, (i == 0) | (i >= 8), True)}
def setup_inputs_shapes(rng):
    d, p = numbers_of(rng), forest(rng)
    e, q = rng.permutation(N), int(rng.integers(8))
    x = d["x"].reshape(N, 8, 16, C, 4)
    u = d["u"].reshape(N, 128, 128, 4)
    for t in range(R): u[:, :, t::16] = 0
    for r in range(N):
        kinds = rng.permutation(8)
        if e[r] == 0: kinds[:] = 4
        if e[r] == 1: kinds[:] = 3
        chain = np.argsort(rng.random((8, T, 32)), axis=2)
        for g in range(8):
            h, at = int(kinds[g]), np.zeros(T, int)
            if h < 7: np.put_along_axis(p[r, g], chain[g], chain[g][:, np.maximum(np.arange(32) - 1, 0)], axis=1)
            if h == 7: chain[g, :, 0] = np.argmax(p[r, g] == np.arange(32), axis=1)
            for t in range(R):
                if h < 3:
                    cutoff = rng.permutation(np.repeat(np.arange(T), 16))[:17 * T - (A, A + 1, A - 1)[h]]
                    n = 16 - np.bincount(cutoff, minlength=T)
                    at = np.where((at + n <= 31) & ((at < n) | (rng.random(T) < 0.5)), at + n, at - n)
                elif h in (4, 5):
                    at = 31 - at
                    if h == 5: at[0] = int(rng.integers(32))
                elif h > 5: at = rng.integers(0, 32, T)
                low = int(rng.integers(2))
                mark = -rng.integers(2, 4, C).astype(np.float32) if low else rng.integers(-1, 2, C).astype(np.float32)
                mark[32 * np.arange(T) + chain[g, np.arange(T), at]] = (2.0, -1.0)[low]
                k = R * g + t
                x[r, q, k // 4, :, k % 4] = mark.astype(BF)
                u[r, 16 * q + k // 4, 16 * g + t, k % 4] = 1.0
    return {"x": x.reshape(N, 128, 4 * C), "u": u.reshape(N, 128, 512), "v": d["v"], "par": stored(p), **weights(rng, np.arange(128) // 8 == 2 * q)}
def setup_inputs_huge(rng):
    d = numbers_of(rng)
    x = 2.0 ** 30 * (0.6 + 0.35 * rng.random((N, 128, C, 4)))
    mixed = rng.permutation(N) < N // 2
    side = (np.argsort(rng.random((N, T, 32)), axis=2) % 2).reshape(N, C)
    first = np.arange(128) % 16 < 8
    x *= (~mixed[:, None, None] | (first[None, :, None] == (side[:, None, :] == 1)))[..., None]
    u = d["u"].reshape(N, 128, 128, 4)
    for t in range(R):
        c = signs(rng)[:, None, :] * np.where(mixed[:, None, None] & ~first[None, :, None], -1.0, 1.0)
        u[:, :, t::16] = (2.0 ** 30 * (0.75 + 0.25 * rng.random((N, 128, 8, 4))) * c[..., None]).astype(np.float32).astype(BF)
    w = np.zeros((N, 128, 4, 128, 4), np.float32)
    i = np.arange(128)
    for b in range(4): w[:, i, b, i, b] = 0.125
    return {"x": x.astype(np.float32).reshape(N, 128, 4 * C).astype(BF), "u": u.reshape(N, 128, 512), "v": d["v"], "par": stored(forest(rng)), **packing(rng, w.reshape(N, 128, 2048).astype(BF))}
def setup_inputs_spread(rng):
    d = setup_inputs(rng)
    d["x"] = wide(rng, N, 128, 4 * C, cols=6)
    return d
def check_inputs(d):
    b = []
    for k in ("x", "u", "v"):
        a = np.abs(d[k].astype(np.float32))
        if not (np.isfinite(a).all() and ((a == 0) | (a >= 2.0 ** -30) & (a <= 2.0 ** 30)).all()): b.append("a value of " + k)
    if np.isin(d["wc"], [127, 255]).any(): b.append("wc: a code that is no number")
    for r in range(N):
        a = np.abs(decode(pk(d["wc"][r], d["ws"][r])))
        if not ((a == 0) | (a >= 2.0 ** -30) & (a <= 2.0 ** 30)).all(): b.append("wc and ws: a number out of range")
        p = gentries(d["par"][r]).astype(np.int64)
        if (p // 32 != np.arange(C) // 32).any():
            b.append("par: a parent outside the tree")
            continue
        a = p
        for i in range(5): a = np.take_along_axis(a, a, axis=1)
        z = a.reshape(8, T, 32)
        if (z != z[:, :, :1]).any() or (np.take_along_axis(p, a, axis=1) != a).any(): b.append("par: a tree without one root that all its nodes come to")
    return b
def reference(x, u, v, par, wc, ws):
    qu = [mx_ref.quantize(u[r]) for r in range(N)]
    lay = [pk(wc[r], ws[r]) for r in range(N)]
    now = [x[r] for r in range(N)]
    parent = [gentries(par[r]).astype(np.int64) for r in range(N)]
    for t in range(R):
        sent, homes, made = [], [], []
        for r in range(N):
            q = mx_ref.quantize(now[r])
            parent[r], slot, home = turn(parent[r], mx_ref.matmul(qu[r], q)[t::16])
            homes.append(home)
            sent.append(mx_ref.quantize(gcols(decode(q).astype(BF), slot)))
        for r in range(N):
            p = sent[r ^ STEP[t]]
            h = tile([np.maximum(mx_ref.matmul(pick(lay[r], np.arange(128 * b, 128 * b + 128)), p), np.float32(0.0)) * np.float32(0.03125) for b in range(4)])
            made.append(mx_ref.quantize(h))
        came = decode(join(*made)).astype(BF)
        for r in range(N):
            got = gcols(cut(came, r ^ STEP[t], 4 * A), homes[r])
            now[r] = (now[r].astype(np.float32) + got.astype(np.float32)).astype(BF)
    y, op = np.zeros((N, 128, C), np.float32), np.zeros((N, 8, C), np.float32)
    oc, osc = np.zeros((N, 128, 4 * C), np.uint8), np.zeros((N, 16, C), np.uint8)
    for r in range(N):
        q = mx_ref.quantize(now[r])
        y[r] = mx_ref.matmul(mx_ref.quantize(v[r]), q)
        op[r] = parent[r]
        oc[r], osc[r] = emit(q)
    return {"y": y, "op": op, "oc": oc, "osc": osc}

@@ -1,0 +1,475 @@
+from concourse.mybir import dt, AluOpType as Op, ActivationFunctionType as Act
+
+C, A, R = 224, 96, 3
+STEP = [1, 2, 4]
+F32, BF, I32, U16, MX, U8 = "float32", "bfloat16", "int32", "uint16", "float8_e4m3fn_x4", "uint8"
+KEEP, DROP = 1000.0, -1.0e6
+HUGE = 1.0e29
+LIFT = 256.0
+BASE = 64.0
+
+
+def _sb(n, t):
+    return ("sbuf", [128, n], t)
+
+
+SCRATCH = {
+    "par_i": _sb(14, I32), "ut": _sb(512, BF), "vt": _sb(512, BF),
+    "wq": _sb(512, MX), "wsc": _sb(512, U8),
+    "uq": _sb(128, MX), "us": _sb(128, U8), "upq": _sb(384, MX), "ups": _sb(384, U8),
+    "vq": _sb(128, MX), "vs": _sb(128, U8),
+    "ez": _sb(520, BF), "eone": _sb(128, BF), "eq": _sb(512, MX), "es": _sb(512, U8),
+    "xy0": _sb(1280, BF), "xy1": _sb(1280, BF), "xy2": _sb(1280, BF), "xy3": _sb(896, BF),
+    "dx": _sb(912, BF), "pt": _sb(512, BF), "pq": _sb(128, MX), "psc": _sb(128, U8),
+    "ht": _sb(512, BF), "xs": _sb(384, BF),
+    "fout": _sb(72, U16), "fin": _sb(72, U16),
+    "ci": _sb(8, I32), "pc": _sb(2, I32), "cf": _sb(8, F32), "cg": _sb(24, F32),
+    "tb": _sb(8 * C, F32), "p8": _sb(C, F32), "p16": _sb(C, F32), "p8b": _sb(C, F32), "idb": _sb(C, F32),
+    "da": _sb(C, F32), "db": _sb(C, F32), "dg": _sb(C, F32), "mk2": _sb(C, F32), "nc": _sb(C, F32),
+    "idw": _sb(14, F32), "e1": _sb(14, F32), "e2": _sb(14, F32), "pm": _sb(14, F32), "el": _sb(14, U16),
+    "aw": _sb(464, F32), "uw0": _sb(464, F32), "uw1": _sb(464, F32),
+    "wl": _sb(80, U16), "sc": _sb(C, F32), "sc2": _sb(C, F32),
+    "s16": _sb(16, F32), "s4": _sb(8, F32), "c16": _sb(C, F32), "c4": _sb(C, F32),
+    "cl": _sb(64, U16), "ul_i": _sb(24, I32), "ul": _sb(24, U16),
+    "cs1": _sb(C, F32), "tp": _sb(C, F32), "ta": _sb(128, F32), "kt": _sb(8, F32),
+    "rr": _sb(C + 8, F32), "nn": _sb(C, F32), "sel": _sb(C, F32),
+    "l1": _sb(2, U16), "l2": _sb(32, U16), "gu": _sb(32, F32), "ee": _sb(32, F32), "ab": _sb(32, F32),
+    "nv": _sb(48, F32), "nt": _sb(48, F32), "nm": _sb(48, F32), "i48a": _sb(48, F32), "i48b": _sb(48, F32),
+    "vv": _sb(48, F32), "fl": _sb(48, F32), "cs": _sb(48, F32), "cw": _sb(6, U16),
+    "rs": _sb(544, F32), "fr": _sb(192, F32), "f4": _sb(A, F32),
+    "am": _sb(8, F32), "val": _sb(8, F32), "mw": _sb(6, U16), "mr": _sb(A, F32), "m16": _sb(6, U16), "m4": _sb(24, U16),
+    "hr": _sb(320, F32), "hw": _sb(56, U16),
+    "k64": _sb(14, F32), "lrf": _sb(14, F32), "cw3": _sb(14, F32), "drn": _sb(8, F32), "mlf": _sb(14, F32), "ml": _sb(14, U16),
+    "ml1f": _sb(14, F32), "ml1": _sb(14, U16), "mark": _sb(C, F32), "rev": _sb(C, F32),
+    "yo": _sb(C, F32),
+    "ps": ("psum", [128, 4096], F32),
+}
+for _t in range(R + 1):
+    SCRATCH["xq%d" % _t] = _sb(C, MX)
+    SCRATCH["xsc%d" % _t] = _sb(C, U8)
+for _t in range(R):
+    SCRATCH["aq%d" % _t] = _sb(C, MX)
+    SCRATCH["asc%d" % _t] = _sb(C, U8)
+    SCRATCH["hq%d" % _t] = _sb(128 + A, MX)
+    SCRATCH["hsc%d" % _t] = _sb(128 + A, U8)
+
+SEMAPHORES = (["nv", "ns", "np", "ng", "ld_par", "ld_x", "ld_u", "ld_w", "ld_v", "stored", "sent"]
+              + ["ax%d" % t for t in range(R)] + ["al%d" % t for t in range(R)] + ["ah%d" % t for t in range(R)])
+
+
+def rank_program(g, core, T, topo):
+    rank = T.rank_of(core)
+    if rank is None:
+        return
+    Q = {"v": g.vector, "s": g.scalar, "p": g.tensor, "g": g, "y": g.sync}
+    CNT = {"v": "nv", "s": "ns", "p": "np", "g": "ng"}
+    count = {k: 0 for k in CNT}
+    clock = {k: {} for k in Q}
+    wrote, readers = {}, {}
+
+    def wait(q, ev):
+        sem, val, clk = ev
+        if clock[q].get(sem, 0) >= val:
+            return
+        Q[q].wait_ge(T.sem[sem], val)
+        clock[q][sem] = val
+        for k, x in clk.items():
+            if clock[q].get(k, 0) < x:
+                clock[q][k] = x
+
+    def order(q, rd, wr):
+        evs = [wrote[k] for k in rd if k in wrote] + [wrote[k] for k in wr if k in wrote]
+        for k in wr:
+            evs += readers.get(k, [])
+        top = {}
+        for ev in evs:
+            if ev[0] not in top or top[ev[0]][1] < ev[1]:
+                top[ev[0]] = ev
+        for ev in sorted(top.values(), key=lambda e: -len(e[2])):
+            wait(q, ev)
+
+    def note(ev, rd, wr):
+        for k in rd:
+            readers.setdefault(k, []).append(ev)
+        for k in wr:
+            wrote[k] = ev
+            readers[k] = []
+
+    def op(q, fn, rd, wr):
+        rd, wr = rd.split(), wr.split()
+        order(q, rd, wr)
+        fn().then_inc(T.sem[CNT[q]], 1)
+        count[q] += 1
+        note((CNT[q], count[q], dict(clock[q])), rd, wr)
+
+    def dma(q, out, in_, sem, val, rd, wr):
+        rd, wr = rd.split(), wr.split()
+        order(q, rd, wr)
+        Q[q].dma_start(out, in_).then_inc(T.sem[sem], 16)
+        note((sem, val, dict(clock[q])), [], wr)
+
+    V, S, P = g.vector, g.scalar, g.tensor
+
+    def ts(out, in0, s1, op0, s2=None, op1=None, rd="", wr=""):
+        if op1 is None:
+            op("v", lambda: V.tensor_scalar(out, in0, s1, None, op0), rd, wr)
+        else:
+            op("v", lambda: V.tensor_scalar(out, in0, s1, s2, op0, op1), rd, wr)
+
+    def tt(out, a, b, o, rd, wr):
+        op("v", lambda: V.tensor_tensor(out, a, b, o), rd, wr)
+
+    def cp(out, a, rd, wr):
+        op("v", lambda: V.tensor_copy(out, a), rd, wr)
+
+    def scan(out, d0, d1, init, o0, o1, rd, wr):
+        op("v", lambda: V.tensor_tensor_scan(out, d0, d1, init, o0, o1), rd, wr)
+
+    def fill(ap, x, wr):
+        op("v", lambda: V.memset(ap, x), "", wr)
+
+    def quant(q, s, src, rd, wr):
+        op("v", lambda: V.quantize_mx(q, s, src), rd, wr)
+
+    def act(out, a, rd, wr, func=None, bias=None, scale=None):
+        kw = {}
+        if bias is not None:
+            kw["bias"] = bias
+        if scale is not None:
+            kw["scale"] = scale
+        f = func if func is not None else (Act.Identity if kw else Act.Copy)
+        op("s", lambda: S.activation(out, a, f, **kw), rd, wr)
+
+    def iota(out, pat, base, cm, wr, fl=True):
+        if fl:
+            op("g", lambda: g.iota(out, pat, base, cm, allow_small_or_imprecise_dtypes=True), "", wr)
+        else:
+            op("g", lambda: g.iota(out, pat, base, cm), "", wr)
+
+    def mm(bank, n, lq, ls, rq, rs, rd):
+        op("p", lambda: P.matmul_mx(T.ps[:, 512 * bank:512 * bank + n], lq, ls, rq, rs, True, True), rd, "b%d" % bank)
+
+    def bank(b, a, z):
+        return T.ps[:, 512 * b + a:512 * b + z]
+
+    nsent = [0]
+
+    def send(t, out, in_, sem, rd):
+        peer = T.cores[rank ^ STEP[t]]
+        rid, pid, se = topo.addr(peer)
+        order("g", rd.split(), [])
+        g.remote_dma(out, in_, T.sem[sem], T.sem.sent, pid, rid, topo.mask(core, peer))
+        nsent[0] += len(topo.engines(core, peer))
+
+    def arrival(t, sem, calls, key):
+        peer = T.cores[rank ^ STEP[t]]
+        wrote[key] = (sem, calls * len(topo.engines(peer, core)), {})
+
+    def tbl(i):
+        return T.tb[:, C * i:C * i + C]
+
+    def wl(i):
+        return T.wl[:, 16 * i:16 * i + 14]
+
+    ident = tbl(0)
+    q_, kq, hh, s8, bit, hi2 = [T.cf[:, i:i + 1] for i in range(6)]
+    (off16, n32, nb, y224, mul, lo, off4, b0, b1, c9, c10, c11, c12, c13, c14, c15, c16, c17, c18,
+     offl) = [T.cg[:, i:i + 1] for i in range(20)]
+    Lq, Lh, LA, LB, LK, Lrev = T.cl[:, 0:14], T.cl[:, 14:28], T.cl[:, 28:31], T.cl[:, 32:35], T.cl[:, 36:39], T.cl[:, 40:54]
+    XY = [T.xy0, T.xy1, T.xy2, T.xy3]
+
+    dma("y", T.par_i[:], T.par[:], "ld_par", 16, "", "par_i")
+    dma("s", T.xy0[:, 0:896], T.x[:], "ld_x", 16, "", "x0")
+    dma("y", T.ut[:], T.u[:], "ld_u", 16, "", "ut")
+    dma("y", T.wq[:].bitcast(dt.uint8), T.wc[:], "ld_w", 32, "", "wq")
+    dma("y", T.wsc[:], T.ws[:], "ld_w", 32, "", "wsc")
+    dma("y", T.vt[:], T.v[:], "ld_v", 16, "", "vt")
+
+    iota(T.pc[:, 0:1], [[0, 1]], 0, 1, "pc", False)
+    iota(ident, [[1, C]], 0, 0, "t0")
+    fill(T.eone[:], 1.0, "eone")
+    fill(T.ez[:], 0.0, "ez")
+    op("g", lambda: g.affine_select(T.ez[:, 3:515:4], T.eone[:], [[-1, 128]], Op.is_equal, 0.0, 0, 1), "eone", "ez")
+    iota(T.kt[:], [[0, 2], [1, 4]], 0, 0, "kt")
+    iota(T.ul_i[:], [[1, 3], [16, 8]], 0, 0, "ul_i", False)
+    iota(T.i48a[:], [[16, 6], [0, 8]], 0, 0, "i48a")
+    iota(T.i48b[:], [[16, 6], [-64, 8]], 448, 0, "i48b")
+    iota(T.ee[:], [[0, 8], [-97, 4]], 97, 0, "ee")
+    iota(T.aw[:, 448:464], [[0, 16]], int(LIFT), 0, "aw2")
+    iota(T.uw0[:, C:464], [[0, 240]], 0, 0, "uw0b")
+    iota(T.rs[:, 448:544], [[0, 96]], C, 0, "rsz")
+    for i, (sh, m) in enumerate([(0, 15), (2, 3), (0, 3), (0, 7), (3, 1), (1, 1)]):
+        ts(T.ci[:, i:i + 1], T.pc[:, 0:1], sh, Op.logical_shift_right, m, Op.bitwise_and, "pc", "ci%d" % i)
+    cp(T.cf[:, 0:6], T.ci[:, 0:6], "ci0 ci1 ci2 ci3 ci4 ci5", "cf")
+    ts(T.s16[:], T.tb[:, 0:16], q_, Op.is_equal, DROP, Op.mult, "t0 cf", "s16")
+    ts(Lq, T.tb[:, 0:14], 0.0, Op.mult, q_, Op.add, "t0 cf", "Lq")
+    ts(T.s4[:], T.tb[:, 0:8], kq, Op.is_equal, DROP, Op.mult, "t0 cf", "s4")
+    ts(Lh, T.tb[:, 0:14], 0.0, Op.mult, hh, Op.add, "t0 cf", "Lh")
+    act(n32, kq, "cf", "n32", scale=-32.0)
+    act(nb, bit, "cf", "nb", scale=-1.0, bias=1.0)
+    act(y224, s8, "cf", "y224", scale=float(C), bias=LIFT)
+    act(T.c16[:], T.s16[:].indirect(Lq), "s16 Lq", "c16", bias=KEEP)
+    act(T.ta[:], T.tb[:, 0:128], "t0 n32", "ta", func=Act.Relu, bias=n32)
+    act(T.idb[:], ident, "t0 nb y224", "idb", scale=nb, bias=y224)
+    act(T.tp[:, 0:128], T.ta[:], "ta", "tpa", scale=-1.0, bias=200.0)
+    act(T.tp[:, 128:C], T.ta[:, 0:96], "ta", "tpb", scale=-1.0, bias=372.0)
+    act(T.c4[:], T.s4[:].indirect(Lh), "s4 Lh", "c4", bias=KEEP)
+    act(T.nt[:], T.i48a[:], "i48a cf", "nt", bias=q_)
+    act(T.nv[:], T.i48b[:], "i48b cf", "nv", bias=q_)
+    ts(off16, q_, KEEP, Op.mult, -15 * KEEP, Op.add, "cf", "off16")
+    fill(T.cs1[:], 0.0, "cs1")
+    ts(mul, hi2, -1.0, Op.add, rd="cf", wr="mul")
+    ts(lo, hi2, -1.0, Op.mult, 1.0, Op.add, "cf", "lo")
+    ts(c9, hh, float(C), Op.mult, 200.0, Op.add, "cf", "c9")
+    ts(c10, hh, 446.0, Op.add, rd="cf", wr="c10")
+    ts(T.cs1[:, 0:C:32], T.kt[:, 0:7], kq, Op.is_equal, -3 * HUGE, Op.mult, "kt cf", "cs1")
+    ts(c11, kq, 32.0, Op.mult, c9, Op.add, "cf c9", "c11")
+    ts(c12, kq, 2.0, Op.mult, c10, Op.add, "cf c10", "c12")
+    ts(c14, lo, 292.0, Op.mult, 8.0, Op.add, "lo", "c14")
+    ts(T.cs1[:, 31:C:32], T.kt[:, 0:7], kq, Op.is_equal, HUGE, Op.mult, "kt cf", "cs1")
+    ts(c13, c11, c12, Op.subtract, lo, Op.mult, "c11 c12 lo", "c13")
+    ts(c15, s8, -4.0, Op.mult, 28.0, Op.add, "cf", "c15")
+    ts(c16, s8, -4.0, Op.mult, 25.0, Op.add, "cf", "c16c")
+    ts(c17, hh, -12 * KEEP, Op.add, rd="cf", wr="c17")
+    ts(b0, c13, c12, Op.add, rd="c13 c12", wr="b0")
+    ts(b1, c13, c12, Op.add, c14, Op.add, "c13 c12 c14", "b1")
+    ts(LA, T.tb[:, 0:3], 0.0, Op.mult, c15, Op.add, "t0 c15", "LA")
+    ts(LB, T.tb[:, 0:3], 0.0, Op.mult, c16, Op.add, "t0 c16c", "LB")
+    ts(off4, kq, 4 * KEEP, Op.mult, c17, Op.add, "cf c17", "off4")
+    cp(wl(0), T.par_i[:], "par_i", "w0")
+    act(tbl(1), ident.indirect(wl(0)), "t0 w0", "t1")
+    act(tbl(2), tbl(1).indirect(wl(0)), "t1 w0", "t2")
+    cp(T.ul[:], T.ul_i[:], "ul_i", "ul")
+    ts(T.idw[:], T.tb[:, 0:14], 16.0, Op.mult, q_, Op.add, "t0 cf", "idw")
+    ts(T.pm[:], T.par_i[:], off16, Op.subtract, rd="par_i off16", wr="pm")
+    tt(T.e1[:], T.par_i[:], T.idw[:], Op.is_equal, "par_i idw", "e1")
+    fill(T.rr[:, 0:8], 0.0, "rr0")
+    fill(T.ab[:], 0.0, "ab")
+    ts(T.ee[:], T.ee[:], 0.0, Op.max, rd="ee", wr="ee")
+
+    def quant_e(b):
+        quant(T.eq[:, 128 * b:128 * b + 128], T.es[:, 128 * b:128 * b + 128], T.ez[:, 3 - b:515 - b], "ez", "e%d" % b)
+
+    def quant_x(t):
+        quant(T["xq%d" % t][:], T["xsc%d" % t][:], XY[t][:, 0:896], "x%d x%db" % (t, t), "xq%d" % t)
+
+    def send_x(t):
+        send(t, T["aq%d" % t][:].bitcast(dt.uint8), T["xq%d" % t][:].bitcast(dt.uint8), "ax%d" % t, "xq%d" % t)
+        send(t, T["asc%d" % t][:], T["xsc%d" % t][:], "ax%d" % t, "xq%d" % t)
+        arrival(t, "ax%d" % t, 2, "aq%d" % t)
+
+    def pick_u(t):
+        lst = T.ul[:, 8 * t:8 * t + 8]
+        cp(T.upq[:, 128 * t:128 * t + 128].bitcast(dt.uint32), T.uq[:].bitcast(dt.uint32).indirect(lst), "uq ul", "upq%d" % t)
+        act(T.ups[:, 128 * t:128 * t + 128], T.us[:].indirect(lst), "uq ul", "ups%d" % t)
+
+    def scores(t):
+        mm(7, C, T.upq[:, 128 * t:128 * t + 128], T.ups[:, 128 * t:128 * t + 128], T["xq%d" % t][:], T["xsc%d" % t][:],
+           "upq%d ups%d xq%d" % (t, t, t))
+
+    def best():
+        scan(T.rr[:, 8:8 + C], T.cs1[:], bank(7, 0, C), -3 * HUGE, Op.add, Op.max, "cs1", "rr b7")
+        tt(T.nn[:], bank(7, 0, C), T.rr[:, 7:7 + C], Op.is_le, "rr rr0", "nn b7")
+        scan(T.sel[:], T.nn[:], T.tp[:], 0.0, Op.mult, Op.max, "nn tpa tpb", "sel")
+        ts(T.l1[:, 0:1], T.sel[:, 127:128], mul, Op.mult, b0, Op.add, "sel mul b0", "l1a")
+        ts(T.l1[:, 1:2], T.sel[:, C - 1:C], mul, Op.mult, b1, Op.add, "sel mul b1", "l1b")
+
+    def wrap16(src, n, rd):
+        scan(T.sc[:, 0:n], T.c16[:, 0:n], src, 0.0, Op.add, Op.max, "c16 " + rd, "sc")
+        return T.sc[:, 15:n:16]
+
+    def wrap4(src, n, rd, out, wr, buf, key):
+        scan(buf[:, 0:n], T.c4[:, 0:n], src, 0.0, Op.add, Op.max, "c4 " + rd, key)
+        ts(out, buf[:, 3:n:4], 4.0, Op.mult, off4, Op.add, key + " off4", wr)
+
+    def level(i, src, rd):
+        ts(wl(i), wrap16(src, C, rd), off16, Op.add, rd="sc off16", wr="w%d" % i)
+
+    def far(src, i, ks, bias=-BASE):
+        act(T.dg[:], src.indirect(wl(i)), "%s w%d" % (ks, i), "dg", bias=bias)
+
+    def near(out, src, ko, ks):
+        scan(out, T.dg[:], src, KEEP, Op.min, Op.add, "dg " + ks, ko)
+
+    def unpacked(b, q):
+        (act if q == "s" else cp)(T.dx[:, b:896:4], bank(b, 0, C), "", "dx%d b%d" % (b, b))
+
+    quant_e(0)
+    quant_x(0)
+    send_x(0)
+    iota(T.dx[:, 896:912], [[0, 16]], 0, 0, "dxz")
+    iota(T.k64[:], [[64, 7], [0, 2]], 0, 0, "k64")
+    iota(T.val[:], [[0, 8]], 0, 0, "val")
+    iota(T.pt[:, 384:512], [[0, 128]], 0, 0, "ptz")
+    level(1, tbl(2), "t2")
+    act(tbl(3), tbl(2).indirect(wl(0)), "t2 w0", "t3")
+    act(tbl(4), tbl(2).indirect(wl(1)), "t2 w1", "t4")
+    tt(T.e2[:], T.sc[:, 15:C:16], T.pm[:], Op.is_equal, "sc pm", "e2")
+    quant(T.uq[:], T.us[:], T.ut[:], "ut", "uq")
+    tt(T.pm[:], T.e1[:], T.e2[:], Op.add, "e1 e2", "pm")
+    cp(T.el[:], T.pm[:], "pm", "el")
+    act(T.db[:], ident.indirect(T.el[:]), "t0 el", "db", bias=BASE)
+    quant_e(1)
+    level(2, tbl(4), "t4")
+    act(T.p8[:], tbl(4).indirect(wl(2)), "t4 w2", "p8")
+    far(T.db[:], 1, "db")
+    cp(tbl(5), tbl(1).indirect(wl(2)), "t1 w2", "t5")
+    level(3, T.p8[:], "p8")
+    act(T.p16[:], T.p8[:].indirect(wl(3)), "p8 w3", "p16")
+    near(T.da[:], T.db[:], "da", "db")
+    far(T.da[:], 2, "da")
+    pick_u(0)
+    scores(0)
+    level(4, T.p16[:], "p16")
+    act(T.p8b[:], T.p8[:], "p8 cf", "p8b", scale=bit)
+    near(T.db[:], T.da[:], "db", "da")
+    far(T.db[:], 3, "db")
+    cp(tbl(6), tbl(2).indirect(wl(2)), "t2 w2", "t6")
+    scan(T.aw[:, 0:C], T.p8b[:], T.idb[:], KEEP, Op.min, Op.add, "p8b idb", "aw0")
+    act(T.aw[:, C:2 * C], T.aw[:, 0:C].indirect(wl(4)), "aw0 w4", "aw1")
+    near(T.da[:], T.db[:], "da", "db")
+    far(T.da[:], 4, "da")
+    act(tbl(7), tbl(3).indirect(wl(2)), "t3 w2", "t7")
+    best()
+
+    tabs = "t0 t1 t2 t3 t4 t5 t6 t7"
+    for t in range(R):
+        uw, uwk = (T.uw0, "uw0a uw0b") if t == 0 else (T.uw1, "uw1a uw1b uw1z")
+        fo, fi = T.fout[:, 24 * t:24 * t + 24], T.fin[:, 24 * t:24 * t + 24]
+        hq, hsc = T["hq%d" % t], T["hsc%d" % t]
+        last = t == R - 1
+        ts(T.l2[:], T.aw[:].indirect(T.l1[:]), -LIFT, Op.add, rd="aw0 aw1 aw2 l1a l1b", wr="l2")
+        act(T.rs[:, 0:448], T.tb[:].indirect(T.l2[:, 0:28]), tabs + " l2", "rs")
+        if t == 0:
+            near(T.uw0[:, 0:C], T.da[:], "uw0a", "da")
+        cp(T.gu[:], uw[:].indirect(T.l1[:]), uwk + " l1a l1b", "gu")
+        scan(T.ab[:, 1:29], T.ee[:, 0:28], T.gu[:, 0:28], 0.0, Op.add, Op.subtract, "ee gu", "ab")
+        tt(T.vv[:], T.ab[:].indirect(LA), T.nv[:], Op.subtract, "ab LA nv", "vv")
+        tt(T.fl[:], T.ab[:].indirect(LB), T.nt[:], Op.is_le, "ab LB nt", "fl")
+        scan(T.cs[:], T.vv[:], T.fl[:], 0.0, Op.min, Op.mult, "vv fl", "cs")
+        ts(T.cw[:], T.cs[:, 7:48:8], -1.0, Op.mult, rd="cs", wr="cw")
+        cp(T.fr[:, 0:A], T.rs[:].indirect(T.cw[:]), "rs rsz cw", "fr")
+        wrap4(T.fr[:, 0:A], A, "fr", fo, "fo%d" % t, T.f4, "f4")
+        send(t, fi, fo, "al%d" % t, "fo%d" % t)
+        arrival(t, "al%d" % t, 1, "fi%d" % t)
+        if t == 0:
+            quant_e(2)
+            quant_e(3)
+            iota(T.ht[:, 384:512], [[0, 128]], 0, 0, "htz")
+            iota(T.fr[:, A:2 * A], [[1, A]], C, 0, "frz")
+            iota(T.lrf[:], [[64, 7], [-16, 2]], 31, 0, "lrf")
+            iota(T.uw1[:, 448:464], [[0, 16]], 0, 0, "uw1z")
+        iota(XY[t][:, 896:1280], [[0, 384]], 0, 0, "y%d" % t)
+        for b in range(4):
+            mm(b, C, T.eq[:, 128 * b:128 * b + 128], T.es[:, 128 * b:128 * b + 128], T["aq%d" % t][:], T["asc%d" % t][:], "e%d aq%d" % (b, t))
+        if t == 0:
+            act(c18, s8, "cf", "c18", scale=-1.0, bias=7.0)
+            act(offl, off16, "off16", "offl", bias=LIFT)
+            act(T.nm[:], T.nt[:], "nt", "nm", scale=-1.0, bias=-1.0)
+            act(T.nm[:, 0:48:8], T.nt[:, 0:48:8], "nt", "nm", bias=float(A))
+            for b in range(4):
+                unpacked(b, "s")
+        tt(T.drn[:, 0:7], T.gu[:, 1:28:4], T.gu[:, 0:28:4], Op.subtract, "gu", "drn")
+        if t == 0:
+            ts(T.mlf[:], wrap16(T.uw0[:, 0:C], C, "uw0a"), off16, Op.add, rd="sc off16", wr="mlf")
+            tt(T.cw3[:], T.mlf[:], T.k64[:], Op.add, "mlf k64", "cw3")
+        tt(T.mlf[:, 0:14:2], T.drn[:, 0:7], T.cw3[:, 0:14:2], Op.add, "drn cw3", "mlf")
+        tt(T.mlf[:, 1:14:2], T.drn[:, 0:7], T.cw3[:, 1:14:2], Op.add, "drn cw3", "mlfb")
+        cp(T.ml[:], T.mlf[:], "mlf mlfb", "ml")
+        tt(T.mark[:], T.rs[:].indirect(T.ml[:]), ident, Op.is_equal, "rs rsz ml t0", "mark")
+        if not last:
+            far(T.mark[:], 0, "mark", 0.0)
+            act(T.mk2[:], T.mark[:], "mark", "mk2", bias=BASE)
+        ts(T.am[:, 0:7], T.ab[:, 4:29:4], float(A), Op.min, rd="ab", wr="am")
+        tt(T.fl[:], T.ab[:].indirect(LA), T.nt[:], Op.is_le, "ab LA nt", "fl")
+        tt(T.val[:, 0:7], T.ab[:, 0:28:4], T.am[:, 0:7], Op.add, "ab am", "val")
+        if t == 0:
+            ts(LK, T.tb[:, 0:3], 0.0, Op.mult, c18, Op.add, "t0 c18", "LK")
+        tt(T.vv[:], T.val[:].indirect(LK), T.nm[:], Op.add, "val LK nm", "vv")
+        scan(T.cs[:], T.vv[:], T.fl[:], 0.0, Op.max, Op.mult, "vv fl", "cs")
+        cp(T.mw[:], T.cs[:, 7:48:8], "cs", "mw")
+        cp(T.mr[:], T.fr[:].indirect(T.mw[:]), "fr frz mw", "mr")
+        wrap4(T.mr[:], A, "mr", T.m4[:], "m4", T.f4, "f4")
+        ts(T.m16[:], wrap16(T.mr[:], A, "mr"), off16, Op.add, rd="sc off16", wr="m16")
+        if not last:
+            near(T.da[:], T.mk2[:], "da", "mk2")
+        if t > 0:
+            for b in range(4):
+                unpacked(b, "sv"[b % 2])
+        dxk = "dx0 dx1 dx2 dx3 dxz fi%d" % t
+        cp(T.pt[:, 0:192], T.dx[:].indirect(T.fin[:, 24 * t:24 * t + 12]), dxk, "pta")
+        act(T.pt[:, 192:384], T.dx[:].indirect(T.fin[:, 24 * t + 12:24 * t + 24]), dxk, "ptb")
+        if not last:
+            far(T.da[:], 1, "da")
+        else:
+            act(T.hr[:, 0:C], ident, "t0", "hr")
+        quant(T.pq[:], T.psc[:], T.pt[:], "pta ptb ptz", "pq")
+        for b in range(4):
+            mm(4 + b, 128, T.wq[:, 128 * b:128 * b + 128], T.wsc[:, 128 * b:128 * b + 128], T.pq[:], T.psc[:], "wq wsc pq")
+        for b in range(4):
+            if b % 2 == 1:
+                act(T.ht[:, b:384:4], bank(4 + b, 0, A), "", "ht%d b%d" % (b, 4 + b), func=Act.Relu, scale=0.03125)
+            else:
+                ts(T.ht[:, b:384:4], bank(4 + b, 0, A), 0.0, Op.max, 0.03125, Op.mult, "", "ht%d b%d" % (b, 4 + b))
+        quant(hq[:, 0:128], hsc[:, 0:128], T.ht[:], "ht0 ht1 ht2 ht3 htz", "hq%d" % t)
+        send(t, hq[:, 128:128 + A].bitcast(dt.uint8), hq[:, 0:A].bitcast(dt.uint8), "ah%d" % t, "hq%d" % t)
+        send(t, hsc[:, 128:128 + A], hsc[:, 0:A], "ah%d" % t, "hq%d" % t)
+        arrival(t, "ah%d" % t, 2, "lq%d" % t)
+        if not last:
+            act(T.hr[:, 0:C], ident, "t0", "hr")
+            near(T.db[:], T.da[:], "db", "da")
+            far(T.db[:], 2, "db")
+        if t == 0:
+            ts(Lrev, T.lrf[:], q_, Op.subtract, rd="lrf cf", wr="Lrev")
+            ts(T.cw3[:], T.cw3[:], -3 * BASE, Op.add, rd="cw3", wr="cw3")
+        cp(T.hr[:].indirect(T.m16[:]), T.fr[:, A:2 * A], "frz m16", "hr")
+        if not last:
+            near(T.da[:], T.db[:], "da", "db")
+            far(T.da[:], 3, "da")
+        act(T.xs[:], XY[t][:].indirect(T.m4[:]), "x%d x%db y%d m4" % (t, t, t), "xs")
+        wrap4(T.hr[:, 0:C], C, "hr", T.hw[:], "hw", T.sc2, "sc2")
+        if not last:
+            near(T.db[:], T.da[:], "db", "da")
+            pick_u(t + 1)
+            far(T.db[:], 4, "db")
+            act(T.rev[:], T.rs[:].indirect(Lrev), "rs rsz Lrev", "rev")
+            if t == 0:
+                act(T.nc[:], T.uw0[:, 0:C], "uw0a", "nc", scale=-1.0, bias=3 * BASE)
+            ts(T.ee[:, 1:28:4], T.drn[:, 0:7], 288.0 if t == 0 else 96.0, Op.add, rd="drn", wr="ee")
+            near(T.uw1[:, 0:C], T.db[:], "uw1a", "db")
+            ts(T.aw[:, 448:462], wrap16(T.rev[:], C, "rev"), offl, Op.add, rd="sc offl", wr="aw2")
+        else:
+            ts(T.ml1f[:], T.mlf[:], -1.0, Op.add, rd="mlf mlfb", wr="ml1f")
+            quant(T.vq[:], T.vs[:], T.vt[:], "vt", "vq")
+            tt(T.mlf[:], T.ml1f[:], T.k64[:], Op.max, "ml1f k64", "mlf mlfb")
+            cp(T.ml1[:], T.mlf[:], "mlf mlfb", "ml1")
+            tt(T.da[:], T.rs[:].indirect(T.ml1[:]), tbl(1), Op.subtract, "rs rsz ml1 t1", "da")
+            tt(T.db[:], T.da[:], T.mark[:], Op.mult, "da mark", "db")
+            tt(T.da[:], T.db[:], tbl(1), Op.add, "db t1", "da")
+            dma("y", T.op[:], T.da[0:128:16, :], "stored", 0, "da", "")
+        for b in range(4):
+            mm(b, 128, T.eq[:, 128 * b:128 * b + 128], T.es[:, 128 * b:128 * b + 128], hq[:, A:128 + A], hsc[:, A:128 + A],
+               "e%d hq%d lq%d" % (b, t, t))
+        for b in range(4):
+            tt(XY[t][:, 896 + b:1280:4], bank(b, 32, 128), T.xs[:, b:384:4], Op.add, "xs", "y%d_%d b%d" % (t, b, b))
+        xk = "x%d x%db y%d y%d_0 y%d_1 y%d_2 y%d_3 hw" % (t, t, t, t, t, t, t)
+        act(XY[t + 1][:, 448:896], XY[t][:].indirect(T.hw[:, 28:56]), xk, "x%db" % (t + 1))
+        cp(XY[t + 1][:, 0:448], XY[t][:].indirect(T.hw[:, 0:28]), xk, "x%d" % (t + 1))
+        quant_x(t + 1)
+        if not last:
+            scores(t + 1)
+            send_x(t + 1)
+            scan(T.uw1[:, C:2 * C], T.uw1[:, 0:C], T.nc[:], KEEP, Op.min, Op.add, "uw1a nc", "uw1b")
+            best()
+
+    mm(7, C, T.vq[:], T.vs[:], T.xq3[:], T.xsc3[:], "vq xq3")
+    dma("y", T.oc[:], T.xq3[:].bitcast(dt.uint8), "stored", 0, "xq3", "")
+    for k in range(4):
+        dma("s", T.osc[4 * k:4 * k + 4, :], T.xsc3[32 * k:32 * k + 4, :], "stored", 0, "xq3", "")
+    cp(T.yo[:], bank(7, 0, C), "", "yo b7")
+    dma("y", T.y[:], T.yo[:], "stored", 0, "yo", "")
+    g.sync.wait_ge(T.sem.stored, 16 * 7)
+    g.wait_ge(T.sem.sent, nsent[0])
+    for q in CNT:
+        if clock[q].get(CNT[q], 0) < count[q]:
+            Q[q].wait_ge(T.sem[CNT[q]], count[q])

@@ -8,50 +8,33 @@ HUGE = 1.0e29
 LIFT = 256.0
 BASE = 64.0
 
+FIRST = ("uq w1a w1b e2 pm t3 el qx p4 w2a db pick w2b t6 f1 b1 p8 n1 w3a w3b f2 b2 n2 E0 p16 w4a p8b f3 a0 w4b a1 n3 f4 "
+         "b3 t5 b4 t7 nt n4 l2 rs")
+LIST = "cwa k0 am hr drn cwb fl cwc lk val mlf vv ml cs mark s0 s1 mw mr f0 v3 n0 s2"
+MID = "lrev f1"
+BACK = "ee n1 m16a m4a rev f2 m16b awa n2 m4b sca f3 hwa n3 xs hwb f4 pick awb n4 nc"
+GAP = "ub cwd"
+
 
 def _sb(n, t):
     return ("sbuf", [128, n], t)
 
 
-SCRATCH = {
-    "par_i": _sb(14, I32), "ut": _sb(512, BF), "vt": _sb(512, BF),
-    "wq": _sb(512, MX), "wsc": _sb(512, U8),
-    "uq": _sb(128, MX), "us": _sb(128, U8), "upq": _sb(384, MX), "ups": _sb(384, U8),
-    "vq": _sb(128, MX), "vs": _sb(128, U8),
-    "ez": _sb(520, BF), "eone": _sb(128, BF), "eq": _sb(512, MX), "es": _sb(512, U8),
-    "xy0": _sb(1280, BF), "xy1": _sb(1280, BF), "xy2": _sb(1280, BF), "xy3": _sb(896, BF),
-    "dx": _sb(912, BF), "pt": _sb(512, BF), "pq": _sb(128, MX), "psc": _sb(128, U8),
-    "ht": _sb(512, BF), "xs": _sb(384, BF),
-    "fout": _sb(72, U16), "fin": _sb(72, U16),
-    "ci": _sb(8, I32), "pc": _sb(2, I32), "cf": _sb(8, F32), "cg": _sb(24, F32),
-    "tb": _sb(8 * C, F32), "p8": _sb(C, F32), "p16": _sb(C, F32), "p8b": _sb(C, F32), "idb": _sb(C, F32),
-    "da": _sb(C, F32), "db": _sb(C, F32), "dg": _sb(C, F32), "mk2": _sb(C, F32), "nc": _sb(C, F32),
-    "idw": _sb(14, F32), "e1": _sb(14, F32), "e2": _sb(14, F32), "pm": _sb(14, F32), "el": _sb(14, U16),
-    "aw": _sb(464, F32), "uw0": _sb(464, F32), "uw1": _sb(464, F32),
-    "wl": _sb(80, U16), "sc": _sb(C, F32), "sc2": _sb(C, F32),
-    "s16": _sb(16, F32), "s4": _sb(8, F32), "c16": _sb(C, F32), "c4": _sb(C, F32),
-    "cl": _sb(64, U16), "ul_i": _sb(24, I32), "ul": _sb(24, U16),
-    "cs1": _sb(C, F32), "tp": _sb(C, F32), "ta": _sb(128, F32), "kt": _sb(8, F32),
-    "rr": _sb(C + 8, F32), "nn": _sb(C, F32), "sel": _sb(C, F32),
-    "l1": _sb(2, U16), "l2": _sb(32, U16), "gu": _sb(32, F32), "ee": _sb(32, F32), "ab": _sb(32, F32),
-    "nv": _sb(48, F32), "nt": _sb(48, F32), "nm": _sb(48, F32), "i48a": _sb(48, F32), "i48b": _sb(48, F32),
-    "vv": _sb(48, F32), "fl": _sb(48, F32), "cs": _sb(48, F32), "cw": _sb(6, U16),
-    "rs": _sb(544, F32), "fr": _sb(192, F32), "f4": _sb(A, F32),
-    "am": _sb(8, F32), "val": _sb(8, F32), "mw": _sb(6, U16), "mr": _sb(A, F32), "m16": _sb(6, U16), "m4": _sb(24, U16),
-    "hr": _sb(320, F32), "hw": _sb(56, U16),
-    "k64": _sb(14, F32), "lrf": _sb(14, F32), "cw3": _sb(14, F32), "drn": _sb(8, F32), "mlf": _sb(14, F32), "ml": _sb(14, U16),
-    "ml1f": _sb(14, F32), "ml1": _sb(14, U16), "mark": _sb(C, F32), "rev": _sb(C, F32),
-    "yo": _sb(C, F32),
-    "ps": ("psum", [128, 4096], F32),
-}
-for _t in range(R + 1):
-    SCRATCH["xq%d" % _t] = _sb(C, MX)
-    SCRATCH["xsc%d" % _t] = _sb(C, U8)
-for _t in range(R):
-    SCRATCH["aq%d" % _t] = _sb(C, MX)
-    SCRATCH["asc%d" % _t] = _sb(C, U8)
-    SCRATCH["hq%d" % _t] = _sb(128 + A, MX)
-    SCRATCH["hsc%d" % _t] = _sb(128 + A, U8)
+SCRATCH = {"ps": ("psum", [128, 4096], F32)}
+for _d, _l in (
+        (I32, "par_i 14 ci 8 pc 2 ul_i 24"),
+        (BF, "ut 512 vt 512 ez 520 eone 128 xy0 1280 xy1 1280 xy2 1280 xy3 896 dx 912 pt 512 ht 512 xs 384 tp 224 nn 224 sel 224"),
+        (MX, "wq 512 uq 128 upq 384 vq 128 eq 512 pq 128 xq0 224 xq1 224 xq2 224 xq3 224 aq0 224 aq1 224 aq2 224 hq0 224 hq1 224 hq2 224"),
+        (U8, "wsc 512 us 128 ups 384 vs 128 es 512 psc 128 xsc0 224 xsc1 224 xsc2 224 xsc3 224 asc0 224 asc1 224 asc2 224 "
+             "hsc0 224 hsc1 224 hsc2 224"),
+        (U16, "fout 72 fin 72 el 14 wl 80 cl 64 ul 24 l1 2 l2 32 cw 6 mw 6 m16 6 m4 24 hw 56 ml 14 ml1 14"),
+        (F32, "cf 8 cg 24 tb 1792 p8 224 p16 224 p8b 224 idb 224 da 224 db 224 dg 224 mk2 224 nc 224 idw 14 e1 14 e2 14 pm 14 "
+              "aw 464 uw0 464 uw1 464 sc 224 sc2 224 s16 16 s4 8 c16 224 c4 224 cs1 224 ta 128 kt 8 rr 232 gu 32 ee 32 ab 32 "
+              "nv 48 nt 48 nm 48 i48a 48 i48b 48 vv 48 fl 48 cs 48 rs 544 fr 192 f4 96 am 8 val 8 mr 96 hr 320 k64 14 lrf 14 "
+              "cw3 14 drn 8 mlf 14 ml1f 14 mark 224 rev 224 yo 224")):
+    _w = _l.split()
+    for _i in range(0, len(_w), 2):
+        SCRATCH[_w[_i]] = _sb(int(_w[_i + 1]), _d)
 
 SEMAPHORES = (["nv", "ns", "np", "ng", "ld_par", "ld_x", "ld_u", "ld_w", "ld_v", "stored", "sent"]
               + ["ax%d" % t for t in range(R)] + ["al%d" % t for t in range(R)] + ["ah%d" % t for t in range(R)])
@@ -211,39 +194,37 @@ def rank_program(g, core, T, topo):
     act(T.c16[:], T.s16[:].indirect(Lq), "s16 Lq", "c16", bias=KEEP)
     act(T.ta[:], T.tb[:, 0:128], "t0 n32", "ta", func=Act.Relu, bias=n32)
     act(T.idb[:], ident, "t0 nb y224", "idb", scale=nb, bias=y224)
-    act(T.tp[:, 0:128], T.ta[:], "ta", "tpa", scale=-1.0, bias=200.0)
-    act(T.tp[:, 128:C], T.ta[:, 0:96], "ta", "tpb", scale=-1.0, bias=372.0)
+    act(T.tp[:, 0:128], T.ta[:], "ta", "tpa", scale=-1.0, bias=100.0)
+    act(T.tp[:, 128:C], T.ta[:, 0:96], "ta", "tpb", scale=-1.0, bias=240.0)
     act(T.c4[:], T.s4[:].indirect(Lh), "s4 Lh", "c4", bias=KEEP)
-    act(T.nt[:], T.i48a[:], "i48a cf", "nt", bias=q_)
-    act(T.nv[:], T.i48b[:], "i48b cf", "nv", bias=q_)
     ts(off16, q_, KEEP, Op.mult, -15 * KEEP, Op.add, "cf", "off16")
     fill(T.cs1[:], 0.0, "cs1")
     ts(mul, hi2, -1.0, Op.add, rd="cf", wr="mul")
     ts(lo, hi2, -1.0, Op.mult, 1.0, Op.add, "cf", "lo")
-    ts(c9, hh, float(C), Op.mult, 200.0, Op.add, "cf", "c9")
+    ts(c9, hh, float(C), Op.mult, 100.0, Op.add, "cf", "c9")
     ts(c10, hh, 446.0, Op.add, rd="cf", wr="c10")
     ts(T.cs1[:, 0:C:32], T.kt[:, 0:7], kq, Op.is_equal, -3 * HUGE, Op.mult, "kt cf", "cs1")
     ts(c11, kq, 32.0, Op.mult, c9, Op.add, "cf c9", "c11")
     ts(c12, kq, 2.0, Op.mult, c10, Op.add, "cf c10", "c12")
-    ts(c14, lo, 292.0, Op.mult, 8.0, Op.add, "lo", "c14")
+    ts(c14, lo, 260.0, Op.mult, 8.0, Op.add, "lo", "c14")
     ts(T.cs1[:, 31:C:32], T.kt[:, 0:7], kq, Op.is_equal, HUGE, Op.mult, "kt cf", "cs1")
     ts(c13, c11, c12, Op.subtract, lo, Op.mult, "c11 c12 lo", "c13")
     ts(c15, s8, -4.0, Op.mult, 28.0, Op.add, "cf", "c15")
     ts(c16, s8, -4.0, Op.mult, 25.0, Op.add, "cf", "c16c")
+    cp(wl(0), T.par_i[:], "par_i", "w0")
+    act(tbl(1), ident.indirect(wl(0)), "t0 w0", "t1")
+    act(tbl(2), tbl(1).indirect(wl(0)), "t1 w0", "t2")
     ts(c17, hh, -12 * KEEP, Op.add, rd="cf", wr="c17")
     ts(b0, c13, c12, Op.add, rd="c13 c12", wr="b0")
     ts(b1, c13, c12, Op.add, c14, Op.add, "c13 c12 c14", "b1")
     ts(LA, T.tb[:, 0:3], 0.0, Op.mult, c15, Op.add, "t0 c15", "LA")
     ts(LB, T.tb[:, 0:3], 0.0, Op.mult, c16, Op.add, "t0 c16c", "LB")
     ts(off4, kq, 4 * KEEP, Op.mult, c17, Op.add, "cf c17", "off4")
-    cp(wl(0), T.par_i[:], "par_i", "w0")
-    act(tbl(1), ident.indirect(wl(0)), "t0 w0", "t1")
-    act(tbl(2), tbl(1).indirect(wl(0)), "t1 w0", "t2")
     cp(T.ul[:], T.ul_i[:], "ul_i", "ul")
     ts(T.idw[:], T.tb[:, 0:14], 16.0, Op.mult, q_, Op.add, "t0 cf", "idw")
     ts(T.pm[:], T.par_i[:], off16, Op.subtract, rd="par_i off16", wr="pm")
-    tt(T.e1[:], T.par_i[:], T.idw[:], Op.is_equal, "par_i idw", "e1")
     fill(T.rr[:, 0:8], 0.0, "rr0")
+    tt(T.e1[:], T.par_i[:], T.idw[:], Op.is_equal, "par_i idw", "e1")
     fill(T.ab[:], 0.0, "ab")
     ts(T.ee[:], T.ee[:], 0.0, Op.max, rd="ee", wr="ee")
 
@@ -267,23 +248,17 @@ def rank_program(g, core, T, topo):
         mm(7, C, T.upq[:, 128 * t:128 * t + 128], T.ups[:, 128 * t:128 * t + 128], T["xq%d" % t][:], T["xsc%d" % t][:],
            "upq%d ups%d xq%d" % (t, t, t))
 
-    def best():
-        scan(T.rr[:, 8:8 + C], T.cs1[:], bank(7, 0, C), -3 * HUGE, Op.add, Op.max, "cs1", "rr b7")
-        tt(T.nn[:], bank(7, 0, C), T.rr[:, 7:7 + C], Op.is_le, "rr rr0", "nn b7")
-        scan(T.sel[:], T.nn[:], T.tp[:], 0.0, Op.mult, Op.max, "nn tpa tpb", "sel")
-        ts(T.l1[:, 0:1], T.sel[:, 127:128], mul, Op.mult, b0, Op.add, "sel mul b0", "l1a")
-        ts(T.l1[:, 1:2], T.sel[:, C - 1:C], mul, Op.mult, b1, Op.add, "sel mul b1", "l1b")
-
     def wrap16(src, n, rd):
         scan(T.sc[:, 0:n], T.c16[:, 0:n], src, 0.0, Op.add, Op.max, "c16 " + rd, "sc")
-        return T.sc[:, 15:n:16]
 
-    def wrap4(src, n, rd, out, wr, buf, key):
+    def taken(out, n, off, ko, wr):
+        ts(out, T.sc[:, 15:n:16], off, Op.add, rd="sc " + ko, wr=wr)
+
+    def wrap4(buf, key, src, n, rd):
         scan(buf[:, 0:n], T.c4[:, 0:n], src, 0.0, Op.add, Op.max, "c4 " + rd, key)
-        ts(out, buf[:, 3:n:4], 4.0, Op.mult, off4, Op.add, key + " off4", wr)
 
-    def level(i, src, rd):
-        ts(wl(i), wrap16(src, C, rd), off16, Op.add, rd="sc off16", wr="w%d" % i)
+    def taken4(out, buf, key, n, wr):
+        ts(out, buf[:, 3:n:4], 4.0, Op.mult, off4, Op.add, key + " off4", wr)
 
     def far(src, i, ks, bias=-BASE):
         act(T.dg[:], src.indirect(wl(i)), "%s w%d" % (ks, i), "dg", bias=bias)
@@ -294,54 +269,58 @@ def rank_program(g, core, T, topo):
     def unpacked(b, q):
         (act if q == "s" else cp)(T.dx[:, b:896:4], bank(b, 0, C), "", "dx%d b%d" % (b, b))
 
-    quant_e(0)
-    quant_x(0)
-    send_x(0)
-    iota(T.dx[:, 896:912], [[0, 16]], 0, 0, "dxz")
-    iota(T.k64[:], [[64, 7], [0, 2]], 0, 0, "k64")
-    iota(T.val[:], [[0, 8]], 0, 0, "val")
-    iota(T.pt[:, 384:512], [[0, 128]], 0, 0, "ptz")
-    level(1, tbl(2), "t2")
-    act(tbl(3), tbl(2).indirect(wl(0)), "t2 w0", "t3")
-    act(tbl(4), tbl(2).indirect(wl(1)), "t2 w1", "t4")
-    tt(T.e2[:], T.sc[:, 15:C:16], T.pm[:], Op.is_equal, "sc pm", "e2")
-    quant(T.uq[:], T.us[:], T.ut[:], "ut", "uq")
-    tt(T.pm[:], T.e1[:], T.e2[:], Op.add, "e1 e2", "pm")
-    cp(T.el[:], T.pm[:], "pm", "el")
-    act(T.db[:], ident.indirect(T.el[:]), "t0 el", "db", bias=BASE)
-    quant_e(1)
-    level(2, tbl(4), "t4")
-    act(T.p8[:], tbl(4).indirect(wl(2)), "t4 w2", "p8")
-    far(T.db[:], 1, "db")
-    cp(tbl(5), tbl(1).indirect(wl(2)), "t1 w2", "t5")
-    level(3, T.p8[:], "p8")
-    act(T.p16[:], T.p8[:].indirect(wl(3)), "p8 w3", "p16")
-    near(T.da[:], T.db[:], "da", "db")
-    far(T.da[:], 2, "da")
-    pick_u(0)
-    scores(0)
-    level(4, T.p16[:], "p16")
-    act(T.p8b[:], T.p8[:], "p8 cf", "p8b", scale=bit)
-    near(T.db[:], T.da[:], "db", "da")
-    far(T.db[:], 3, "db")
-    cp(tbl(6), tbl(2).indirect(wl(2)), "t2 w2", "t6")
-    scan(T.aw[:, 0:C], T.p8b[:], T.idb[:], KEEP, Op.min, Op.add, "p8b idb", "aw0")
-    act(T.aw[:, C:2 * C], T.aw[:, 0:C].indirect(wl(4)), "aw0 w4", "aw1")
-    near(T.da[:], T.db[:], "da", "db")
-    far(T.da[:], 4, "da")
-    act(tbl(7), tbl(3).indirect(wl(2)), "t3 w2", "t7")
-    best()
+    def first_x():
+        quant_x(0)
+        send_x(0)
+        iota(T.dx[:, 896:912], [[0, 16]], 0, 0, "dxz")
+        iota(T.k64[:], [[64, 7], [0, 2]], 0, 0, "k64")
+        iota(T.val[:], [[0, 8]], 0, 0, "val")
+        iota(T.pt[:, 384:512], [[0, 128]], 0, 0, "ptz")
 
-    tabs = "t0 t1 t2 t3 t4 t5 t6 t7"
+    da, db = T.da[:], T.db[:]
+    one = {
+        "b1": lambda: scan(T.rr[:, 8:8 + C], T.cs1[:], bank(7, 0, C), -3 * HUGE, Op.add, Op.max, "cs1", "rr b7"),
+        "b2": lambda: tt(T.nn[:], bank(7, 0, C), T.rr[:, 7:7 + C], Op.is_le, "rr rr0", "nn b7"),
+        "b3": lambda: scan(T.sel[:], T.nn[:], T.tp[:], 0.0, Op.mult, Op.max, "nn tpa tpb", "sel"),
+        "b4": lambda: (ts(T.l1[:, 0:1], T.sel[:, 127:128], mul, Op.mult, b0, Op.add, "sel mul b0", "l1a"),
+                       ts(T.l1[:, 1:2], T.sel[:, C - 1:C], mul, Op.mult, b1, Op.add, "sel mul b1", "l1b")),
+        "l2": lambda: ts(T.l2[:], T.aw[:].indirect(T.l1[:]), -LIFT, Op.add, rd="aw0 aw1 aw2 l1a l1b", wr="l2"),
+        "rs": lambda: act(T.rs[:, 0:448], T.tb[:].indirect(T.l2[:, 0:28]), "t0 t1 t2 t3 t4 t5 t6 t7 l2", "rs"),
+        "qx": first_x, "E0": lambda: quant_e(0),
+        "uq": lambda: quant(T.uq[:], T.us[:], T.ut[:], "ut", "uq"),
+        "pick": lambda: (pick_u(0), scores(0)),
+        "w1a": lambda: wrap16(tbl(2), C, "t2"), "w2a": lambda: wrap16(tbl(4), C, "t4"),
+        "w3a": lambda: wrap16(T.p8[:], C, "p8"), "w4a": lambda: wrap16(T.p16[:], C, "p16"),
+        "e2": lambda: tt(T.e2[:], T.sc[:, 15:C:16], T.pm[:], Op.is_equal, "sc pm", "e2"),
+        "pm": lambda: tt(T.pm[:], T.e1[:], T.e2[:], Op.add, "e1 e2", "pm"),
+        "el": lambda: cp(T.el[:], T.pm[:], "pm", "el"),
+        "db": lambda: act(db, ident.indirect(T.el[:]), "t0 el", "db", bias=BASE),
+        "t3": lambda: act(tbl(3), tbl(2).indirect(wl(0)), "t2 w0", "t3"),
+        "p4": lambda: act(tbl(4), tbl(2).indirect(wl(1)), "t2 w1", "t4"),
+        "t5": lambda: cp(tbl(5), tbl(1).indirect(wl(2)), "t1 w2", "t5"),
+        "t6": lambda: cp(tbl(6), tbl(2).indirect(wl(2)), "t2 w2", "t6"),
+        "t7": lambda: act(tbl(7), tbl(3).indirect(wl(2)), "t3 w2", "t7"),
+        "p8": lambda: act(T.p8[:], tbl(4).indirect(wl(2)), "t4 w2", "p8"),
+        "p16": lambda: act(T.p16[:], T.p8[:].indirect(wl(3)), "p8 w3", "p16"),
+        "p8b": lambda: act(T.p8b[:], T.p8[:], "p8 cf", "p8b", scale=bit),
+        "a0": lambda: scan(T.aw[:, 0:C], T.p8b[:], T.idb[:], KEEP, Op.min, Op.add, "p8b idb", "aw0"),
+        "a1": lambda: act(T.aw[:, C:2 * C], T.aw[:, 0:C].indirect(wl(4)), "aw0 w4", "aw1"),
+        "f1": lambda: far(db, 1, "db"), "n1": lambda: near(da, db, "da", "db"),
+        "f2": lambda: far(da, 2, "da"), "n2": lambda: near(db, da, "db", "da"),
+        "f3": lambda: far(db, 3, "db"), "n3": lambda: near(da, db, "da", "db"),
+        "f4": lambda: far(da, 4, "da"), "n4": lambda: near(T.uw0[:, 0:C], da, "uw0a", "da"),
+        "nt": lambda: (act(T.nt[:], T.i48a[:], "i48a cf", "nt", bias=q_), act(T.nv[:], T.i48b[:], "i48b cf", "nv", bias=q_)),
+    }
+    for i in range(1, 5):
+        one["w%db" % i] = lambda i=i: taken(wl(i), C, off16, "off16", "w%d" % i)
+    for n in FIRST.split():
+        one[n]()
+
     for t in range(R):
         uw, uwk = (T.uw0, "uw0a uw0b") if t == 0 else (T.uw1, "uw1a uw1b uw1z")
         fo, fi = T.fout[:, 24 * t:24 * t + 24], T.fin[:, 24 * t:24 * t + 24]
         hq, hsc = T["hq%d" % t], T["hsc%d" % t]
         last = t == R - 1
-        ts(T.l2[:], T.aw[:].indirect(T.l1[:]), -LIFT, Op.add, rd="aw0 aw1 aw2 l1a l1b", wr="l2")
-        act(T.rs[:, 0:448], T.tb[:].indirect(T.l2[:, 0:28]), tabs + " l2", "rs")
-        if t == 0:
-            near(T.uw0[:, 0:C], T.da[:], "uw0a", "da")
         cp(T.gu[:], uw[:].indirect(T.l1[:]), uwk + " l1a l1b", "gu")
         scan(T.ab[:, 1:29], T.ee[:, 0:28], T.gu[:, 0:28], 0.0, Op.add, Op.subtract, "ee gu", "ab")
         tt(T.vv[:], T.ab[:].indirect(LA), T.nv[:], Op.subtract, "ab LA nv", "vv")
@@ -349,60 +328,79 @@ def rank_program(g, core, T, topo):
         scan(T.cs[:], T.vv[:], T.fl[:], 0.0, Op.min, Op.mult, "vv fl", "cs")
         ts(T.cw[:], T.cs[:, 7:48:8], -1.0, Op.mult, rd="cs", wr="cw")
         cp(T.fr[:, 0:A], T.rs[:].indirect(T.cw[:]), "rs rsz cw", "fr")
-        wrap4(T.fr[:, 0:A], A, "fr", fo, "fo%d" % t, T.f4, "f4")
+        wrap4(T.f4, "f4", T.fr[:, 0:A], A, "fr")
+        taken4(fo, T.f4, "f4", A, "fo%d" % t)
         send(t, fi, fo, "al%d" % t, "fo%d" % t)
         arrival(t, "al%d" % t, 1, "fi%d" % t)
         if t == 0:
-            quant_e(2)
-            quant_e(3)
-            iota(T.ht[:, 384:512], [[0, 128]], 0, 0, "htz")
+            for b in (1, 2, 3):
+                quant_e(b)
             iota(T.fr[:, A:2 * A], [[1, A]], C, 0, "frz")
+            iota(T.ht[:, 384:512], [[0, 128]], 0, 0, "htz")
             iota(T.lrf[:], [[64, 7], [-16, 2]], 31, 0, "lrf")
             iota(T.uw1[:, 448:464], [[0, 16]], 0, 0, "uw1z")
         iota(XY[t][:, 896:1280], [[0, 384]], 0, 0, "y%d" % t)
         for b in range(4):
             mm(b, C, T.eq[:, 128 * b:128 * b + 128], T.es[:, 128 * b:128 * b + 128], T["aq%d" % t][:], T["asc%d" % t][:], "e%d aq%d" % (b, t))
-        if t == 0:
-            act(c18, s8, "cf", "c18", scale=-1.0, bias=7.0)
-            act(offl, off16, "off16", "offl", bias=LIFT)
-            act(T.nm[:], T.nt[:], "nt", "nm", scale=-1.0, bias=-1.0)
-            act(T.nm[:, 0:48:8], T.nt[:, 0:48:8], "nt", "nm", bias=float(A))
-            for b in range(4):
-                unpacked(b, "s")
-        tt(T.drn[:, 0:7], T.gu[:, 1:28:4], T.gu[:, 0:28:4], Op.subtract, "gu", "drn")
-        if t == 0:
-            ts(T.mlf[:], wrap16(T.uw0[:, 0:C], C, "uw0a"), off16, Op.add, rd="sc off16", wr="mlf")
-            tt(T.cw3[:], T.mlf[:], T.k64[:], Op.add, "mlf k64", "cw3")
-        tt(T.mlf[:, 0:14:2], T.drn[:, 0:7], T.cw3[:, 0:14:2], Op.add, "drn cw3", "mlf")
-        tt(T.mlf[:, 1:14:2], T.drn[:, 0:7], T.cw3[:, 1:14:2], Op.add, "drn cw3", "mlfb")
-        cp(T.ml[:], T.mlf[:], "mlf mlfb", "ml")
-        tt(T.mark[:], T.rs[:].indirect(T.ml[:]), ident, Op.is_equal, "rs rsz ml t0", "mark")
-        if not last:
-            far(T.mark[:], 0, "mark", 0.0)
-            act(T.mk2[:], T.mark[:], "mark", "mk2", bias=BASE)
-        ts(T.am[:, 0:7], T.ab[:, 4:29:4], float(A), Op.min, rd="ab", wr="am")
-        tt(T.fl[:], T.ab[:].indirect(LA), T.nt[:], Op.is_le, "ab LA nt", "fl")
-        tt(T.val[:, 0:7], T.ab[:, 0:28:4], T.am[:, 0:7], Op.add, "ab am", "val")
-        if t == 0:
-            ts(LK, T.tb[:, 0:3], 0.0, Op.mult, c18, Op.add, "t0 c18", "LK")
-        tt(T.vv[:], T.val[:].indirect(LK), T.nm[:], Op.add, "val LK nm", "vv")
-        scan(T.cs[:], T.vv[:], T.fl[:], 0.0, Op.max, Op.mult, "vv fl", "cs")
-        cp(T.mw[:], T.cs[:, 7:48:8], "cs", "mw")
-        cp(T.mr[:], T.fr[:].indirect(T.mw[:]), "fr frz mw", "mr")
-        wrap4(T.mr[:], A, "mr", T.m4[:], "m4", T.f4, "f4")
-        ts(T.m16[:], wrap16(T.mr[:], A, "mr"), off16, Op.add, rd="sc off16", wr="m16")
-        if not last:
-            near(T.da[:], T.mk2[:], "da", "mk2")
-        if t > 0:
-            for b in range(4):
-                unpacked(b, "sv"[b % 2])
+        bufs = [(T.mk2[:], "mk2"), (da, "da"), (db, "db"), (da, "da"), (db, "db"), (T.uw1[:, 0:C], "uw1a")]
+        steps = {
+            "k0": ("0", lambda: (act(c18, s8, "cf", "c18", scale=-1.0, bias=7.0), act(offl, off16, "off16", "offl", bias=LIFT),
+                                 act(T.nm[:], T.nt[:], "nt", "nm", scale=-1.0, bias=-1.0),
+                                 act(T.nm[:, 0:48:8], T.nt[:, 0:48:8], "nt", "nm", bias=float(A)))),
+            "drn": ("012", lambda: tt(T.drn[:, 0:7], T.gu[:, 1:28:4], T.gu[:, 0:28:4], Op.subtract, "gu", "drn")),
+            "cwa": ("0", lambda: wrap16(T.uw0[:, 0:C], C, "uw0a")),
+            "cwb": ("0", lambda: taken(T.mlf[:], C, off16, "off16", "mlf")),
+            "cwc": ("0", lambda: tt(T.cw3[:], T.mlf[:], T.k64[:], Op.add, "mlf k64", "cw3")),
+            "cwd": ("0", lambda: ts(T.cw3[:], T.cw3[:], -3 * BASE, Op.add, rd="cw3", wr="cw3")),
+            "mlf": ("012", lambda: (tt(T.mlf[:, 0:14:2], T.drn[:, 0:7], T.cw3[:, 0:14:2], Op.add, "drn cw3", "mlf"),
+                                    tt(T.mlf[:, 1:14:2], T.drn[:, 0:7], T.cw3[:, 1:14:2], Op.add, "drn cw3", "mlfb"))),
+            "ml": ("012", lambda: cp(T.ml[:], T.mlf[:], "mlf mlfb", "ml")),
+            "mark": ("012", lambda: tt(T.mark[:], T.rs[:].indirect(T.ml[:]), ident, Op.is_equal, "rs rsz ml t0", "mark")),
+            "f0": ("01", lambda: (far(T.mark[:], 0, "mark", 0.0), act(T.mk2[:], T.mark[:], "mark", "mk2", bias=BASE))),
+            "am": ("012", lambda: ts(T.am[:, 0:7], T.ab[:, 4:29:4], float(A), Op.min, rd="ab", wr="am")),
+            "fl": ("012", lambda: tt(T.fl[:], T.ab[:].indirect(LA), T.nt[:], Op.is_le, "ab LA nt", "fl")),
+            "val": ("012", lambda: tt(T.val[:, 0:7], T.ab[:, 0:28:4], T.am[:, 0:7], Op.add, "ab am", "val")),
+            "lk": ("0", lambda: ts(LK, T.tb[:, 0:3], 0.0, Op.mult, c18, Op.add, "t0 c18", "LK")),
+            "vv": ("012", lambda: tt(T.vv[:], T.val[:].indirect(LK), T.nm[:], Op.add, "val LK nm", "vv")),
+            "cs": ("012", lambda: scan(T.cs[:], T.vv[:], T.fl[:], 0.0, Op.max, Op.mult, "vv fl", "cs")),
+            "mw": ("012", lambda: cp(T.mw[:], T.cs[:, 7:48:8], "cs", "mw")),
+            "mr": ("012", lambda: cp(T.mr[:], T.fr[:].indirect(T.mw[:]), "fr frz mw", "mr")),
+            "m4a": ("012", lambda: wrap4(T.f4, "f4", T.mr[:], A, "mr")),
+            "m4b": ("012", lambda: taken4(T.m4[:], T.f4, "f4", A, "m4")),
+            "m16a": ("012", lambda: wrap16(T.mr[:], A, "mr")),
+            "m16b": ("012", lambda: taken(T.m16[:], A, off16, "off16", "m16")),
+            "hr": ("012", lambda: act(T.hr[:, 0:C], ident, "t0", "hr")),
+            "sca": ("012", lambda: cp(T.hr[:].indirect(T.m16[:]), T.fr[:, A:2 * A], "frz m16", "hr")),
+            "hwa": ("012", lambda: wrap4(T.sc2, "sc2", T.hr[:, 0:C], C, "hr")),
+            "hwb": ("012", lambda: taken4(T.hw[:], T.sc2, "sc2", C, "hw")),
+            "xs": ("012", lambda: act(T.xs[:], XY[t][:].indirect(T.m4[:]), "x%d x%db y%d m4" % (t, t, t), "xs")),
+            "lrev": ("0", lambda: ts(Lrev, T.lrf[:], q_, Op.subtract, rd="lrf cf", wr="Lrev")),
+            "rev": ("01", lambda: act(T.rev[:], T.rs[:].indirect(Lrev), "rs rsz Lrev", "rev")),
+            "awa": ("01", lambda: wrap16(T.rev[:], C, "rev")),
+            "awb": ("01", lambda: taken(T.aw[:, 448:462], C, offl, "offl", "aw2")),
+            "nc": ("0", lambda: act(T.nc[:], T.uw0[:, 0:C], "uw0a", "nc", scale=-1.0, bias=3 * BASE)),
+            "ee": ("01", lambda: ts(T.ee[:, 1:28:4], T.drn[:, 0:7], 288.0 if t == 0 else 96.0, Op.add, rd="drn", wr="ee")),
+            "ub": ("01", lambda: scan(T.uw1[:, C:2 * C], T.uw1[:, 0:C], T.nc[:], KEEP, Op.min, Op.add, "uw1a nc", "uw1b")),
+            "pick": ("01", lambda: pick_u(t + 1)),
+        }
+        for i in range(5):
+            steps["n%d" % i] = ("01", lambda i=i: near(bufs[i + 1][0], bufs[i][0], bufs[i + 1][1], bufs[i][1]))
+            if i:
+                steps["f%d" % i] = ("01", lambda i=i: far(bufs[i][0], i, bufs[i][1]))
+        for b in range(4):
+            steps["s%d" % b] = ("012", lambda b=b: unpacked(b, "s"))
+            steps["v%d" % b] = ("012", lambda b=b: unpacked(b, "v"))
+
+        def run(names):
+            for n in names.split():
+                if str(t) in steps[n][0]:
+                    steps[n][1]()
+
+        run(LIST)
         dxk = "dx0 dx1 dx2 dx3 dxz fi%d" % t
         cp(T.pt[:, 0:192], T.dx[:].indirect(T.fin[:, 24 * t:24 * t + 12]), dxk, "pta")
         act(T.pt[:, 192:384], T.dx[:].indirect(T.fin[:, 24 * t + 12:24 * t + 24]), dxk, "ptb")
-        if not last:
-            far(T.da[:], 1, "da")
-        else:
-            act(T.hr[:, 0:C], ident, "t0", "hr")
+        run(MID)
         quant(T.pq[:], T.psc[:], T.pt[:], "pta ptb ptz", "pq")
         for b in range(4):
             mm(4 + b, 128, T.wq[:, 128 * b:128 * b + 128], T.wsc[:, 128 * b:128 * b + 128], T.pq[:], T.psc[:], "wq wsc pq")
@@ -415,37 +413,15 @@ def rank_program(g, core, T, topo):
         send(t, hq[:, 128:128 + A].bitcast(dt.uint8), hq[:, 0:A].bitcast(dt.uint8), "ah%d" % t, "hq%d" % t)
         send(t, hsc[:, 128:128 + A], hsc[:, 0:A], "ah%d" % t, "hq%d" % t)
         arrival(t, "ah%d" % t, 2, "lq%d" % t)
-        if not last:
-            act(T.hr[:, 0:C], ident, "t0", "hr")
-            near(T.db[:], T.da[:], "db", "da")
-            far(T.db[:], 2, "db")
-        if t == 0:
-            ts(Lrev, T.lrf[:], q_, Op.subtract, rd="lrf cf", wr="Lrev")
-            ts(T.cw3[:], T.cw3[:], -3 * BASE, Op.add, rd="cw3", wr="cw3")
-        cp(T.hr[:].indirect(T.m16[:]), T.fr[:, A:2 * A], "frz m16", "hr")
-        if not last:
-            near(T.da[:], T.db[:], "da", "db")
-            far(T.da[:], 3, "da")
-        act(T.xs[:], XY[t][:].indirect(T.m4[:]), "x%d x%db y%d m4" % (t, t, t), "xs")
-        wrap4(T.hr[:, 0:C], C, "hr", T.hw[:], "hw", T.sc2, "sc2")
-        if not last:
-            near(T.db[:], T.da[:], "db", "da")
-            pick_u(t + 1)
-            far(T.db[:], 4, "db")
-            act(T.rev[:], T.rs[:].indirect(Lrev), "rs rsz Lrev", "rev")
-            if t == 0:
-                act(T.nc[:], T.uw0[:, 0:C], "uw0a", "nc", scale=-1.0, bias=3 * BASE)
-            ts(T.ee[:, 1:28:4], T.drn[:, 0:7], 288.0 if t == 0 else 96.0, Op.add, rd="drn", wr="ee")
-            near(T.uw1[:, 0:C], T.db[:], "uw1a", "db")
-            ts(T.aw[:, 448:462], wrap16(T.rev[:], C, "rev"), offl, Op.add, rd="sc offl", wr="aw2")
-        else:
+        run(BACK)
+        if last:
             ts(T.ml1f[:], T.mlf[:], -1.0, Op.add, rd="mlf mlfb", wr="ml1f")
             quant(T.vq[:], T.vs[:], T.vt[:], "vt", "vq")
             tt(T.mlf[:], T.ml1f[:], T.k64[:], Op.max, "ml1f k64", "mlf mlfb")
             cp(T.ml1[:], T.mlf[:], "mlf mlfb", "ml1")
-            tt(T.da[:], T.rs[:].indirect(T.ml1[:]), tbl(1), Op.subtract, "rs rsz ml1 t1", "da")
-            tt(T.db[:], T.da[:], T.mark[:], Op.mult, "da mark", "db")
-            tt(T.da[:], T.db[:], tbl(1), Op.add, "db t1", "da")
+            tt(da, T.rs[:].indirect(T.ml1[:]), tbl(1), Op.subtract, "rs rsz ml1 t1", "da")
+            tt(db, da, T.mark[:], Op.mult, "da mark", "db")
+            tt(da, db, tbl(1), Op.add, "db t1", "da")
             dma("y", T.op[:], T.da[0:128:16, :], "stored", 0, "da", "")
         for b in range(4):
             mm(b, 128, T.eq[:, 128 * b:128 * b + 128], T.es[:, 128 * b:128 * b + 128], hq[:, A:128 + A], hsc[:, A:128 + A],
@@ -459,13 +435,14 @@ def rank_program(g, core, T, topo):
         if not last:
             scores(t + 1)
             send_x(t + 1)
-            scan(T.uw1[:, C:2 * C], T.uw1[:, 0:C], T.nc[:], KEEP, Op.min, Op.add, "uw1a nc", "uw1b")
-            best()
+            run(GAP)
+            for n in "b1 b2 b3 b4 l2 rs".split():
+                one[n]()
 
     mm(7, C, T.vq[:], T.vs[:], T.xq3[:], T.xsc3[:], "vq xq3")
-    dma("y", T.oc[:], T.xq3[:].bitcast(dt.uint8), "stored", 0, "xq3", "")
+    dma("s", T.oc[:], T.xq3[:].bitcast(dt.uint8), "stored", 0, "xq3", "")
     for k in range(4):
-        dma("s", T.osc[4 * k:4 * k + 4, :], T.xsc3[32 * k:32 * k + 4, :], "stored", 0, "xq3", "")
+        dma("ys"[k % 2], T.osc[4 * k:4 * k + 4, :], T.xsc3[32 * k:32 * k + 4, :], "stored", 0, "xq3", "")
     cp(T.yo[:], bank(7, 0, C), "", "yo b7")
     dma("y", T.y[:], T.yo[:], "stored", 0, "yo", "")
     g.sync.wait_ge(T.sem.stored, 16 * 7)

@@ -8,12 +8,16 @@ HUGE = 1.0e29
 LIFT = 256.0
 BASE = 64.0
 
-FIRST = ("uq w1a w1b e2 pm t3 el qx p4 w2a db pick w2b t6 f1 b1 p8 n1 w3a w3b f2 b2 n2 E0 p16 w4a p8b f3 a0 w4b a1 n3 f4 "
-         "b3 t5 b4 t7 nt n4 l2 rs")
-LIST = "cwa k0 am hr drn cwb fl cwc lk val mlf vv ml cs mark s0 s1 mw mr f0 v3 n0 s2"
-MID = "lrev f1"
-BACK = "ee n1 m16a m4a rev f2 m16b awa n2 m4b sca f3 hwa n3 xs hwb f4 pick awb n4 nc"
-GAP = "ub cwd"
+FIRST = ("uq qx w1a c1 pick t3 w1b p4 e2 c2 pm c3 el w2a c4 db w2b t6 f1 b1 c5 p8 n1 w3a c6 w3b b2 E0 f2 p16 n2 p8b f3 w4a a0 "
+         "w4b n3 a1 f4 b3 t5 t7 b4 nt n4 l2 rs")
+ROUND = [
+    "gu ab E1 va fa fl ca E3 cw am fr k0 cwa f4a E2 D fo cwb lk drn s2 val hr cwc mlf vv ml s3 cs mark v1 s0 lrev f0 mw mr pv ps "
+    "n0 pq m16a f1 sr1 sr3 rev vr0 m16b cwd vr2 nc m4a hq n1 pick f2 m4b n2 sca hwa hwb awa f3 xs n3 awb f4 nx n4 xq ub b1 b2 "
+    "b3 ee b4 l2 rs",
+    "gu D ab va fa ca s0 s2 drn cw fl fr hr am f4a mlf fo ml val mark f0 ee vv v1 cs mw smr v3 n0 ps pv f1 pq m4a m16a n1 sr0 "
+    "vr3 sr2 m4b sr1 hq f2 m16b pick n2 sca f3 n3 rev f4 xs hwa awa n4 awb hwb nx xq ub b1 b2 b3 b4 l2 rs",
+    "gu D ab fa va ca cw drn am s0 fr f4a fo fl s3 val mlf hr vv ml s1 o1 s2 cs mw ps mr mark pv pq m16a m4a sr2 sr3 vr0 vq vr1 "
+    "hq m16b o2 o3 sca hwa o4 hwb m4b xs o5 o6 nx xq"]
 
 
 def _sb(n, t):
@@ -30,8 +34,8 @@ for _d, _l in (
         (U16, "fout 72 fin 72 el 14 wl 80 cl 64 ul 24 l1 2 l2 32 cw 6 mw 6 m16 6 m4 24 hw 56 ml 14 ml1 14"),
         (F32, "cf 8 cg 24 tb 1792 p8 224 p16 224 p8b 224 idb 224 da 224 db 224 dg 224 mk2 224 nc 224 idw 14 e1 14 e2 14 pm 14 "
               "aw 464 uw0 464 uw1 464 sc 224 sc2 224 s16 16 s4 8 c16 224 c4 224 cs1 224 ta 128 kt 8 rr 232 gu 32 ee 32 ab 32 "
-              "nv 48 nt 48 nm 48 i48a 48 i48b 48 vv 48 fl 48 cs 48 rs 544 fr 192 f4 96 am 8 val 8 mr 96 hr 320 k64 14 lrf 14 "
-              "cw3 14 drn 8 mlf 14 ml1f 14 mark 224 rev 224 yo 224")):
+              "nv 48 nt 48 nm 48 i48a 48 i48b 48 vv 48 fa 48 fl 48 cs 48 rs 544 fr 192 f4 96 am 8 val 8 mr 96 hr 320 k64 14 "
+              "lrf 14 cw3 14 drn 8 mlf 14 ml1f 14 mark 224 rev 224 yo 224")):
     _w = _l.split()
     for _i in range(0, len(_w), 2):
         SCRATCH[_w[_i]] = _sb(int(_w[_i + 1]), _d)
@@ -183,7 +187,10 @@ def rank_program(g, core, T, topo):
     iota(T.rs[:, 448:544], [[0, 96]], C, 0, "rsz")
     for i, (sh, m) in enumerate([(0, 15), (2, 3), (0, 3), (0, 7), (3, 1), (1, 1)]):
         ts(T.ci[:, i:i + 1], T.pc[:, 0:1], sh, Op.logical_shift_right, m, Op.bitwise_and, "pc", "ci%d" % i)
+    fill(T.rr[:, 0:8], 0.0, "rr0")
+    fill(T.ab[:], 0.0, "ab")
     cp(T.cf[:, 0:6], T.ci[:, 0:6], "ci0 ci1 ci2 ci3 ci4 ci5", "cf")
+    fill(T.cs1[:], 0.0, "cs1")
     ts(T.s16[:], T.tb[:, 0:16], q_, Op.is_equal, DROP, Op.mult, "t0 cf", "s16")
     ts(Lq, T.tb[:, 0:14], 0.0, Op.mult, q_, Op.add, "t0 cf", "Lq")
     ts(T.s4[:], T.tb[:, 0:8], kq, Op.is_equal, DROP, Op.mult, "t0 cf", "s4")
@@ -198,7 +205,6 @@ def rank_program(g, core, T, topo):
     act(T.tp[:, 128:C], T.ta[:, 0:96], "ta", "tpb", scale=-1.0, bias=240.0)
     act(T.c4[:], T.s4[:].indirect(Lh), "s4 Lh", "c4", bias=KEEP)
     ts(off16, q_, KEEP, Op.mult, -15 * KEEP, Op.add, "cf", "off16")
-    fill(T.cs1[:], 0.0, "cs1")
     ts(mul, hi2, -1.0, Op.add, rd="cf", wr="mul")
     ts(lo, hi2, -1.0, Op.mult, 1.0, Op.add, "cf", "lo")
     ts(c9, hh, float(C), Op.mult, 100.0, Op.add, "cf", "c9")
@@ -209,24 +215,16 @@ def rank_program(g, core, T, topo):
     ts(c14, lo, 260.0, Op.mult, 8.0, Op.add, "lo", "c14")
     ts(T.cs1[:, 31:C:32], T.kt[:, 0:7], kq, Op.is_equal, HUGE, Op.mult, "kt cf", "cs1")
     ts(c13, c11, c12, Op.subtract, lo, Op.mult, "c11 c12 lo", "c13")
-    ts(c15, s8, -4.0, Op.mult, 28.0, Op.add, "cf", "c15")
-    ts(c16, s8, -4.0, Op.mult, 25.0, Op.add, "cf", "c16c")
+    ts(T.idw[:], T.tb[:, 0:14], 16.0, Op.mult, q_, Op.add, "t0 cf", "idw")
+    cp(T.ul[:], T.ul_i[:], "ul_i", "ul")
     cp(wl(0), T.par_i[:], "par_i", "w0")
     act(tbl(1), ident.indirect(wl(0)), "t0 w0", "t1")
     act(tbl(2), tbl(1).indirect(wl(0)), "t1 w0", "t2")
-    ts(c17, hh, -12 * KEEP, Op.add, rd="cf", wr="c17")
-    ts(b0, c13, c12, Op.add, rd="c13 c12", wr="b0")
-    ts(b1, c13, c12, Op.add, c14, Op.add, "c13 c12 c14", "b1")
-    ts(LA, T.tb[:, 0:3], 0.0, Op.mult, c15, Op.add, "t0 c15", "LA")
-    ts(LB, T.tb[:, 0:3], 0.0, Op.mult, c16, Op.add, "t0 c16c", "LB")
-    ts(off4, kq, 4 * KEEP, Op.mult, c17, Op.add, "cf c17", "off4")
-    cp(T.ul[:], T.ul_i[:], "ul_i", "ul")
-    ts(T.idw[:], T.tb[:, 0:14], 16.0, Op.mult, q_, Op.add, "t0 cf", "idw")
     ts(T.pm[:], T.par_i[:], off16, Op.subtract, rd="par_i off16", wr="pm")
-    fill(T.rr[:, 0:8], 0.0, "rr0")
     tt(T.e1[:], T.par_i[:], T.idw[:], Op.is_equal, "par_i idw", "e1")
-    fill(T.ab[:], 0.0, "ab")
-    ts(T.ee[:], T.ee[:], 0.0, Op.max, rd="ee", wr="ee")
+    ts(c15, s8, -4.0, Op.mult, 28.0, Op.add, "cf", "c15")
+    ts(c16, s8, -4.0, Op.mult, 25.0, Op.add, "cf", "c16c")
+    ts(c17, hh, -12 * KEEP, Op.add, rd="cf", wr="c17")
 
     def quant_e(b):
         quant(T.eq[:, 128 * b:128 * b + 128], T.es[:, 128 * b:128 * b + 128], T.ez[:, 3 - b:515 - b], "ez", "e%d" % b)
@@ -269,6 +267,12 @@ def rank_program(g, core, T, topo):
     def unpacked(b, q):
         (act if q == "s" else cp)(T.dx[:, b:896:4], bank(b, 0, C), "", "dx%d b%d" % (b, b))
 
+    def relu(b, q):
+        if q == "s":
+            act(T.ht[:, b:384:4], bank(4 + b, 0, A), "", "ht%d b%d" % (b, 4 + b), func=Act.Relu, scale=0.03125)
+        else:
+            ts(T.ht[:, b:384:4], bank(4 + b, 0, A), 0.0, Op.max, 0.03125, Op.mult, "", "ht%d b%d" % (b, 4 + b))
+
     def first_x():
         quant_x(0)
         send_x(0)
@@ -289,6 +293,12 @@ def rank_program(g, core, T, topo):
         "qx": first_x, "E0": lambda: quant_e(0),
         "uq": lambda: quant(T.uq[:], T.us[:], T.ut[:], "ut", "uq"),
         "pick": lambda: (pick_u(0), scores(0)),
+        "c1": lambda: ts(b0, c13, c12, Op.add, rd="c13 c12", wr="b0"),
+        "c2": lambda: ts(b1, c13, c12, Op.add, c14, Op.add, "c13 c12 c14", "b1"),
+        "c3": lambda: ts(LA, T.tb[:, 0:3], 0.0, Op.mult, c15, Op.add, "t0 c15", "LA"),
+        "c4": lambda: ts(LB, T.tb[:, 0:3], 0.0, Op.mult, c16, Op.add, "t0 c16c", "LB"),
+        "c5": lambda: ts(off4, kq, 4 * KEEP, Op.mult, c17, Op.add, "cf c17", "off4"),
+        "c6": lambda: ts(T.ee[:], T.ee[:], 0.0, Op.max, rd="ee", wr="ee"),
         "w1a": lambda: wrap16(tbl(2), C, "t2"), "w2a": lambda: wrap16(tbl(4), C, "t4"),
         "w3a": lambda: wrap16(T.p8[:], C, "p8"), "w4a": lambda: wrap16(T.p16[:], C, "p16"),
         "e2": lambda: tt(T.e2[:], T.sc[:, 15:C:16], T.pm[:], Op.is_equal, "sc pm", "e2"),
@@ -320,124 +330,125 @@ def rank_program(g, core, T, topo):
         uw, uwk = (T.uw0, "uw0a uw0b") if t == 0 else (T.uw1, "uw1a uw1b uw1z")
         fo, fi = T.fout[:, 24 * t:24 * t + 24], T.fin[:, 24 * t:24 * t + 24]
         hq, hsc = T["hq%d" % t], T["hsc%d" % t]
-        last = t == R - 1
-        cp(T.gu[:], uw[:].indirect(T.l1[:]), uwk + " l1a l1b", "gu")
-        scan(T.ab[:, 1:29], T.ee[:, 0:28], T.gu[:, 0:28], 0.0, Op.add, Op.subtract, "ee gu", "ab")
-        tt(T.vv[:], T.ab[:].indirect(LA), T.nv[:], Op.subtract, "ab LA nv", "vv")
-        tt(T.fl[:], T.ab[:].indirect(LB), T.nt[:], Op.is_le, "ab LB nt", "fl")
-        scan(T.cs[:], T.vv[:], T.fl[:], 0.0, Op.min, Op.mult, "vv fl", "cs")
-        ts(T.cw[:], T.cs[:, 7:48:8], -1.0, Op.mult, rd="cs", wr="cw")
-        cp(T.fr[:, 0:A], T.rs[:].indirect(T.cw[:]), "rs rsz cw", "fr")
-        wrap4(T.f4, "f4", T.fr[:, 0:A], A, "fr")
-        taken4(fo, T.f4, "f4", A, "fo%d" % t)
-        send(t, fi, fo, "al%d" % t, "fo%d" % t)
-        arrival(t, "al%d" % t, 1, "fi%d" % t)
-        if t == 0:
-            for b in (1, 2, 3):
-                quant_e(b)
-            iota(T.fr[:, A:2 * A], [[1, A]], C, 0, "frz")
-            iota(T.ht[:, 384:512], [[0, 128]], 0, 0, "htz")
-            iota(T.lrf[:], [[64, 7], [-16, 2]], 31, 0, "lrf")
-            iota(T.uw1[:, 448:464], [[0, 16]], 0, 0, "uw1z")
-        iota(XY[t][:, 896:1280], [[0, 384]], 0, 0, "y%d" % t)
-        for b in range(4):
-            mm(b, C, T.eq[:, 128 * b:128 * b + 128], T.es[:, 128 * b:128 * b + 128], T["aq%d" % t][:], T["asc%d" % t][:], "e%d aq%d" % (b, t))
+        dxk = "dx0 dx1 dx2 dx3 dxz fi%d" % t
+        xk = "x%d x%db y%d y%d_0 y%d_1 y%d_2 y%d_3 hw" % (t, t, t, t, t, t, t)
+
+        def list_out():
+            taken4(fo, T.f4, "f4", A, "fo%d" % t)
+            send(t, fi, fo, "al%d" % t, "fo%d" % t)
+            arrival(t, "al%d" % t, 1, "fi%d" % t)
+            if t == 0:
+                iota(T.fr[:, A:2 * A], [[1, A]], C, 0, "frz")
+                iota(T.ht[:, 384:512], [[0, 128]], 0, 0, "htz")
+                iota(T.lrf[:], [[64, 7], [-16, 2]], 31, 0, "lrf")
+                iota(T.uw1[:, 448:464], [[0, 16]], 0, 0, "uw1z")
+            iota(XY[t][:, 896:1280], [[0, 384]], 0, 0, "y%d" % t)
+
+        def unpack_x():
+            for b in range(4):
+                mm(b, C, T.eq[:, 128 * b:128 * b + 128], T.es[:, 128 * b:128 * b + 128], T["aq%d" % t][:], T["asc%d" % t][:],
+                   "e%d aq%d" % (b, t))
+
+        def layer():
+            quant(T.pq[:], T.psc[:], T.pt[:], "pta ptb ptz", "pq")
+            for b in range(4):
+                mm(4 + b, 128, T.wq[:, 128 * b:128 * b + 128], T.wsc[:, 128 * b:128 * b + 128], T.pq[:], T.psc[:], "wq wsc pq")
+
+        def h_out():
+            quant(hq[:, 0:128], hsc[:, 0:128], T.ht[:], "ht0 ht1 ht2 ht3 htz", "hq%d" % t)
+            send(t, hq[:, 128:128 + A].bitcast(dt.uint8), hq[:, 0:A].bitcast(dt.uint8), "ah%d" % t, "hq%d" % t)
+            send(t, hsc[:, 128:128 + A], hsc[:, 0:A], "ah%d" % t, "hq%d" % t)
+            arrival(t, "ah%d" % t, 2, "lq%d" % t)
+            for b in range(4):
+                mm(b, 128, T.eq[:, 128 * b:128 * b + 128], T.es[:, 128 * b:128 * b + 128], hq[:, A:128 + A], hsc[:, A:128 + A],
+                   "e%d hq%d lq%d" % (b, t, t))
+
+        def new_x():
+            for b in range(4):
+                tt(XY[t][:, 896 + b:1280:4], bank(b, 32, 128), T.xs[:, b:384:4], Op.add, "xs", "y%d_%d b%d" % (t, b, b))
+            act(XY[t + 1][:, 448:896], XY[t][:].indirect(T.hw[:, 28:56]), xk, "x%db" % (t + 1))
+            cp(XY[t + 1][:, 0:448], XY[t][:].indirect(T.hw[:, 0:28]), xk, "x%d" % (t + 1))
+
+        def x_out():
+            quant_x(t + 1)
+            if t < R - 1:
+                scores(t + 1)
+                send_x(t + 1)
+
         bufs = [(T.mk2[:], "mk2"), (da, "da"), (db, "db"), (da, "da"), (db, "db"), (T.uw1[:, 0:C], "uw1a")]
         steps = {
-            "k0": ("0", lambda: (act(c18, s8, "cf", "c18", scale=-1.0, bias=7.0), act(offl, off16, "off16", "offl", bias=LIFT),
-                                 act(T.nm[:], T.nt[:], "nt", "nm", scale=-1.0, bias=-1.0),
-                                 act(T.nm[:, 0:48:8], T.nt[:, 0:48:8], "nt", "nm", bias=float(A)))),
-            "drn": ("012", lambda: tt(T.drn[:, 0:7], T.gu[:, 1:28:4], T.gu[:, 0:28:4], Op.subtract, "gu", "drn")),
-            "cwa": ("0", lambda: wrap16(T.uw0[:, 0:C], C, "uw0a")),
-            "cwb": ("0", lambda: taken(T.mlf[:], C, off16, "off16", "mlf")),
-            "cwc": ("0", lambda: tt(T.cw3[:], T.mlf[:], T.k64[:], Op.add, "mlf k64", "cw3")),
-            "cwd": ("0", lambda: ts(T.cw3[:], T.cw3[:], -3 * BASE, Op.add, rd="cw3", wr="cw3")),
-            "mlf": ("012", lambda: (tt(T.mlf[:, 0:14:2], T.drn[:, 0:7], T.cw3[:, 0:14:2], Op.add, "drn cw3", "mlf"),
-                                    tt(T.mlf[:, 1:14:2], T.drn[:, 0:7], T.cw3[:, 1:14:2], Op.add, "drn cw3", "mlfb"))),
-            "ml": ("012", lambda: cp(T.ml[:], T.mlf[:], "mlf mlfb", "ml")),
-            "mark": ("012", lambda: tt(T.mark[:], T.rs[:].indirect(T.ml[:]), ident, Op.is_equal, "rs rsz ml t0", "mark")),
-            "f0": ("01", lambda: (far(T.mark[:], 0, "mark", 0.0), act(T.mk2[:], T.mark[:], "mark", "mk2", bias=BASE))),
-            "am": ("012", lambda: ts(T.am[:, 0:7], T.ab[:, 4:29:4], float(A), Op.min, rd="ab", wr="am")),
-            "fl": ("012", lambda: tt(T.fl[:], T.ab[:].indirect(LA), T.nt[:], Op.is_le, "ab LA nt", "fl")),
-            "val": ("012", lambda: tt(T.val[:, 0:7], T.ab[:, 0:28:4], T.am[:, 0:7], Op.add, "ab am", "val")),
-            "lk": ("0", lambda: ts(LK, T.tb[:, 0:3], 0.0, Op.mult, c18, Op.add, "t0 c18", "LK")),
-            "vv": ("012", lambda: tt(T.vv[:], T.val[:].indirect(LK), T.nm[:], Op.add, "val LK nm", "vv")),
-            "cs": ("012", lambda: scan(T.cs[:], T.vv[:], T.fl[:], 0.0, Op.max, Op.mult, "vv fl", "cs")),
-            "mw": ("012", lambda: cp(T.mw[:], T.cs[:, 7:48:8], "cs", "mw")),
-            "mr": ("012", lambda: cp(T.mr[:], T.fr[:].indirect(T.mw[:]), "fr frz mw", "mr")),
-            "m4a": ("012", lambda: wrap4(T.f4, "f4", T.mr[:], A, "mr")),
-            "m4b": ("012", lambda: taken4(T.m4[:], T.f4, "f4", A, "m4")),
-            "m16a": ("012", lambda: wrap16(T.mr[:], A, "mr")),
-            "m16b": ("012", lambda: taken(T.m16[:], A, off16, "off16", "m16")),
-            "hr": ("012", lambda: act(T.hr[:, 0:C], ident, "t0", "hr")),
-            "sca": ("012", lambda: cp(T.hr[:].indirect(T.m16[:]), T.fr[:, A:2 * A], "frz m16", "hr")),
-            "hwa": ("012", lambda: wrap4(T.sc2, "sc2", T.hr[:, 0:C], C, "hr")),
-            "hwb": ("012", lambda: taken4(T.hw[:], T.sc2, "sc2", C, "hw")),
-            "xs": ("012", lambda: act(T.xs[:], XY[t][:].indirect(T.m4[:]), "x%d x%db y%d m4" % (t, t, t), "xs")),
-            "lrev": ("0", lambda: ts(Lrev, T.lrf[:], q_, Op.subtract, rd="lrf cf", wr="Lrev")),
-            "rev": ("01", lambda: act(T.rev[:], T.rs[:].indirect(Lrev), "rs rsz Lrev", "rev")),
-            "awa": ("01", lambda: wrap16(T.rev[:], C, "rev")),
-            "awb": ("01", lambda: taken(T.aw[:, 448:462], C, offl, "offl", "aw2")),
-            "nc": ("0", lambda: act(T.nc[:], T.uw0[:, 0:C], "uw0a", "nc", scale=-1.0, bias=3 * BASE)),
-            "ee": ("01", lambda: ts(T.ee[:, 1:28:4], T.drn[:, 0:7], 288.0 if t == 0 else 96.0, Op.add, rd="drn", wr="ee")),
-            "ub": ("01", lambda: scan(T.uw1[:, C:2 * C], T.uw1[:, 0:C], T.nc[:], KEEP, Op.min, Op.add, "uw1a nc", "uw1b")),
-            "pick": ("01", lambda: pick_u(t + 1)),
+            "gu": lambda: cp(T.gu[:], uw[:].indirect(T.l1[:]), uwk + " l1a l1b", "gu"),
+            "ab": lambda: scan(T.ab[:, 1:29], T.ee[:, 0:28], T.gu[:, 0:28], 0.0, Op.add, Op.subtract, "ee gu", "ab"),
+            "va": lambda: tt(T.vv[:], T.ab[:].indirect(LA), T.nv[:], Op.subtract, "ab LA nv", "vv"),
+            "fa": lambda: tt(T.fa[:], T.ab[:].indirect(LB), T.nt[:], Op.is_le, "ab LB nt", "fa"),
+            "ca": lambda: scan(T.cs[:], T.vv[:], T.fa[:], 0.0, Op.min, Op.mult, "vv fa", "cs"),
+            "cw": lambda: ts(T.cw[:], T.cs[:, 7:48:8], -1.0, Op.mult, rd="cs", wr="cw"),
+            "fr": lambda: cp(T.fr[:, 0:A], T.rs[:].indirect(T.cw[:]), "rs rsz cw", "fr"),
+            "f4a": lambda: wrap4(T.f4, "f4", T.fr[:, 0:A], A, "fr"),
+            "fo": list_out, "D": unpack_x, "pq": layer, "hq": h_out, "nx": new_x, "xq": x_out,
+            "pv": lambda: cp(T.pt[:, 0:192], T.dx[:].indirect(T.fin[:, 24 * t:24 * t + 12]), dxk, "pta"),
+            "ps": lambda: act(T.pt[:, 192:384], T.dx[:].indirect(T.fin[:, 24 * t + 12:24 * t + 24]), dxk, "ptb"),
+            "k0": lambda: (act(c18, s8, "cf", "c18", scale=-1.0, bias=7.0), act(offl, off16, "off16", "offl", bias=LIFT),
+                           act(T.nm[:], T.nt[:], "nt", "nm", scale=-1.0, bias=-1.0),
+                           act(T.nm[:, 0:48:8], T.nt[:, 0:48:8], "nt", "nm", bias=float(A))),
+            "drn": lambda: tt(T.drn[:, 0:7], T.gu[:, 1:28:4], T.gu[:, 0:28:4], Op.subtract, "gu", "drn"),
+            "cwa": lambda: wrap16(T.uw0[:, 0:C], C, "uw0a"),
+            "cwb": lambda: taken(T.mlf[:], C, off16, "off16", "mlf"),
+            "cwc": lambda: tt(T.cw3[:], T.mlf[:], T.k64[:], Op.add, "mlf k64", "cw3"),
+            "cwd": lambda: ts(T.cw3[:], T.cw3[:], -3 * BASE, Op.add, rd="cw3", wr="cw3"),
+            "mlf": lambda: (tt(T.mlf[:, 0:14:2], T.drn[:, 0:7], T.cw3[:, 0:14:2], Op.add, "drn cw3", "mlf"),
+                            tt(T.mlf[:, 1:14:2], T.drn[:, 0:7], T.cw3[:, 1:14:2], Op.add, "drn cw3", "mlfb")),
+            "ml": lambda: cp(T.ml[:], T.mlf[:], "mlf mlfb", "ml"),
+            "mark": lambda: tt(T.mark[:], T.rs[:].indirect(T.ml[:]), ident, Op.is_equal, "rs rsz ml t0", "mark"),
+            "f0": lambda: (far(T.mark[:], 0, "mark", 0.0), act(T.mk2[:], T.mark[:], "mark", "mk2", bias=BASE)),
+            "am": lambda: ts(T.am[:, 0:7], T.ab[:, 4:29:4], float(A), Op.min, rd="ab", wr="am"),
+            "fl": lambda: tt(T.fl[:], T.ab[:].indirect(LA), T.nt[:], Op.is_le, "ab LA nt", "fl"),
+            "val": lambda: tt(T.val[:, 0:7], T.ab[:, 0:28:4], T.am[:, 0:7], Op.add, "ab am", "val"),
+            "lk": lambda: ts(LK, T.tb[:, 0:3], 0.0, Op.mult, c18, Op.add, "t0 c18", "LK"),
+            "vv": lambda: tt(T.vv[:], T.val[:].indirect(LK), T.nm[:], Op.add, "val LK nm", "vv"),
+            "cs": lambda: scan(T.cs[:], T.vv[:], T.fl[:], 0.0, Op.max, Op.mult, "vv fl", "cs"),
+            "mw": lambda: cp(T.mw[:], T.cs[:, 7:48:8], "cs", "mw"),
+            "mr": lambda: cp(T.mr[:], T.fr[:].indirect(T.mw[:]), "fr frz mw", "mr"),
+            "smr": lambda: act(T.mr[:], T.fr[:].indirect(T.mw[:]), "fr frz mw", "mr"),
+            "m4a": lambda: wrap4(T.f4, "f4", T.mr[:], A, "mr"),
+            "m4b": lambda: taken4(T.m4[:], T.f4, "f4", A, "m4"),
+            "m16a": lambda: wrap16(T.mr[:], A, "mr"),
+            "m16b": lambda: taken(T.m16[:], A, off16, "off16", "m16"),
+            "hr": lambda: act(T.hr[:, 0:C], ident, "t0", "hr"),
+            "sca": lambda: cp(T.hr[:].indirect(T.m16[:]), T.fr[:, A:2 * A], "frz m16", "hr"),
+            "hwa": lambda: wrap4(T.sc2, "sc2", T.hr[:, 0:C], C, "hr"),
+            "hwb": lambda: taken4(T.hw[:], T.sc2, "sc2", C, "hw"),
+            "xs": lambda: act(T.xs[:], XY[t][:].indirect(T.m4[:]), "x%d x%db y%d m4" % (t, t, t), "xs"),
+            "lrev": lambda: ts(Lrev, T.lrf[:], q_, Op.subtract, rd="lrf cf", wr="Lrev"),
+            "rev": lambda: act(T.rev[:], T.rs[:].indirect(Lrev), "rs rsz Lrev", "rev"),
+            "awa": lambda: wrap16(T.rev[:], C, "rev"),
+            "awb": lambda: taken(T.aw[:, 448:462], C, offl, "offl", "aw2"),
+            "nc": lambda: act(T.nc[:], T.uw0[:, 0:C], "uw0a", "nc", scale=-1.0, bias=3 * BASE),
+            "ee": lambda: ts(T.ee[:, 1:28:4], T.drn[:, 0:7], 288.0 if t == 0 else 96.0, Op.add, rd="drn", wr="ee"),
+            "ub": lambda: scan(T.uw1[:, C:2 * C], T.uw1[:, 0:C], T.nc[:], KEEP, Op.min, Op.add, "uw1a nc", "uw1b"),
+            "pick": lambda: pick_u(t + 1),
+            "o1": lambda: ts(T.ml1f[:], T.mlf[:], -1.0, Op.add, rd="mlf mlfb", wr="ml1f"),
+            "o2": lambda: tt(T.mlf[:], T.ml1f[:], T.k64[:], Op.max, "ml1f k64", "mlf mlfb"),
+            "o3": lambda: cp(T.ml1[:], T.mlf[:], "mlf mlfb", "ml1"),
+            "o4": lambda: tt(da, T.rs[:].indirect(T.ml1[:]), tbl(1), Op.subtract, "rs rsz ml1 t1", "da"),
+            "o5": lambda: tt(db, da, T.mark[:], Op.mult, "da mark", "db"),
+            "o6": lambda: (tt(da, db, tbl(1), Op.add, "db t1", "da"), dma("y", T.op[:], T.da[0:128:16, :], "stored", 0, "da", "")),
+            "vq": lambda: quant(T.vq[:], T.vs[:], T.vt[:], "vt", "vq"),
         }
         for i in range(5):
-            steps["n%d" % i] = ("01", lambda i=i: near(bufs[i + 1][0], bufs[i][0], bufs[i + 1][1], bufs[i][1]))
+            steps["n%d" % i] = lambda i=i: near(bufs[i + 1][0], bufs[i][0], bufs[i + 1][1], bufs[i][1])
             if i:
-                steps["f%d" % i] = ("01", lambda i=i: far(bufs[i][0], i, bufs[i][1]))
+                steps["f%d" % i] = lambda i=i: far(bufs[i][0], i, bufs[i][1])
         for b in range(4):
-            steps["s%d" % b] = ("012", lambda b=b: unpacked(b, "s"))
-            steps["v%d" % b] = ("012", lambda b=b: unpacked(b, "v"))
-
-        def run(names):
-            for n in names.split():
-                if str(t) in steps[n][0]:
-                    steps[n][1]()
-
-        run(LIST)
-        dxk = "dx0 dx1 dx2 dx3 dxz fi%d" % t
-        cp(T.pt[:, 0:192], T.dx[:].indirect(T.fin[:, 24 * t:24 * t + 12]), dxk, "pta")
-        act(T.pt[:, 192:384], T.dx[:].indirect(T.fin[:, 24 * t + 12:24 * t + 24]), dxk, "ptb")
-        run(MID)
-        quant(T.pq[:], T.psc[:], T.pt[:], "pta ptb ptz", "pq")
-        for b in range(4):
-            mm(4 + b, 128, T.wq[:, 128 * b:128 * b + 128], T.wsc[:, 128 * b:128 * b + 128], T.pq[:], T.psc[:], "wq wsc pq")
-        for b in range(4):
-            if b % 2 == 1:
-                act(T.ht[:, b:384:4], bank(4 + b, 0, A), "", "ht%d b%d" % (b, 4 + b), func=Act.Relu, scale=0.03125)
-            else:
-                ts(T.ht[:, b:384:4], bank(4 + b, 0, A), 0.0, Op.max, 0.03125, Op.mult, "", "ht%d b%d" % (b, 4 + b))
-        quant(hq[:, 0:128], hsc[:, 0:128], T.ht[:], "ht0 ht1 ht2 ht3 htz", "hq%d" % t)
-        send(t, hq[:, 128:128 + A].bitcast(dt.uint8), hq[:, 0:A].bitcast(dt.uint8), "ah%d" % t, "hq%d" % t)
-        send(t, hsc[:, 128:128 + A], hsc[:, 0:A], "ah%d" % t, "hq%d" % t)
-        arrival(t, "ah%d" % t, 2, "lq%d" % t)
-        run(BACK)
-        if last:
-            ts(T.ml1f[:], T.mlf[:], -1.0, Op.add, rd="mlf mlfb", wr="ml1f")
-            quant(T.vq[:], T.vs[:], T.vt[:], "vt", "vq")
-            tt(T.mlf[:], T.ml1f[:], T.k64[:], Op.max, "ml1f k64", "mlf mlfb")
-            cp(T.ml1[:], T.mlf[:], "mlf mlfb", "ml1")
-            tt(da, T.rs[:].indirect(T.ml1[:]), tbl(1), Op.subtract, "rs rsz ml1 t1", "da")
-            tt(db, da, T.mark[:], Op.mult, "da mark", "db")
-            tt(da, db, tbl(1), Op.add, "db t1", "da")
-            dma("y", T.op[:], T.da[0:128:16, :], "stored", 0, "da", "")
-        for b in range(4):
-            mm(b, 128, T.eq[:, 128 * b:128 * b + 128], T.es[:, 128 * b:128 * b + 128], hq[:, A:128 + A], hsc[:, A:128 + A],
-               "e%d hq%d lq%d" % (b, t, t))
-        for b in range(4):
-            tt(XY[t][:, 896 + b:1280:4], bank(b, 32, 128), T.xs[:, b:384:4], Op.add, "xs", "y%d_%d b%d" % (t, b, b))
-        xk = "x%d x%db y%d y%d_0 y%d_1 y%d_2 y%d_3 hw" % (t, t, t, t, t, t, t)
-        act(XY[t + 1][:, 448:896], XY[t][:].indirect(T.hw[:, 28:56]), xk, "x%db" % (t + 1))
-        cp(XY[t + 1][:, 0:448], XY[t][:].indirect(T.hw[:, 0:28]), xk, "x%d" % (t + 1))
-        quant_x(t + 1)
-        if not last:
-            scores(t + 1)
-            send_x(t + 1)
-            run(GAP)
-            for n in "b1 b2 b3 b4 l2 rs".split():
-                one[n]()
+            steps["s%d" % b] = lambda b=b: unpacked(b, "s")
+            steps["v%d" % b] = lambda b=b: unpacked(b, "v")
+            steps["sr%d" % b] = lambda b=b: relu(b, "s")
+            steps["vr%d" % b] = lambda b=b: relu(b, "v")
+            steps["E%d" % b] = lambda b=b: quant_e(b)
+        for n in "b1 b2 b3 b4 l2 rs".split():
+            steps[n] = one[n]
+        for n in ROUND[t].split():
+            steps[n]()
 
     mm(7, C, T.vq[:], T.vs[:], T.xq3[:], T.xsc3[:], "vq xq3")
     dma("s", T.oc[:], T.xq3[:].bitcast(dt.uint8), "stored", 0, "xq3", "")

@@ -2,462 +2,502 @@ from concourse.mybir import dt, AluOpType as Op, ActivationFunctionType as Act
 
 C, A, R = 224, 96, 3
 STEP = [1, 2, 4]
+HOME = [False, False, False]
+LEVEL = "sssss"
+DEPTH = "ssss"
+LAZY = 0.5
+SPLIT = True
+TURNS = 3
 F32, BF, I32, U16, MX, U8 = "float32", "bfloat16", "int32", "uint16", "float8_e4m3fn_x4", "uint8"
-KEEP, DROP = 1000.0, -1.0e6
 HUGE = 1.0e29
-LIFT = 256.0
-BASE = 64.0
-
-FIRST = ("uq qx w1a c1 pick t3 w1b p4 e2 c2 pm c3 el w2a c4 db w2b t6 f1 b1 c5 p8 n1 w3a c6 w3b b2 E0 f2 p16 n2 p8b f3 w4a a0 "
-         "w4b n3 a1 f4 b3 t5 t7 b4 nt n4 l2 rs")
-ROUND = [
-    "gu ab E1 va fa fl ca E3 cw am fr k0 cwa f4a E2 D fo cwb lk drn s2 val hr cwc mlf vv ml s3 cs mark v1 s0 lrev f0 mw mr pv ps "
-    "n0 pq m16a f1 sr1 sr3 rev vr0 m16b cwd vr2 nc m4a hq n1 pick f2 m4b n2 sca hwa hwb awa f3 xs n3 awb f4 nx n4 xq ub b1 b2 "
-    "b3 ee b4 l2 rs",
-    "gu D ab va fa ca s0 s2 drn cw fl fr hr am f4a mlf fo ml val mark f0 ee vv v1 cs mw smr v3 n0 ps pv f1 pq m4a m16a n1 sr0 "
-    "vr3 sr2 m4b sr1 hq f2 m16b pick n2 sca f3 n3 rev f4 xs hwa awa n4 awb hwb nx xq ub b1 b2 b3 b4 l2 rs",
-    "gu D ab fa va ca cw drn am s0 fr f4a fo fl s3 val mlf hr vv ml s1 o1 s2 cs mw ps mr mark pv pq m16a m4a sr2 sr3 vr0 vq vr1 "
-    "hq m16b o2 o3 sca hwa o4 hwb m4b xs o5 o6 nx xq"]
-
-
-def _sb(n, t):
-    return ("sbuf", [128, n], t)
-
+HOLD = 512.0
+SLOPE, HALF = 127.0 / 64, 63.0 / 128
+WHOLE = 12582912.0
+BASE = 16.0
+WAIT, ISSUE, START, WAKE, ROWNS, BYTENS, LOAD = 220, 300, 500, 200, 10, 0.1, 2000
 
 SCRATCH = {"ps": ("psum", [128, 4096], F32)}
 for _d, _l in (
         (I32, "par_i 14 ci 8 pc 2 ul_i 24"),
-        (BF, "ut 512 vt 512 ez 520 eone 128 xy0 1280 xy1 1280 xy2 1280 xy3 896 dx 912 pt 512 ht 512 xs 384 tp 224 nn 224 sel 224"),
-        (MX, "wq 512 uq 128 upq 384 vq 128 eq 512 pq 128 xq0 224 xq1 224 xq2 224 xq3 224 aq0 224 aq1 224 aq2 224 hq0 224 hq1 224 hq2 224"),
-        (U8, "wsc 512 us 128 ups 384 vs 128 es 512 psc 128 xsc0 224 xsc1 224 xsc2 224 xsc3 224 asc0 224 asc1 224 asc2 224 "
-             "hsc0 224 hsc1 224 hsc2 224"),
-        (U16, "fout 72 fin 72 el 14 wl 80 cl 64 ul 24 l1 2 l2 32 cw 6 mw 6 m16 6 m4 24 hw 56 ml 14 ml1 14"),
-        (F32, "cf 8 cg 24 tb 1792 p8 224 p16 224 p8b 224 idb 224 da 224 db 224 dg 224 mk2 224 nc 224 idw 14 e1 14 e2 14 pm 14 "
-              "aw 464 uw0 464 uw1 464 sc 224 sc2 224 s16 16 s4 8 c16 224 c4 224 cs1 224 ta 128 kt 8 rr 232 gu 32 ee 32 ab 32 "
-              "nv 48 nt 48 nm 48 i48a 48 i48b 48 vv 48 fa 48 fl 48 cs 48 rs 544 fr 192 f4 96 am 8 val 8 mr 96 hr 320 k64 14 "
-              "lrf 14 cw3 14 drn 8 mlf 14 ml1f 14 mark 224 rev 224 yo 224")):
+        (BF, "ut 512 vt 512 ez 520 eone 128 xy0 1280 xy1 1280 xy2 1280 xy3 896 dx 912 pt 512 ht 512 xs 384 tp 224 nn 224 sel 224 "
+             "tb 1792 p8 224 p16 224 t4b 224 pat 96 c16 224 c4 224 sc 224 sc2 224 ta 224 rs0 640 rs1 640 fr 192 f4 96 "
+             "mr 96 mr4 96 scm 96 scn 96 dd 1792 un 224 ca 224 cb 224 cc 224 dg 224 nd 224 top 224 cum 240"),
+        (MX, "wq 512 uq 128 upq 384 vq 128 eq 512 pq0 224 pq1 224 pq2 224 xq0 224 xq1 224 xq2 224 xq3 224 aq0 224 aq1 224 aq2 224 "
+             "hq0 224 hq1 224 hq2 224"),
+        (U8, "wsc 512 us 128 ups 384 vs 128 es 512 psc0 224 psc1 224 psc2 224 xsc0 224 xsc1 224 xsc2 224 xsc3 224 "
+             "asc0 224 asc1 224 asc2 224 hsc0 224 hsc1 224 hsc2 224"),
+        (U16, "fout 72 fin 72 wl 80 cl 64 ul 24 l1 4 l2 16 cw 6 mw 6 m16 6 m4 24 hw 56 ml 28"),
+        (F32, "cf 8 cg 16 r32 32 px 32 idb 224 aw 448 awm 224 uw1 448 uw2 448 cs1 224 rr 232 gu 16 ee 16 ab 16 gd 16 "
+              "k48 384 vv 48 fa 48 cs 48 vm 48 fl 48 cm 48 sr 32 hr 424 slot 96 sch 224 k14 112 mlf 28 oa 224 yo 224")):
     _w = _l.split()
     for _i in range(0, len(_w), 2):
-        SCRATCH[_w[_i]] = _sb(int(_w[_i + 1]), _d)
+        SCRATCH[_w[_i]] = ("sbuf", [128, int(_w[_i + 1])], _d)
 
-SEMAPHORES = (["nv", "ns", "np", "ng", "ld_par", "ld_x", "ld_u", "ld_w", "ld_v", "stored", "sent"]
-              + ["ax%d" % t for t in range(R)] + ["al%d" % t for t in range(R)] + ["ah%d" % t for t in range(R)])
+SEMAPHORES = (["nv", "ns", "np", "ng", "ld_par", "ld_x", "ld_u", "ld_w", "ld_s", "ld_v", "stored", "sent"]
+              + [n + str(t) for n in ("ax", "al", "ah") for t in range(R)])
+
+
+def v(name, a=0, z=None, s=1):
+    return (name, a, SCRATCH[name][1][1] if z is None else z, s)
+
+
+def by(win, lst):
+    return win + (lst,)
+
+
+def width(x):
+    return 16 * width(x[4]) if len(x) > 4 else len(range(*x[1:4]))
+
+
+def bank(b, a, z):
+    return ("ps", 512 * b + a, 512 * b + z, 1)
 
 
 def rank_program(g, core, T, topo):
     rank = T.rank_of(core)
     if rank is None:
         return
-    Q = {"v": g.vector, "s": g.scalar, "p": g.tensor, "g": g, "y": g.sync}
-    CNT = {"v": "nv", "s": "ns", "p": "np", "g": "ng"}
-    count = {k: 0 for k in CNT}
-    clock = {k: {} for k in Q}
-    wrote, readers = {}, {}
-
-    def wait(q, ev):
-        sem, val, clk = ev
-        if clock[q].get(sem, 0) >= val:
-            return
-        Q[q].wait_ge(T.sem[sem], val)
-        clock[q][sem] = val
-        for k, x in clk.items():
-            if clock[q].get(k, 0) < x:
-                clock[q][k] = x
-
-    def order(q, rd, wr):
-        evs = [wrote[k] for k in rd if k in wrote] + [wrote[k] for k in wr if k in wrote]
-        for k in wr:
-            evs += readers.get(k, [])
-        top = {}
-        for ev in evs:
-            if ev[0] not in top or top[ev[0]][1] < ev[1]:
-                top[ev[0]] = ev
-        for ev in sorted(top.values(), key=lambda e: -len(e[2])):
-            wait(q, ev)
-
-    def note(ev, rd, wr):
-        for k in rd:
-            readers.setdefault(k, []).append(ev)
-        for k in wr:
-            wrote[k] = ev
-            readers[k] = []
-
-    def op(q, fn, rd, wr):
-        rd, wr = rd.split(), wr.split()
-        order(q, rd, wr)
-        fn().then_inc(T.sem[CNT[q]], 1)
-        count[q] += 1
-        note((CNT[q], count[q], dict(clock[q])), rd, wr)
-
-    def dma(q, out, in_, sem, val, rd, wr):
-        rd, wr = rd.split(), wr.split()
-        order(q, rd, wr)
-        Q[q].dma_start(out, in_).then_inc(T.sem[sem], 16)
-        note((sem, val, dict(clock[q])), [], wr)
-
     V, S, P = g.vector, g.scalar, g.tensor
+    calls, seen = [], {}
 
-    def ts(out, in0, s1, op0, s2=None, op1=None, rd="", wr=""):
-        if op1 is None:
-            op("v", lambda: V.tensor_scalar(out, in0, s1, None, op0), rd, wr)
-        else:
-            op("v", lambda: V.tensor_scalar(out, in0, s1, s2, op0, op1), rd, wr)
+    def ap(x, cast=None):
+        if not isinstance(x, tuple):
+            return x
+        a = T[x[0]][:, x[1]:x[2]:x[3]] if x[3] != 1 else T[x[0]][:, x[1]:x[2]]
+        if cast:
+            a = a.bitcast(cast)
+        return a.indirect(ap(x[4])) if len(x) > 4 else a
 
-    def tt(out, a, b, o, rd, wr):
-        op("v", lambda: V.tensor_tensor(out, a, b, o), rd, wr)
+    def call(ways, rd, wr, lag=WAIT, after=(), sem=None):
+        me, deps = len(calls), set(after)
+        rd = [x for x in rd if isinstance(x, tuple)]
+        rd += [x[4] for x in rd + wr if len(x) > 4]
+        for x, w in [(x, False) for x in rd] + [(x, True) for x in wr]:
+            cols = set(range(*x[1:4]))
+            if x[0] == "ps":
+                cols, w = {x[1] // 512}, True
+            deps |= {o for c, ow, o in seen.setdefault(x[0], []) if (w or ow) and o != me and c & cols}
+            seen[x[0]].append((cols, w, me))
+        calls.append({"ways": ways, "deps": deps, "lag": lag, "sem": sem})
+        return me
 
-    def cp(out, a, rd, wr):
-        op("v", lambda: V.tensor_copy(out, a), rd, wr)
+    def ns(out, ins, q="v", both=False):
+        n = width(out)
+        if len(out) > 4:
+            return 50 + 3.2 * n
+        if any(len(x) > 4 for x in ins):
+            return (50 if q == "v" else 65) + 1.3 * n
+        if q == "v" and all(x[0] != "ps" and SCRATCH[x[0]][2] in (BF, U16) for x in [out] + ins):
+            n = n / 2
+        return 0.83 * max(64, n * (2 if both else 1))
 
-    def scan(out, d0, d1, init, o0, o1, rd, wr):
-        op("v", lambda: V.tensor_tensor_scan(out, d0, d1, init, o0, o1), rd, wr)
+    def ts(out, a, s1, o0, s2=None, o1=None):
+        f = (lambda: V.tensor_scalar(ap(out), ap(a), ap(s1), None, o0)) if o1 is None else (
+            lambda: V.tensor_scalar(ap(out), ap(a), ap(s1), ap(s2), o0, o1))
+        call({"v": (ns(out, [a]), f)}, [a, s1, s2], [out])
 
-    def fill(ap, x, wr):
-        op("v", lambda: V.memset(ap, x), "", wr)
+    def tt(out, a, b, o):
+        call({"v": (ns(out, [a, b], both=a[0] != "ps"), lambda: V.tensor_tensor(ap(out), ap(a), ap(b), o))}, [a, b], [out])
 
-    def quant(q, s, src, rd, wr):
-        op("v", lambda: V.quantize_mx(q, s, src), rd, wr)
+    def scan(out, a, b, init, o0, o1):
+        call({"v": (ns(out, [a, b]), lambda: V.tensor_tensor_scan(ap(out), ap(a), ap(b), init, o0, o1))}, [a, b], [out])
 
-    def act(out, a, rd, wr, func=None, bias=None, scale=None):
-        kw = {}
-        if bias is not None:
-            kw["bias"] = bias
-        if scale is not None:
-            kw["scale"] = scale
-        f = func if func is not None else (Act.Identity if kw else Act.Copy)
-        op("s", lambda: S.activation(out, a, f, **kw), rd, wr)
+    def cp(out, a, qs="vs"):
+        ways = {"v": (ns(out, [a]), lambda: V.tensor_copy(ap(out), ap(a))),
+                "s": (ns(out, [a], "s"), lambda: S.activation(ap(out), ap(a), Act.Copy))}
+        call({q: ways[q] for q in qs}, [a], [out])
 
-    def iota(out, pat, base, cm, wr, fl=True):
-        if fl:
-            op("g", lambda: g.iota(out, pat, base, cm, allow_small_or_imprecise_dtypes=True), "", wr)
-        else:
-            op("g", lambda: g.iota(out, pat, base, cm), "", wr)
+    def lin(out, a, scale, bias, qs="vs"):
+        ways = {"v": (ns(out, [a]), lambda: V.tensor_scalar(ap(out), ap(a), ap(scale), ap(bias), Op.mult, Op.add)),
+                "s": (ns(out, [a], "s"), lambda: S.activation(ap(out), ap(a), Act.Identity, bias=ap(bias), scale=ap(scale)))}
+        call({q: ways[q] for q in qs}, [a, scale, bias], [out])
 
-    def mm(bank, n, lq, ls, rq, rs, rd):
-        op("p", lambda: P.matmul_mx(T.ps[:, 512 * bank:512 * bank + n], lq, ls, rq, rs, True, True), rd, "b%d" % bank)
+    def relu(out, a, scale, qs="vs"):
+        ways = {"v": (ns(out, [a]), lambda: V.tensor_scalar(ap(out), ap(a), 0.0, scale, Op.max, Op.mult)),
+                "s": (ns(out, [a], "s"), lambda: S.activation(ap(out), ap(a), Act.Relu, scale=scale))}
+        call({q: ways[q] for q in qs}, [a], [out])
 
-    def bank(b, a, z):
-        return T.ps[:, 512 * b + a:512 * b + z]
+    def iota(out, pat, base, cm=0):
+        kw = {} if SCRATCH[out[0]][2] == I32 else {"allow_small_or_imprecise_dtypes": True}
+        call({"g": (130 + 1.66 * width(out), lambda: g.iota(ap(out), pat, base, cm, **kw))}, [], [out])
+
+    def fill(out, x):
+        call({"v": (ns(out, []), lambda: V.memset(ap(out), x))}, [], [out])
+
+    def quant(q, s, a):
+        call({"v": (12 + 0.22 * width(a), lambda: V.quantize_mx(ap(q), ap(s), ap(a)))}, [a], [q, s])
+
+    def mm(b, lq, ls, rq, rs):
+        out = bank(b, 0, width(rq))
+        call({"p": (0.6 * (width(rq) + 16), lambda: P.matmul_mx(ap(out), ap(lq), ap(ls), ap(rq), ap(rs), True, True))},
+             [lq, ls, rq, rs], [out])
+
+    def load(q, out, src, sem, lag, cast=None):
+        call({q: (60, lambda: Q[q].dma_start(ap(out, cast), src))}, [], [out], lag, sem=(sem, 16))
+
+    def store(q, dst, src, rd):
+        call({q: (60, lambda: Q[q].dma_start(dst, src))}, [rd], [], LOAD, sem=("stored", 0))
 
     nsent = [0]
 
-    def send(t, out, in_, sem, rd):
+    def send(t, sem, pairs):
         peer = T.cores[rank ^ STEP[t]]
         rid, pid, se = topo.addr(peer)
-        order("g", rd.split(), [])
-        g.remote_dma(out, in_, T.sem[sem], T.sem.sent, pid, rid, topo.mask(core, peer))
-        nsent[0] += len(topo.engines(core, peer))
+        ids, time = [], 0
+        for out, a in pairs:
+            cast = dt.uint8 if SCRATCH[a[0]][2] == MX else None
+            ids.append(call({"g": (ISSUE, lambda out=out, a=a, cast=cast: g.remote_dma(
+                ap(out, cast), ap(a, cast), T.sem[sem], T.sem.sent, pid, rid, topo.mask(core, peer)))}, [a], [], START, sem=("sent", 0)))
+            nsent[0] += len(topo.engines(core, peer))
+            time += 16 * (ROWNS + BYTENS * width(a) * {MX: 4, U8: 1, U16: 2}[SCRATCH[a[0]][2]])
+        call({"link": (time, None)}, [], [o for o, a in pairs], WAKE, ids, (sem, len(pairs) * len(topo.engines(peer, core))))
 
-    def arrival(t, sem, calls, key):
-        peer = T.cores[rank ^ STEP[t]]
-        wrote[key] = (sem, calls * len(topo.engines(peer, core)), {})
+    Q = {"v": V, "s": S, "p": P, "g": g, "y": g.sync}
 
     def tbl(i):
-        return T.tb[:, C * i:C * i + C]
+        return v("tb", C * i, C * i + C)
 
-    def wl(i):
-        return T.wl[:, 16 * i:16 * i + 14]
+    def wl(i, a=0, z=14):
+        return v("wl", 16 * i + a, 16 * i + z)
+
+    def part(x, a, z):
+        return (x[0], x[1] + a * x[3], x[1] + z * x[3], x[3])
+
+    def gather(out, win, i, split=False):
+        if split:
+            cp(part(out, 0, 128), by(win, wl(i, 0, 8)), "v")
+            cp(part(out, 128, C), by(win, wl(i, 8, 14)), "s")
+        else:
+            cp(out, by(win, wl(i)))
 
     ident = tbl(0)
-    q_, kq, hh, s8, bit, hi2 = [T.cf[:, i:i + 1] for i in range(6)]
-    (off16, n32, nb, y224, mul, lo, off4, b0, b1, c9, c10, c11, c12, c13, c14, c15, c16, c17, c18,
-     offl) = [T.cg[:, i:i + 1] for i in range(20)]
-    Lq, Lh, LA, LB, LK, Lrev = T.cl[:, 0:14], T.cl[:, 14:28], T.cl[:, 28:31], T.cl[:, 32:35], T.cl[:, 36:39], T.cl[:, 40:54]
-    XY = [T.xy0, T.xy1, T.xy2, T.xy3]
+    q_, k_, h_, s8, bit, kq, hh = [v("cf", i, i + 1) for i in range(7)]
+    m16, m4, off4, k32, nk32, c1, c1b, nb, y224, q2, la, lk, lc = [v("cg", i, i + 1) for i in range(13)]
+    Lq, Lh, Lrev = v("cl", 0, 14), v("cl", 14, 28), v("cl", 28, 42)
+    LA, LB, LC, LK = [v("cl", 44 + 4 * i, 47 + 4 * i) for i in range(4)]
+    i48a, i48b, nt, nv, n48, nm, nv0, nt0 = [v("k48", 48 * i, 48 * i + 48) for i in range(8)]
+    lrf, k64, dw, cw3, idw, e1, e2, lend = [v("k14", 14 * i, 14 * i + 14) for i in range(8)]
 
-    dma("y", T.par_i[:], T.par[:], "ld_par", 16, "", "par_i")
-    dma("s", T.xy0[:, 0:896], T.x[:], "ld_x", 16, "", "x0")
-    dma("y", T.ut[:], T.u[:], "ld_u", 16, "", "ut")
-    dma("y", T.wq[:].bitcast(dt.uint8), T.wc[:], "ld_w", 32, "", "wq")
-    dma("y", T.wsc[:], T.ws[:], "ld_w", 32, "", "wsc")
-    dma("y", T.vt[:], T.v[:], "ld_v", 16, "", "vt")
+    def wrap16(out, buf, src, s2, o1):
+        n = width(src)
+        scan(part(buf, 0, n), v("c16", 0, n), src, 0.0, Op.mult, Op.max)
+        ts(out, (buf[0], 15, n, 16), m16, Op.mult, s2, o1)
 
-    iota(T.pc[:, 0:1], [[0, 1]], 0, 1, "pc", False)
-    iota(ident, [[1, C]], 0, 0, "t0")
-    fill(T.eone[:], 1.0, "eone")
-    fill(T.ez[:], 0.0, "ez")
-    op("g", lambda: g.affine_select(T.ez[:, 3:515:4], T.eone[:], [[-1, 128]], Op.is_equal, 0.0, 0, 1), "eone", "ez")
-    iota(T.kt[:], [[0, 2], [1, 4]], 0, 0, "kt")
-    iota(T.ul_i[:], [[1, 3], [16, 8]], 0, 0, "ul_i", False)
-    iota(T.i48a[:], [[16, 6], [0, 8]], 0, 0, "i48a")
-    iota(T.i48b[:], [[16, 6], [-64, 8]], 448, 0, "i48b")
-    iota(T.ee[:], [[0, 8], [-97, 4]], 97, 0, "ee")
-    iota(T.aw[:, 448:464], [[0, 16]], int(LIFT), 0, "aw2")
-    iota(T.uw0[:, C:464], [[0, 240]], 0, 0, "uw0b")
-    iota(T.rs[:, 448:544], [[0, 96]], C, 0, "rsz")
-    for i, (sh, m) in enumerate([(0, 15), (2, 3), (0, 3), (0, 7), (3, 1), (1, 1)]):
-        ts(T.ci[:, i:i + 1], T.pc[:, 0:1], sh, Op.logical_shift_right, m, Op.bitwise_and, "pc", "ci%d" % i)
-    fill(T.rr[:, 0:8], 0.0, "rr0")
-    fill(T.ab[:], 0.0, "ab")
-    cp(T.cf[:, 0:6], T.ci[:, 0:6], "ci0 ci1 ci2 ci3 ci4 ci5", "cf")
-    fill(T.cs1[:], 0.0, "cs1")
-    ts(T.s16[:], T.tb[:, 0:16], q_, Op.is_equal, DROP, Op.mult, "t0 cf", "s16")
-    ts(Lq, T.tb[:, 0:14], 0.0, Op.mult, q_, Op.add, "t0 cf", "Lq")
-    ts(T.s4[:], T.tb[:, 0:8], kq, Op.is_equal, DROP, Op.mult, "t0 cf", "s4")
-    ts(Lh, T.tb[:, 0:14], 0.0, Op.mult, hh, Op.add, "t0 cf", "Lh")
-    act(n32, kq, "cf", "n32", scale=-32.0)
-    act(nb, bit, "cf", "nb", scale=-1.0, bias=1.0)
-    act(y224, s8, "cf", "y224", scale=float(C), bias=LIFT)
-    act(T.c16[:], T.s16[:].indirect(Lq), "s16 Lq", "c16", bias=KEEP)
-    act(T.ta[:], T.tb[:, 0:128], "t0 n32", "ta", func=Act.Relu, bias=n32)
-    act(T.idb[:], ident, "t0 nb y224", "idb", scale=nb, bias=y224)
-    act(T.tp[:, 0:128], T.ta[:], "ta", "tpa", scale=-1.0, bias=100.0)
-    act(T.tp[:, 128:C], T.ta[:, 0:96], "ta", "tpb", scale=-1.0, bias=240.0)
-    act(T.c4[:], T.s4[:].indirect(Lh), "s4 Lh", "c4", bias=KEEP)
-    ts(off16, q_, KEEP, Op.mult, -15 * KEEP, Op.add, "cf", "off16")
-    ts(mul, hi2, -1.0, Op.add, rd="cf", wr="mul")
-    ts(lo, hi2, -1.0, Op.mult, 1.0, Op.add, "cf", "lo")
-    ts(c9, hh, float(C), Op.mult, 100.0, Op.add, "cf", "c9")
-    ts(c10, hh, 446.0, Op.add, rd="cf", wr="c10")
-    ts(T.cs1[:, 0:C:32], T.kt[:, 0:7], kq, Op.is_equal, -3 * HUGE, Op.mult, "kt cf", "cs1")
-    ts(c11, kq, 32.0, Op.mult, c9, Op.add, "cf c9", "c11")
-    ts(c12, kq, 2.0, Op.mult, c10, Op.add, "cf c10", "c12")
-    ts(c14, lo, 260.0, Op.mult, 8.0, Op.add, "lo", "c14")
-    ts(T.cs1[:, 31:C:32], T.kt[:, 0:7], kq, Op.is_equal, HUGE, Op.mult, "kt cf", "cs1")
-    ts(c13, c11, c12, Op.subtract, lo, Op.mult, "c11 c12 lo", "c13")
-    ts(T.idw[:], T.tb[:, 0:14], 16.0, Op.mult, q_, Op.add, "t0 cf", "idw")
-    cp(T.ul[:], T.ul_i[:], "ul_i", "ul")
-    cp(wl(0), T.par_i[:], "par_i", "w0")
-    act(tbl(1), ident.indirect(wl(0)), "t0 w0", "t1")
-    act(tbl(2), tbl(1).indirect(wl(0)), "t1 w0", "t2")
-    ts(T.pm[:], T.par_i[:], off16, Op.subtract, rd="par_i off16", wr="pm")
-    tt(T.e1[:], T.par_i[:], T.idw[:], Op.is_equal, "par_i idw", "e1")
-    ts(c15, s8, -4.0, Op.mult, 28.0, Op.add, "cf", "c15")
-    ts(c16, s8, -4.0, Op.mult, 25.0, Op.add, "cf", "c16c")
-    ts(c17, hh, -12 * KEEP, Op.add, rd="cf", wr="c17")
+    def wrap4(out, buf, src):
+        n = width(src)
+        scan(part(buf, 0, n), v("c4", 0, n), src, 0.0, Op.mult, Op.max)
+        ts(out, (buf[0], 3, n, 4), m4, Op.mult, off4, Op.add)
 
-    def quant_e(b):
-        quant(T.eq[:, 128 * b:128 * b + 128], T.es[:, 128 * b:128 * b + 128], T.ez[:, 3 - b:515 - b], "ez", "e%d" % b)
+    def level(out, src, i, own=None, q="v", base=0.0, ownbase=0.0):
+        if q == "v":
+            if own is None:
+                own = v("dg")
+                cp(own, src)
+            tt(out, by(src, wl(i)), own, Op.add)
+            return base + ownbase
+        lin(v("dg"), by(src, wl(i)), 1.0, -base, "s")
+        scan(out, v("dg"), own or src, 1000.0, Op.min, Op.add)
+        return ownbase
 
-    def quant_x(t):
-        quant(T["xq%d" % t][:], T["xsc%d" % t][:], XY[t][:, 0:896], "x%d x%db" % (t, t), "xq%d" % t)
+    def piece(name, b, n=128):
+        return v(name, n * b, n * b + n)
 
-    def send_x(t):
-        send(t, T["aq%d" % t][:].bitcast(dt.uint8), T["xq%d" % t][:].bitcast(dt.uint8), "ax%d" % t, "xq%d" % t)
-        send(t, T["asc%d" % t][:], T["xsc%d" % t][:], "ax%d" % t, "xq%d" % t)
-        arrival(t, "ax%d" % t, 2, "aq%d" % t)
+    load("y", v("par_i"), T.par[:], "ld_par", LOAD)
+    load("s", v("xy0", 0, 896), T.x[:], "ld_x", LOAD)
+    load("y", v("ut"), T.u[:], "ld_u", LOAD + 500)
+    load("y", v("wq"), T.wc[:], "ld_w", LOAD + 2000, dt.uint8)
+    load("y", v("wsc"), T.ws[:], "ld_s", LOAD + 2000)
+    load("y", v("vt"), T.v[:], "ld_v", LOAD + 2000)
 
-    def pick_u(t):
-        lst = T.ul[:, 8 * t:8 * t + 8]
-        cp(T.upq[:, 128 * t:128 * t + 128].bitcast(dt.uint32), T.uq[:].bitcast(dt.uint32).indirect(lst), "uq ul", "upq%d" % t)
-        act(T.ups[:, 128 * t:128 * t + 128], T.us[:].indirect(lst), "uq ul", "ups%d" % t)
+    iota(v("pc", 0, 1), [[0, 1]], 0, 1)
+    iota(v("r32"), [[1, 32]], 0)
+    iota(ident, [[1, C]], 1)
+    for i, (sh, m) in enumerate([(0, 15), (1, 7), (0, 1), (0, 7), (3, 1), (2, 3), (0, 3)]):
+        ts(v("ci", i, i + 1), v("pc", 0, 1), sh, Op.logical_shift_right, m, Op.bitwise_and)
+    cp(v("cf", 0, 7), v("ci", 0, 7), "v")
+    ts(v("px", 0, 16), v("r32", 0, 16), q_, Op.subtract)
+    ts(v("px", 16, 32), v("r32", 0, 16), kq, Op.subtract)
+    ts(v("pat", 32, 64), v("px"), 0.0, Op.not_equal)
+    ts(v("pat", 64, 96), v("px"), 1.0, Op.is_equal, HOLD - 1, Op.mult)
+    tt(v("pat", 0, 32), v("pat", 32, 64), v("pat", 64, 96), Op.add)
+    ts(Lq, v("r32", 0, 14), 0.0, Op.mult, q_, Op.add)
+    ts(Lh, v("r32", 0, 14), 0.0, Op.mult, hh, Op.add)
+    cp(v("c16"), by(v("pat", 0, 16), Lq))
+    cp(v("c4"), by(v("pat", 16, 32), Lh))
+    lin(m16, v("pat", 47, 48), 1 / HOLD - 1, 1.0)
+    lin(m4, v("pat", 51, 52), 4 / HOLD - 4, 4.0)
+    lin(off4, hh, 1.0, -4.0)
+    ts(k32, k_, 32.0, Op.mult, 192.0, Op.min)
+    lin(nk32, k32, -1.0, -1.0)
+    lin(c1b, k32, 1.0, 100.0)
+    lin(c1, h_, float(C), c1b)
+    lin(nb, bit, -1.0, 1.0)
+    lin(y224, s8, float(C), -1.0)
+    call({"s": (190, lambda: S.activation(ap(v("ta")), ap(ident), Act.Relu, bias=ap(nk32)))}, [ident, nk32], [v("ta")])
+    lin(v("tp"), v("ta"), -1.0, 100.0)
+    lin(v("idb"), ident, nb, y224)
+    fill(v("cs1"), 0.0)
+    ts(v("cs1", 0, C, 32), v("r32", 0, 7), k_, Op.is_equal, -3 * HUGE, Op.mult)
+    ts(v("cs1", 31, C, 32), v("r32", 0, 7), k_, Op.is_equal, HUGE, Op.mult)
+    fill(v("rr", 0, 8), 0.0)
+    fill(v("ab"), 0.0)
+    fill(v("ee"), 0.0)
+    fill(v("sr"), 0.0)
+    iota(v("ul_i"), [[1, 3], [16, 8]], 0)
+    cp(v("ul"), v("ul_i"), "v")
+    iota(i48a, [[16, 6], [0, 8]], 0)
+    iota(i48b, [[0, 6], [-64, 8]], 448)
+    lin(n48, i48a, 1.0, q_)
+    lin(nt, n48, -SLOPE, 0.0)
+    lin(i48a, i48b, 1.0, HALF)
+    tt(nv, i48a, nt, Op.subtract)
+    lin(nm, n48, -1.0, -1.0)
+    lin(v("k48", 240, 288, 8), v("k48", 192, 240, 8), 1.0, float(A))
+    lin(la, s8, -2.0, 14.0)
+    lin(lk, s8, -1.0, 7.0)
+    ts(LA, v("r32", 0, 3), 0.0, Op.mult, la, Op.add)
+    ts(LB, LA, -1.0, Op.add)
+    ts(LK, v("r32", 0, 3), 0.0, Op.mult, lk, Op.add)
+    iota(nv0, [[32, 6], [2, 8]], -14)
+    iota(nt0, [[-32, 6], [-66, 8]], 462)
+    lin(q2, q_, 2.0, 0.0)
+    lin(nv0, nv0, 1.0, q2)
+    ts(nt0, nt0, q2, Op.subtract)
+    lin(lc, lk, 32.0, 15.0)
+    ts(LC, v("r32", 0, 3), 0.0, Op.mult, lc, Op.add)
+    lin(v("gu", 0, 8), v("r32", 0, 8), 33.0, 0.0)
+    fill(v("cum", 0, 16), 0.0)
+    iota(lrf, [[64, 7], [-32, 2]], 62)
+    iota(k64, [[64, 7], [0, 2]], 0)
+    ts(Lrev, lrf, q2, Op.subtract)
+    fill(v("rs0", 1, 448, 2), C + 1.0)
+    fill(v("rs0", 448), C + 1.0)
+    fill(v("rs1", 448), C + 1.0)
+    iota(v("fr", A), [[2, A]], C + 2)
+    iota(v("slot"), [[1, A]], C + 1)
+    fill(v("dx", 896), 0.0)
+    fill(v("pt", 384), 0.0)
+    fill(v("ht", 384), 0.0)
+    fill(v("eone"), 1.0)
+    fill(v("ez"), 0.0)
+    call({"g": (385, lambda: g.affine_select(ap(v("ez", 3, 515, 4)), ap(v("eone")), [[-1, 128]], Op.is_equal, 0.0, 0, 1))},
+         [v("eone")], [v("ez", 3, 515, 4)])
+    for b in range(4):
+        quant(piece("eq", b), piece("es", b), v("ez", 3 - b, 515 - b))
 
-    def scores(t):
-        mm(7, C, T.upq[:, 128 * t:128 * t + 128], T.ups[:, 128 * t:128 * t + 128], T["xq%d" % t][:], T["xsc%d" % t][:],
-           "upq%d ups%d xq%d" % (t, t, t))
+    cp(wl(0), v("par_i"), "v")
+    gather(tbl(1), ident, 0, SPLIT)
+    gather(tbl(2), tbl(1), 0, SPLIT)
+    wrap16(wl(1), v("sc"), tbl(2), -1.0, Op.add)
+    ts(e2, v("sc", 15, C, 16), m16, Op.mult, -1.0, Op.add)
+    gather(tbl(4), tbl(2), 1, SPLIT)
+    wrap16(wl(2), v("sc"), tbl(4), -1.0, Op.add)
+    gather(v("p8"), tbl(4), 2, SPLIT)
+    wrap16(wl(3), v("sc"), v("p8"), -1.0, Op.add)
+    gather(tbl(3), tbl(2), 0)
+    gather(tbl(5), tbl(4), 0)
+    gather(tbl(6), tbl(4), 1)
+    gather(tbl(7), tbl(3), 2)
+    lin(v("t4b"), tbl(4), bit, 0.0)
+    level(v("aw", 0, C), v("t4b"), 2, v("idb"))
+    gather(v("awm"), v("aw", 0, C), 3, SPLIT)
+    gather(v("aw", C), v("awm"), 3, SPLIT)
+    gather(v("p16"), v("p8"), 3)
+    wrap16(wl(4), v("sc"), v("p16"), -1.0, Op.add)
+    tt(v("un"), tbl(1), ident, Op.not_equal)
+    fill(v("un", 0, C, 32), 0.0)
+    lin(v("ca"), ident, -1.0, 256.0)
+    scan(v("cb"), v("un"), v("ca"), 0.0, Op.mult, Op.max)
+    iota(lend, [[32, 7], [0, 2]], 31)
+    cp(v("ml", 0, 14), lend, "v")
+    lin(v("top"), by(v("cb"), v("ml", 0, 14)), -1.0, 256.0)
+    d1, d2, d4, d8, d16, d24, d32, d2x = [piece("dd", i, C) for i in range(8)]
+    ts(idw, v("r32", 0, 14), 16.0, Op.mult, q_, Op.add)
+    tt(e1, v("par_i"), idw, Op.not_equal)
+    tt(e2, e2, v("par_i"), Op.not_equal)
+    tt(e2, e1, e2, Op.add)
+    cp(v("ml", 14, 28), e2, "v")
+    o = BASE if "s" in DEPTH else 0.0
+    lin(d2, by(ident, v("ml", 14, 28)), 1.0, o - 1, "s")
+    o4 = level(d4, d2, 1, None, DEPTH[0], o, o)
+    o8 = level(d8, d4, 2, None, DEPTH[1], o4, o4)
+    o16 = level(d16, d8, 3, None, DEPTH[2], o8, o8)
+    o32 = level(d32, d16, 4, None, DEPTH[3], o16, o16)
+    lin(d2x, d32, 2.0, 2.0 - 2 * o32)
+    lin(v("nd"), d32, -1.0, A + o32)
+    wrap16(dw, v("sc2"), d2x, -1.0, Op.mult)
+    tt(cw3, dw, k64, Op.add)
 
-    def wrap16(src, n, rd):
-        scan(T.sc[:, 0:n], T.c16[:, 0:n], src, 0.0, Op.add, Op.max, "c16 " + rd, "sc")
-
-    def taken(out, n, off, ko, wr):
-        ts(out, T.sc[:, 15:n:16], off, Op.add, rd="sc " + ko, wr=wr)
-
-    def wrap4(buf, key, src, n, rd):
-        scan(buf[:, 0:n], T.c4[:, 0:n], src, 0.0, Op.add, Op.max, "c4 " + rd, key)
-
-    def taken4(out, buf, key, n, wr):
-        ts(out, buf[:, 3:n:4], 4.0, Op.mult, off4, Op.add, key + " off4", wr)
-
-    def far(src, i, ks, bias=-BASE):
-        act(T.dg[:], src.indirect(wl(i)), "%s w%d" % (ks, i), "dg", bias=bias)
-
-    def near(out, src, ko, ks):
-        scan(out, T.dg[:], src, KEEP, Op.min, Op.add, "dg " + ks, ko)
-
-    def unpacked(b, q):
-        (act if q == "s" else cp)(T.dx[:, b:896:4], bank(b, 0, C), "", "dx%d b%d" % (b, b))
-
-    def relu(b, q):
-        if q == "s":
-            act(T.ht[:, b:384:4], bank(4 + b, 0, A), "", "ht%d b%d" % (b, 4 + b), func=Act.Relu, scale=0.03125)
-        else:
-            ts(T.ht[:, b:384:4], bank(4 + b, 0, A), 0.0, Op.max, 0.03125, Op.mult, "", "ht%d b%d" % (b, 4 + b))
-
-    def first_x():
-        quant_x(0)
-        send_x(0)
-        iota(T.dx[:, 896:912], [[0, 16]], 0, 0, "dxz")
-        iota(T.k64[:], [[64, 7], [0, 2]], 0, 0, "k64")
-        iota(T.val[:], [[0, 8]], 0, 0, "val")
-        iota(T.pt[:, 384:512], [[0, 128]], 0, 0, "ptz")
-
-    da, db = T.da[:], T.db[:]
-    one = {
-        "b1": lambda: scan(T.rr[:, 8:8 + C], T.cs1[:], bank(7, 0, C), -3 * HUGE, Op.add, Op.max, "cs1", "rr b7"),
-        "b2": lambda: tt(T.nn[:], bank(7, 0, C), T.rr[:, 7:7 + C], Op.is_le, "rr rr0", "nn b7"),
-        "b3": lambda: scan(T.sel[:], T.nn[:], T.tp[:], 0.0, Op.mult, Op.max, "nn tpa tpb", "sel"),
-        "b4": lambda: (ts(T.l1[:, 0:1], T.sel[:, 127:128], mul, Op.mult, b0, Op.add, "sel mul b0", "l1a"),
-                       ts(T.l1[:, 1:2], T.sel[:, C - 1:C], mul, Op.mult, b1, Op.add, "sel mul b1", "l1b")),
-        "l2": lambda: ts(T.l2[:], T.aw[:].indirect(T.l1[:]), -LIFT, Op.add, rd="aw0 aw1 aw2 l1a l1b", wr="l2"),
-        "rs": lambda: act(T.rs[:, 0:448], T.tb[:].indirect(T.l2[:, 0:28]), "t0 t1 t2 t3 t4 t5 t6 t7 l2", "rs"),
-        "qx": first_x, "E0": lambda: quant_e(0),
-        "uq": lambda: quant(T.uq[:], T.us[:], T.ut[:], "ut", "uq"),
-        "pick": lambda: (pick_u(0), scores(0)),
-        "c1": lambda: ts(b0, c13, c12, Op.add, rd="c13 c12", wr="b0"),
-        "c2": lambda: ts(b1, c13, c12, Op.add, c14, Op.add, "c13 c12 c14", "b1"),
-        "c3": lambda: ts(LA, T.tb[:, 0:3], 0.0, Op.mult, c15, Op.add, "t0 c15", "LA"),
-        "c4": lambda: ts(LB, T.tb[:, 0:3], 0.0, Op.mult, c16, Op.add, "t0 c16c", "LB"),
-        "c5": lambda: ts(off4, kq, 4 * KEEP, Op.mult, c17, Op.add, "cf c17", "off4"),
-        "c6": lambda: ts(T.ee[:], T.ee[:], 0.0, Op.max, rd="ee", wr="ee"),
-        "w1a": lambda: wrap16(tbl(2), C, "t2"), "w2a": lambda: wrap16(tbl(4), C, "t4"),
-        "w3a": lambda: wrap16(T.p8[:], C, "p8"), "w4a": lambda: wrap16(T.p16[:], C, "p16"),
-        "e2": lambda: tt(T.e2[:], T.sc[:, 15:C:16], T.pm[:], Op.is_equal, "sc pm", "e2"),
-        "pm": lambda: tt(T.pm[:], T.e1[:], T.e2[:], Op.add, "e1 e2", "pm"),
-        "el": lambda: cp(T.el[:], T.pm[:], "pm", "el"),
-        "db": lambda: act(db, ident.indirect(T.el[:]), "t0 el", "db", bias=BASE),
-        "t3": lambda: act(tbl(3), tbl(2).indirect(wl(0)), "t2 w0", "t3"),
-        "p4": lambda: act(tbl(4), tbl(2).indirect(wl(1)), "t2 w1", "t4"),
-        "t5": lambda: cp(tbl(5), tbl(1).indirect(wl(2)), "t1 w2", "t5"),
-        "t6": lambda: cp(tbl(6), tbl(2).indirect(wl(2)), "t2 w2", "t6"),
-        "t7": lambda: act(tbl(7), tbl(3).indirect(wl(2)), "t3 w2", "t7"),
-        "p8": lambda: act(T.p8[:], tbl(4).indirect(wl(2)), "t4 w2", "p8"),
-        "p16": lambda: act(T.p16[:], T.p8[:].indirect(wl(3)), "p8 w3", "p16"),
-        "p8b": lambda: act(T.p8b[:], T.p8[:], "p8 cf", "p8b", scale=bit),
-        "a0": lambda: scan(T.aw[:, 0:C], T.p8b[:], T.idb[:], KEEP, Op.min, Op.add, "p8b idb", "aw0"),
-        "a1": lambda: act(T.aw[:, C:2 * C], T.aw[:, 0:C].indirect(wl(4)), "aw0 w4", "aw1"),
-        "f1": lambda: far(db, 1, "db"), "n1": lambda: near(da, db, "da", "db"),
-        "f2": lambda: far(da, 2, "da"), "n2": lambda: near(db, da, "db", "da"),
-        "f3": lambda: far(db, 3, "db"), "n3": lambda: near(da, db, "da", "db"),
-        "f4": lambda: far(da, 4, "da"), "n4": lambda: near(T.uw0[:, 0:C], da, "uw0a", "da"),
-        "nt": lambda: (act(T.nt[:], T.i48a[:], "i48a cf", "nt", bias=q_), act(T.nv[:], T.i48b[:], "i48b cf", "nv", bias=q_)),
-    }
-    for i in range(1, 5):
-        one["w%db" % i] = lambda i=i: taken(wl(i), C, off16, "off16", "w%d" % i)
-    for n in FIRST.split():
-        one[n]()
+    quant(v("uq"), v("us"), v("ut"))
+    for t in range(R):
+        lst, oq = piece("ul", t, 8), piece("upq", t)
+        call({"v": (216, lambda oq=oq, lst=lst: V.tensor_copy(ap(oq, dt.uint32), ap(by(v("uq"), lst), dt.uint32)))}, [by(v("uq"), lst)], [oq])
+        cp(piece("ups", t), by(v("us"), lst))
+    quant(v("vq"), v("vs"), v("vt"))
 
     for t in range(R):
-        uw, uwk = (T.uw0, "uw0a uw0b") if t == 0 else (T.uw1, "uw1a uw1b uw1z")
-        fo, fi = T.fout[:, 24 * t:24 * t + 24], T.fin[:, 24 * t:24 * t + 24]
-        hq, hsc = T["hq%d" % t], T["hsc%d" % t]
-        dxk = "dx0 dx1 dx2 dx3 dxz fi%d" % t
-        xk = "x%d x%db y%d y%d_0 y%d_1 y%d_2 y%d_3 hw" % (t, t, t, t, t, t, t)
-
-        def list_out():
-            taken4(fo, T.f4, "f4", A, "fo%d" % t)
-            send(t, fi, fo, "al%d" % t, "fo%d" % t)
-            arrival(t, "al%d" % t, 1, "fi%d" % t)
-            if t == 0:
-                iota(T.fr[:, A:2 * A], [[1, A]], C, 0, "frz")
-                iota(T.ht[:, 384:512], [[0, 128]], 0, 0, "htz")
-                iota(T.lrf[:], [[64, 7], [-16, 2]], 31, 0, "lrf")
-                iota(T.uw1[:, 448:464], [[0, 16]], 0, 0, "uw1z")
-            iota(XY[t][:, 896:1280], [[0, 384]], 0, 0, "y%d" % t)
-
-        def unpack_x():
-            for b in range(4):
-                mm(b, C, T.eq[:, 128 * b:128 * b + 128], T.es[:, 128 * b:128 * b + 128], T["aq%d" % t][:], T["asc%d" % t][:],
-                   "e%d aq%d" % (b, t))
-
-        def layer():
-            quant(T.pq[:], T.psc[:], T.pt[:], "pta ptb ptz", "pq")
-            for b in range(4):
-                mm(4 + b, 128, T.wq[:, 128 * b:128 * b + 128], T.wsc[:, 128 * b:128 * b + 128], T.pq[:], T.psc[:], "wq wsc pq")
-
-        def h_out():
-            quant(hq[:, 0:128], hsc[:, 0:128], T.ht[:], "ht0 ht1 ht2 ht3 htz", "hq%d" % t)
-            send(t, hq[:, 128:128 + A].bitcast(dt.uint8), hq[:, 0:A].bitcast(dt.uint8), "ah%d" % t, "hq%d" % t)
-            send(t, hsc[:, 128:128 + A], hsc[:, 0:A], "ah%d" % t, "hq%d" % t)
-            arrival(t, "ah%d" % t, 2, "lq%d" % t)
-            for b in range(4):
-                mm(b, 128, T.eq[:, 128 * b:128 * b + 128], T.es[:, 128 * b:128 * b + 128], hq[:, A:128 + A], hsc[:, A:128 + A],
-                   "e%d hq%d lq%d" % (b, t, t))
-
-        def new_x():
-            for b in range(4):
-                tt(XY[t][:, 896 + b:1280:4], bank(b, 32, 128), T.xs[:, b:384:4], Op.add, "xs", "y%d_%d b%d" % (t, b, b))
-            act(XY[t + 1][:, 448:896], XY[t][:].indirect(T.hw[:, 28:56]), xk, "x%db" % (t + 1))
-            cp(XY[t + 1][:, 0:448], XY[t][:].indirect(T.hw[:, 0:28]), xk, "x%d" % (t + 1))
-
-        def x_out():
-            quant_x(t + 1)
-            if t < R - 1:
-                scores(t + 1)
-                send_x(t + 1)
-
-        bufs = [(T.mk2[:], "mk2"), (da, "da"), (db, "db"), (da, "da"), (db, "db"), (T.uw1[:, 0:C], "uw1a")]
-        steps = {
-            "gu": lambda: cp(T.gu[:], uw[:].indirect(T.l1[:]), uwk + " l1a l1b", "gu"),
-            "ab": lambda: scan(T.ab[:, 1:29], T.ee[:, 0:28], T.gu[:, 0:28], 0.0, Op.add, Op.subtract, "ee gu", "ab"),
-            "va": lambda: tt(T.vv[:], T.ab[:].indirect(LA), T.nv[:], Op.subtract, "ab LA nv", "vv"),
-            "fa": lambda: tt(T.fa[:], T.ab[:].indirect(LB), T.nt[:], Op.is_le, "ab LB nt", "fa"),
-            "ca": lambda: scan(T.cs[:], T.vv[:], T.fa[:], 0.0, Op.min, Op.mult, "vv fa", "cs"),
-            "cw": lambda: ts(T.cw[:], T.cs[:, 7:48:8], -1.0, Op.mult, rd="cs", wr="cw"),
-            "fr": lambda: cp(T.fr[:, 0:A], T.rs[:].indirect(T.cw[:]), "rs rsz cw", "fr"),
-            "f4a": lambda: wrap4(T.f4, "f4", T.fr[:, 0:A], A, "fr"),
-            "fo": list_out, "D": unpack_x, "pq": layer, "hq": h_out, "nx": new_x, "xq": x_out,
-            "pv": lambda: cp(T.pt[:, 0:192], T.dx[:].indirect(T.fin[:, 24 * t:24 * t + 12]), dxk, "pta"),
-            "ps": lambda: act(T.pt[:, 192:384], T.dx[:].indirect(T.fin[:, 24 * t + 12:24 * t + 24]), dxk, "ptb"),
-            "k0": lambda: (act(c18, s8, "cf", "c18", scale=-1.0, bias=7.0), act(offl, off16, "off16", "offl", bias=LIFT),
-                           act(T.nm[:], T.nt[:], "nt", "nm", scale=-1.0, bias=-1.0),
-                           act(T.nm[:, 0:48:8], T.nt[:, 0:48:8], "nt", "nm", bias=float(A))),
-            "drn": lambda: tt(T.drn[:, 0:7], T.gu[:, 1:28:4], T.gu[:, 0:28:4], Op.subtract, "gu", "drn"),
-            "cwa": lambda: wrap16(T.uw0[:, 0:C], C, "uw0a"),
-            "cwb": lambda: taken(T.mlf[:], C, off16, "off16", "mlf"),
-            "cwc": lambda: tt(T.cw3[:], T.mlf[:], T.k64[:], Op.add, "mlf k64", "cw3"),
-            "cwd": lambda: ts(T.cw3[:], T.cw3[:], -3 * BASE, Op.add, rd="cw3", wr="cw3"),
-            "mlf": lambda: (tt(T.mlf[:, 0:14:2], T.drn[:, 0:7], T.cw3[:, 0:14:2], Op.add, "drn cw3", "mlf"),
-                            tt(T.mlf[:, 1:14:2], T.drn[:, 0:7], T.cw3[:, 1:14:2], Op.add, "drn cw3", "mlfb")),
-            "ml": lambda: cp(T.ml[:], T.mlf[:], "mlf mlfb", "ml"),
-            "mark": lambda: tt(T.mark[:], T.rs[:].indirect(T.ml[:]), ident, Op.is_equal, "rs rsz ml t0", "mark"),
-            "f0": lambda: (far(T.mark[:], 0, "mark", 0.0), act(T.mk2[:], T.mark[:], "mark", "mk2", bias=BASE)),
-            "am": lambda: ts(T.am[:, 0:7], T.ab[:, 4:29:4], float(A), Op.min, rd="ab", wr="am"),
-            "fl": lambda: tt(T.fl[:], T.ab[:].indirect(LA), T.nt[:], Op.is_le, "ab LA nt", "fl"),
-            "val": lambda: tt(T.val[:, 0:7], T.ab[:, 0:28:4], T.am[:, 0:7], Op.add, "ab am", "val"),
-            "lk": lambda: ts(LK, T.tb[:, 0:3], 0.0, Op.mult, c18, Op.add, "t0 c18", "LK"),
-            "vv": lambda: tt(T.vv[:], T.val[:].indirect(LK), T.nm[:], Op.add, "val LK nm", "vv"),
-            "cs": lambda: scan(T.cs[:], T.vv[:], T.fl[:], 0.0, Op.max, Op.mult, "vv fl", "cs"),
-            "mw": lambda: cp(T.mw[:], T.cs[:, 7:48:8], "cs", "mw"),
-            "mr": lambda: cp(T.mr[:], T.fr[:].indirect(T.mw[:]), "fr frz mw", "mr"),
-            "smr": lambda: act(T.mr[:], T.fr[:].indirect(T.mw[:]), "fr frz mw", "mr"),
-            "m4a": lambda: wrap4(T.f4, "f4", T.mr[:], A, "mr"),
-            "m4b": lambda: taken4(T.m4[:], T.f4, "f4", A, "m4"),
-            "m16a": lambda: wrap16(T.mr[:], A, "mr"),
-            "m16b": lambda: taken(T.m16[:], A, off16, "off16", "m16"),
-            "hr": lambda: act(T.hr[:, 0:C], ident, "t0", "hr"),
-            "sca": lambda: cp(T.hr[:].indirect(T.m16[:]), T.fr[:, A:2 * A], "frz m16", "hr"),
-            "hwa": lambda: wrap4(T.sc2, "sc2", T.hr[:, 0:C], C, "hr"),
-            "hwb": lambda: taken4(T.hw[:], T.sc2, "sc2", C, "hw"),
-            "xs": lambda: act(T.xs[:], XY[t][:].indirect(T.m4[:]), "x%d x%db y%d m4" % (t, t, t), "xs"),
-            "lrev": lambda: ts(Lrev, T.lrf[:], q_, Op.subtract, rd="lrf cf", wr="Lrev"),
-            "rev": lambda: act(T.rev[:], T.rs[:].indirect(Lrev), "rs rsz Lrev", "rev"),
-            "awa": lambda: wrap16(T.rev[:], C, "rev"),
-            "awb": lambda: taken(T.aw[:, 448:462], C, offl, "offl", "aw2"),
-            "nc": lambda: act(T.nc[:], T.uw0[:, 0:C], "uw0a", "nc", scale=-1.0, bias=3 * BASE),
-            "ee": lambda: ts(T.ee[:, 1:28:4], T.drn[:, 0:7], 288.0 if t == 0 else 96.0, Op.add, rd="drn", wr="ee"),
-            "ub": lambda: scan(T.uw1[:, C:2 * C], T.uw1[:, 0:C], T.nc[:], KEEP, Op.min, Op.add, "uw1a nc", "uw1b"),
-            "pick": lambda: pick_u(t + 1),
-            "o1": lambda: ts(T.ml1f[:], T.mlf[:], -1.0, Op.add, rd="mlf mlfb", wr="ml1f"),
-            "o2": lambda: tt(T.mlf[:], T.ml1f[:], T.k64[:], Op.max, "ml1f k64", "mlf mlfb"),
-            "o3": lambda: cp(T.ml1[:], T.mlf[:], "mlf mlfb", "ml1"),
-            "o4": lambda: tt(da, T.rs[:].indirect(T.ml1[:]), tbl(1), Op.subtract, "rs rsz ml1 t1", "da"),
-            "o5": lambda: tt(db, da, T.mark[:], Op.mult, "da mark", "db"),
-            "o6": lambda: (tt(da, db, tbl(1), Op.add, "db t1", "da"), dma("y", T.op[:], T.da[0:128:16, :], "stored", 0, "da", "")),
-            "vq": lambda: quant(T.vq[:], T.vs[:], T.vt[:], "vt", "vq"),
-        }
-        for i in range(5):
-            steps["n%d" % i] = lambda i=i: near(bufs[i + 1][0], bufs[i][0], bufs[i + 1][1], bufs[i][1])
-            if i:
-                steps["f%d" % i] = lambda i=i: far(bufs[i][0], i, bufs[i][1])
+        n = str(t)
+        xy, xq, xsc, rs, uw = "xy" + n, v("xq" + n), v("xsc" + n), "rs" + str(t % 2), t and v("uw" + n)
+        pq, psc, hq, hsc = "pq" + n, "psc" + n, "hq" + n, "hsc" + n
+        fo, fi = piece("fout", t, 24), piece("fin", t, 24)
+        quant(xq, xsc, v(xy, 0, 896))
+        mm(7, piece("upq", t), piece("ups", t), xq, xsc)
+        if not HOME[t]:
+            send(t, "ax" + n, [(v("aq" + n), xq), (v("asc" + n), xsc)])
+            xq, xsc = v("aq" + n), v("asc" + n)
         for b in range(4):
-            steps["s%d" % b] = lambda b=b: unpacked(b, "s")
-            steps["v%d" % b] = lambda b=b: unpacked(b, "v")
-            steps["sr%d" % b] = lambda b=b: relu(b, "s")
-            steps["vr%d" % b] = lambda b=b: relu(b, "v")
-            steps["E%d" % b] = lambda b=b: quant_e(b)
-        for n in "b1 b2 b3 b4 l2 rs".split():
-            steps[n] = one[n]
-        for n in ROUND[t].split():
-            steps[n]()
+            mm(b, piece("eq", b), piece("es", b), xq, xsc)
+            cp(v("dx", b, 896, 4), bank(b, 0, C))
+        scan(v("rr", 8), v("cs1"), bank(7, 0, C), -3 * HUGE, Op.add, Op.max)
+        tt(v("nn"), bank(7, 0, C), v("rr", 7, 7 + C), Op.is_le)
+        scan(v("sel"), v("nn"), v("tp"), 0.0, Op.mult, Op.max)
+        ts(v("l1", 0, 1), v("sel", C - 1), -1.0, Op.mult, c1, Op.add)
+        cp(v("l2"), by(v("aw"), v("l1", 0, 1)), "v")
+        cp(v(rs, 0, 448, 2), by(v("tb"), v("l2", 0, 14)), "s")
+        if t:
+            cp(v("gu"), by(uw, v("l1", 0, 1)), "v")
+            scan(v("ab", 1, 15), v("gu", 0, 14), v("ee", 0, 14), 0.0, Op.add, Op.add)
+            tt(v("vv"), by(v("ab"), LA), nv, Op.add)
+            tt(v("fa"), by(v("ab"), LB), nt, Op.is_ge)
+            ts(v("sr", 16, 24), v("ab", 0, 16, 2), -1 / SLOPE, Op.mult, WHOLE, Op.add)
+            ts(v("sr", 0, 8), v("sr", 16, 24), WHOLE, Op.subtract)
+        else:
+            tt(v("nn"), by(v("tb"), v("l2", 0, 14)), v("top"), Op.is_equal)
+            scan(v("cum", 16), v("nn"), v("nn"), 0.0, Op.add, Op.add)
+            tt(v("vv"), by(v("cum"), LC), nv0, Op.add)
+            tt(v("fa"), by(v("cum"), LC), nt0, Op.is_ge)
+            lin(v("sr", 16, 24), v("cum", 15, 240, 32), -0.5, 0.0)
+            tt(v("sr", 0, 8), v("sr", 16, 24), v("gu", 0, 8), Op.add)
+        scan(v("cs"), v("vv"), v("fa"), 0.0, Op.max, Op.mult)
+        ts(v("cw"), v("cs", 7, 48, 8), WHOLE, Op.add, WHOLE, Op.subtract)
+        cp(v("fr", 0, A), by(v(rs), v("cw")), "v")
+        wrap4(fo, v("f4"), v("fr", 0, A))
+        if HOME[t]:
+            fi = fo
+        else:
+            send(t, "al" + n, [(fi, fo)])
+        cp(v("pt", 0, 192), by(v("dx"), part(fi, 0, 12)), "v")
+        cp(v("pt", 192, 384), by(v("dx"), part(fi, 12, 24)), "s")
+        quant(v(pq, 0, 128), v(psc, 0, 128), v("pt"))
+        o = 0
+        if HOME[t]:
+            send(t, "al" + n, [(v(pq, 128), v(pq, 0, A)), (v(psc, 128), v(psc, 0, A))])
+            o = 128 - A
+        for b in range(4):
+            mm(4 + b, piece("wq", b), piece("wsc", b), v(pq, 3 * o, 3 * o + 128), v(psc, 3 * o, 3 * o + 128))
+            relu(v("ht", b, 384, 4), bank(4 + b, o, o + A), 0.03125, "vs"[b % 2])
+        quant(v(hq, 0, 128), v(hsc, 0, 128), v("ht"))
+        send(t, "ah" + n, [(v(hq, 128), v(hq, 0, A)), (v(hsc, 128), v(hsc, 0, A))])
+        ts(v("sr", 24, 31), v("sr", 1, 8), float(A), Op.min)
+        tt(v("sr", 8, 15), v("sr", 0, 7), v("sr", 24, 31), Op.add)
+        tt(v("vm"), by(v("sr", 8, 16), LK), nm, Op.add)
+        tt(v("fl"), by(v("sr", 0, 8), LK), n48, Op.is_le)
+        scan(v("cm"), v("vm"), v("fl"), 0.0, Op.max, Op.mult)
+        cp(v("mw"), v("cm", 7, 48, 8), "v")
+        cp(v("mr"), by(v("fr"), v("mw")))
+        ts(v("mr4"), v("mr"), float(C), Op.min)
+        wrap4(v("m4"), v("scn"), v("mr4"))
+        cp(v("xs"), by(v(xy, 0, 896), v("m4")))
+        wrap16(v("m16"), v("scm"), v("mr"), -1.0, Op.add)
+        cp(v("hr", 0, C), ident)
+        cp(by(v("hr"), v("m16")), v("slot"), "v")
+        wrap4(v("hw"), v("sch"), v("hr", 0, C))
+        ts(v("l1", 2, 3), v("sel", C - 1), -1.0, Op.mult, c1b, Op.add)
+        cp(v("gd"), by(d2x, v("l1", 2, 3)))
+        tt(v("mlf", 0, 14), v("gd", 0, 14), cw3, Op.add)
+        cp(v("ml", 0, 14), v("mlf", 0, 14), "v")
+        if t < R - 1:
+            nxt = "uw" + str(t + 1)
+            tt(v("un"), by(v(rs), v("ml", 0, 14)), ident, Op.not_equal)
+            o = BASE if "s" in LEVEL else 0.0
+            if o:
+                lin(v("cc"), v("un"), 1.0, o)
+            o = level(v("ca"), v("un"), 0, v("cc" if o else "un"), LEVEL[0], 0.0, o)
+            for i in range(1, 5):
+                o = level(v(("ca", "cb")[i % 2]), v(("cb", "ca")[i % 2]), i, None, LEVEL[i], o, o)
+            lin(v(nxt, 0, C), v("ca"), -SLOPE, o * SLOPE)
+            scan(v("cb"), v("ca"), v("nd"), 1000.0, Op.min, Op.add)
+            lin(v(nxt, C), v("cb"), -SLOPE, (o + A) * SLOPE)
+            lin(v("ee", 1, 14, 2), v("gd", 0, 14, 2), -SLOPE / 2, 0.0)
+            cp(v("rs" + str(1 - t % 2), 1, 448, 2), by(v(rs), Lrev))
+        else:
+            ts(v("mlf", 14, 28), v("mlf", 0, 14), -2.0, Op.add)
+            tt(v("mlf", 14, 28), v("mlf", 14, 28), k64, Op.max)
+            cp(v("ml", 14, 28), v("mlf", 14, 28), "v")
+            tt(v("un"), by(v(rs), v("ml", 0, 14)), ident, Op.is_equal)
+            tt(v("ca"), by(v(rs), v("ml", 14, 28)), tbl(1), Op.subtract)
+            tt(v("cb"), v("ca"), v("un"), Op.mult)
+            tt(v("ca"), v("cb"), tbl(1), Op.add)
+            lin(v("oa"), v("ca"), 1.0, -1.0)
+            store("y", T.op[:], T.oa[0:128:16, :], v("oa"))
+        for b in range(4):
+            mm(b, piece("eq", b), piece("es", b), v(hq, A), v(hsc, A))
+            tt(v(xy, 896 + b, 1280, 4), bank(b, 128 - A, 128), v("xs", b, 384, 4), Op.add)
+        cp(v("xy" + str(t + 1), 0, 448), by(v(xy), v("hw", 0, 28)), "v")
+        cp(v("xy" + str(t + 1), 448, 896), by(v(xy), v("hw", 28, 56)), "s")
 
-    mm(7, C, T.vq[:], T.vs[:], T.xq3[:], T.xsc3[:], "vq xq3")
-    dma("s", T.oc[:], T.xq3[:].bitcast(dt.uint8), "stored", 0, "xq3", "")
+    quant(v("xq3"), v("xsc3"), v("xy3"))
+    mm(7, v("vq"), v("vs"), v("xq3"), v("xsc3"))
+    store("s", T.oc[:], ap(v("xq3"), dt.uint8), v("xq3"))
     for k in range(4):
-        dma("ys"[k % 2], T.osc[4 * k:4 * k + 4, :], T.xsc3[32 * k:32 * k + 4, :], "stored", 0, "xq3", "")
-    cp(T.yo[:], bank(7, 0, C), "", "yo b7")
-    dma("y", T.y[:], T.yo[:], "stored", 0, "yo", "")
+        store("ys"[k % 2], T.osc[4 * k:4 * k + 4, :], T.xsc3[32 * k:32 * k + 4, :], v("xsc3"))
+    cp(v("yo"), bank(7, 0, C), "v")
+    store("y", T.y[:], T.yo[:], v("yo"))
+
+    def place(rank_of, before):
+        busy, plan = {}, {}
+        for i in sorted(range(len(calls)), key=lambda i: -rank_of[i]):
+            ready = max([plan[d][1] + lag for d, lag in before[i]] + [0])
+            best = None
+            for q, (time, f) in calls[i]["ways"].items():
+                at = ready
+                for a, z in busy.setdefault(q, []):
+                    if at + time <= a:
+                        break
+                    at = max(at, z)
+                worth = at + time * (1 + LAZY * (q == "v"))
+                if best is None or worth < best[0]:
+                    best = (worth, at, at + time, q)
+            plan[i] = best[1:]
+            busy[best[3]] = sorted(busy[best[3]] + [best[1:3]])
+        return plan
+
+    ahead = [[(d, calls[d]["lag"]) for d in c["deps"]] for c in calls]
+    behind = [[] for c in calls]
+    tail = [0.0] * len(calls)
+    for i in reversed(range(len(calls))):
+        tail[i] += min(w[0] for w in calls[i]["ways"].values()) + calls[i]["lag"]
+        for d, lag in ahead[i]:
+            tail[d] = max(tail[d], tail[i])
+            behind[d].append((i, lag))
+    plans = [place(tail, ahead)]
+    for turn in range(TURNS):
+        back = place([plans[-1][i][1] for i in range(len(calls))], behind)
+        plans.append(place([back[i][1] for i in range(len(calls))], ahead))
+    plan = min(plans, key=lambda p: max(e[1] for e in p.values()))
+
+    count = {q: 0 for q in "vspg"}
+    clock = {q: {} for q in Q}
+    for i in sorted(plan, key=lambda i: plan[i][0]):
+        c, q = calls[i], plan[i][2]
+        if q == "link":
+            c["ev"] = c["sem"] + ({},)
+            continue
+        for sem, val, known in sorted([calls[d]["ev"] for d in c["deps"]], key=lambda e: (-len(e[2]), e[0], -e[1])):
+            if clock[q].get(sem, 0) < val:
+                Q[q].wait_ge(T.sem[sem], val)
+                for k, x in list(known.items()) + [(sem, val)]:
+                    clock[q][k] = max(clock[q].get(k, 0), x)
+        done = c["ways"][q][1]()
+        if c["sem"] is None:
+            count[q] += 1
+            done.then_inc(T.sem["n" + q], 1)
+            c["ev"] = ("n" + q, count[q], dict(clock[q]))
+        else:
+            if q != "g":
+                done.then_inc(T.sem[c["sem"][0]], 16)
+            c["ev"] = c["sem"] + (dict(clock[q]),)
     g.sync.wait_ge(T.sem.stored, 16 * 7)
     g.wait_ge(T.sem.sent, nsent[0])
-    for q in CNT:
-        if clock[q].get(CNT[q], 0) < count[q]:
-            Q[q].wait_ge(T.sem[CNT[q]], count[q])
+    for q in count:
+        Q[q].wait_ge(T.sem["n" + q], count[q])

@@ -2,39 +2,45 @@ from concourse.mybir import dt, AluOpType as Op, ActivationFunctionType as Act
 
 C, A, R = 224, 96, 3
 STEP = [1, 2, 4]
-HOME = [False, False, False]
-LEVEL = "sssss"
-DEPTH = "ssss"
-LAZY = 0.5
+SOFT = 0
+LAZY = 1.0
 SPLIT = True
 TURNS = 3
+DXQ = "s"
+GFILL = True
+SOON = 0
+PARTS = ((0, 14),)
+PARTS2 = ((0, 14),)
+HALVES = ((0, 128), (128, C))
+CUTS = ((0, 16), (16, 32), (32, 42), (42, 56))
 F32, BF, I32, U16, MX, U8 = "float32", "bfloat16", "int32", "uint16", "float8_e4m3fn_x4", "uint8"
 HUGE = 1.0e29
 HOLD = 512.0
 SLOPE, HALF = 127.0 / 64, 63.0 / 128
 WHOLE = 12582912.0
-BASE = 16.0
-WAIT, ISSUE, START, WAKE, ROWNS, BYTENS, LOAD = 220, 300, 500, 200, 10, 0.1, 2000
+BIG = 2048.0
+BASE, DEEP, FAR = 16.0, 1052.0, 262144.0
+WAIT, ISSUE, START, WAKE, ROWNS, BYTENS, LOAD = 220, 700, 200, 300, 5, 0.04, 2100
 
 SCRATCH = {"ps": ("psum", [128, 4096], F32)}
 for _d, _l in (
-        (I32, "par_i 14 ci 8 pc 2 ul_i 24"),
-        (BF, "ut 512 vt 512 ez 520 eone 128 xy0 1280 xy1 1280 xy2 1280 xy3 896 dx 912 pt 512 ht 512 xs 384 tp 224 nn 224 sel 224 "
+        (I32, "par_i 14 ci 10 pc 6 ul_i 24"),
+        (BF, "ut 512 vt 512 ez 520 eone 128 xy0 1408 xy1 1408 xy2 1408 xy3 1024 dx 912 pt 512 ht 512 xs 384 tp 224 nn 224 sel 224 "
              "tb 1792 p8 224 p16 224 t4b 224 pat 96 c16 224 c4 224 sc 224 sc2 224 ta 224 rs0 640 rs1 640 fr 192 f4 96 "
-             "mr 96 mr4 96 scm 96 scn 96 dd 1792 un 224 ca 224 cb 224 cc 224 dg 224 nd 224 top 224 cum 240"),
-        (MX, "wq 512 uq 128 upq 384 vq 128 eq 512 pq0 224 pq1 224 pq2 224 xq0 224 xq1 224 xq2 224 xq3 224 aq0 224 aq1 224 aq2 224 "
+             "mr 96 mr4 96 scm 96 scn 96 dd 240 t64 224 un 224 ca 224 cb 224 cc 224 dg 224 top 224 cum 240"),
+        (MX, "wq 512 uq 128 upq 384 vq 128 eq 512 pq 128 xq0 256 xq1 256 xq2 256 xq3 256 aq0 224 aq1 224 aq2 224 "
              "hq0 224 hq1 224 hq2 224"),
-        (U8, "wsc 512 us 128 ups 384 vs 128 es 512 psc0 224 psc1 224 psc2 224 xsc0 224 xsc1 224 xsc2 224 xsc3 224 "
+        (U8, "wsc 512 us 128 ups 384 vs 128 es 512 psc 128 xsc0 256 xsc1 256 xsc2 256 xsc3 256 "
              "asc0 224 asc1 224 asc2 224 hsc0 224 hsc1 224 hsc2 224"),
-        (U16, "fout 72 fin 72 wl 80 cl 64 ul 24 l1 4 l2 16 cw 6 mw 6 m16 6 m4 24 hw 56 ml 28"),
-        (F32, "cf 8 cg 16 r32 32 px 32 idb 224 aw 448 awm 224 uw1 448 uw2 448 cs1 224 rr 232 gu 16 ee 16 ab 16 gd 16 "
-              "k48 384 vv 48 fa 48 cs 48 vm 48 fl 48 cm 48 sr 32 hr 424 slot 96 sch 224 k14 112 mlf 28 oa 224 yo 224")):
+        (U16, "fout 72 fin 72 wl 80 cl 64 ul 24 l1 8 l2 18 cw 6 mw 6 m16 6 m4 24 hw 56 ml 28"),
+        (F32, "cf 10 cg 48 r32 32 idb 224 aw 456 awm 224 uw1 456 uw2 456 cs1 224 rr 232 gu 96 mz 96 ab 96 ee 16 gd 16 "
+              "nd 224 r1 224 r2 224 ff 1344 k48 192 vv 48 fa 48 cs 48 vm 48 fl 48 cm 48 sr 32 hr 424 slot 96 sch 224 k14 126 mlf 28 oa 224 yo 224")):
     _w = _l.split()
     for _i in range(0, len(_w), 2):
         SCRATCH[_w[_i]] = ("sbuf", [128, int(_w[_i + 1])], _d)
 
 SEMAPHORES = (["nv", "ns", "np", "ng", "ld_par", "ld_x", "ld_u", "ld_w", "ld_s", "ld_v", "stored", "sent"]
-              + [n + str(t) for n in ("ax", "al", "ah") for t in range(R)])
+              + [n + str(t) for n in ("ax", "ay", "al", "ah") for t in range(R)])
 
 
 def v(name, a=0, z=None, s=1):
@@ -63,7 +69,7 @@ def rank_program(g, core, T, topo):
     def ap(x, cast=None):
         if not isinstance(x, tuple):
             return x
-        a = T[x[0]][:, x[1]:x[2]:x[3]] if x[3] != 1 else T[x[0]][:, x[1]:x[2]]
+        a = T[x[0]][:, x[1]:(x[2] if x[2] >= 0 else None):x[3]] if x[3] != 1 else T[x[0]][:, x[1]:x[2]]
         if cast:
             a = a.bitcast(cast)
         return a.indirect(ap(x[4])) if len(x) > 4 else a
@@ -100,7 +106,7 @@ def rank_program(g, core, T, topo):
         call({"v": (ns(out, [a, b], both=a[0] != "ps"), lambda: V.tensor_tensor(ap(out), ap(a), ap(b), o))}, [a, b], [out])
 
     def scan(out, a, b, init, o0, o1):
-        call({"v": (ns(out, [a, b]), lambda: V.tensor_tensor_scan(ap(out), ap(a), ap(b), init, o0, o1))}, [a, b], [out])
+        call({"v": (ns(out, [a, b]), lambda: V.tensor_tensor_scan(ap(out), ap(a), ap(b), ap(init), o0, o1))}, [a, b, init], [out])
 
     def cp(out, a, qs="vs"):
         ways = {"v": (ns(out, [a]), lambda: V.tensor_copy(ap(out), ap(a))),
@@ -119,10 +125,13 @@ def rank_program(g, core, T, topo):
 
     def iota(out, pat, base, cm=0):
         kw = {} if SCRATCH[out[0]][2] == I32 else {"allow_small_or_imprecise_dtypes": True}
-        call({"g": (130 + 1.66 * width(out), lambda: g.iota(ap(out), pat, base, cm, **kw))}, [], [out])
+        call({"g": (180 + 2.3 * width(out), lambda: g.iota(ap(out), pat, base, cm, **kw))}, [], [out])
 
     def fill(out, x):
-        call({"v": (ns(out, []), lambda: V.memset(ap(out), x))}, [], [out])
+        ways = {"v": (ns(out, []), lambda: V.memset(ap(out), x))}
+        if x == int(x) and GFILL:
+            ways["g"] = (180 + 2.3 * width(out), lambda: g.iota(ap(out), [[0, width(out)]], int(x), 0, allow_small_or_imprecise_dtypes=True))
+        call(ways, [], [out])
 
     def quant(q, s, a):
         call({"v": (12 + 0.22 * width(a), lambda: V.quantize_mx(ap(q), ap(s), ap(a)))}, [a], [q, s])
@@ -171,12 +180,13 @@ def rank_program(g, core, T, topo):
             cp(out, by(win, wl(i)))
 
     ident = tbl(0)
-    q_, k_, h_, s8, bit, kq, hh = [v("cf", i, i + 1) for i in range(7)]
-    m16, m4, off4, k32, nk32, c1, c1b, nb, y224, q2, la, lk, lc = [v("cg", i, i + 1) for i in range(13)]
-    Lq, Lh, Lrev = v("cl", 0, 14), v("cl", 14, 28), v("cl", 28, 42)
-    LA, LB, LC, LK = [v("cl", 44 + 4 * i, 47 + 4 * i) for i in range(4)]
-    i48a, i48b, nt, nv, n48, nm, nv0, nt0 = [v("k48", 48 * i, 48 * i + 48) for i in range(8)]
-    lrf, k64, dw, cw3, idw, e1, e2, lend = [v("k14", 14 * i, 14 * i + 14) for i in range(8)]
+    q_, q1, k_, h_, s8, bit, kq, kq1, hh = [v("cf", i, i + 1) for i in range(9)]
+    m16, m4, off4, z0, nk32, c1, c1b, nb, y224, q2, nq, lk, lc, q225, later = [v("cg", i, i + 1) for i in range(15)]
+    c6, k8, k33 = v("cg", 16, 22), v("cg", 24, 32), v("cg", 32, 40)
+    Lq, Lh, Lrev, Ltree = [v("cl", 14 * i, 14 * i + 14) for i in range(4)]
+    LC, LK = v("cl", 56, 59), v("cl", 60, 63)
+    n48, nm, nv0, nt0 = [v("k48", 48 * i, 48 * i + 48) for i in range(4)]
+    lrf, k64, dw, cw3, spare, e1, e2, lend, ltr = [v("k14", 14 * i, 14 * i + 14) for i in range(9)]
 
     def wrap16(out, buf, src, s2, o1):
         n = width(src)
@@ -188,16 +198,21 @@ def rank_program(g, core, T, topo):
         scan(part(buf, 0, n), v("c4", 0, n), src, 0.0, Op.mult, Op.max)
         ts(out, (buf[0], 3, n, 4), m4, Op.mult, off4, Op.add)
 
-    def level(out, src, i, own=None, q="v", base=0.0, ownbase=0.0):
-        if q == "v":
-            if own is None:
-                own = v("dg")
-                cp(own, src)
-            tt(out, by(src, wl(i)), own, Op.add)
-            return base + ownbase
-        lin(v("dg"), by(src, wl(i)), 1.0, -base, "s")
-        scan(out, v("dg"), own or src, 1000.0, Op.min, Op.add)
-        return ownbase
+    def doubled(outs, twin, far, src, own, base):
+        lift = 0.0
+        for i, out in enumerate(outs):
+            if i % 2:
+                for a, z in PARTS:
+                    tt(part(out, 16 * a, 16 * z), by(src, wl(i, a, z)), part(twin, 16 * a, 16 * z), Op.add)
+                lift *= 2
+            else:
+                for a, z in PARTS2:
+                    lin(part(far, 16 * a, 16 * z), by(src, wl(i, a, z)), 1.0, -lift, "s")
+                for o in [out, twin][:len(outs) - i]:
+                    scan(o, far, own, FAR, Op.min, Op.add)
+                lift = max(lift, base)
+            src = own = out
+        return lift
 
     def piece(name, b, n=128):
         return v(name, n * b, n * b + n)
@@ -209,17 +224,18 @@ def rank_program(g, core, T, topo):
     load("y", v("wsc"), T.ws[:], "ld_s", LOAD + 2000)
     load("y", v("vt"), T.v[:], "ld_v", LOAD + 2000)
 
-    iota(v("pc", 0, 1), [[0, 1]], 0, 1)
+    iota(v("pc"), [[5, 2], [1, 3]], 15, 1)
     iota(v("r32"), [[1, 32]], 0)
     iota(ident, [[1, C]], 1)
-    for i, (sh, m) in enumerate([(0, 15), (1, 7), (0, 1), (0, 7), (3, 1), (2, 3), (0, 3)]):
-        ts(v("ci", i, i + 1), v("pc", 0, 1), sh, Op.logical_shift_right, m, Op.bitwise_and)
-    cp(v("cf", 0, 7), v("ci", 0, 7), "v")
-    ts(v("px", 0, 16), v("r32", 0, 16), q_, Op.subtract)
-    ts(v("px", 16, 32), v("r32", 0, 16), kq, Op.subtract)
-    ts(v("pat", 32, 64), v("px"), 0.0, Op.not_equal)
-    ts(v("pat", 64, 96), v("px"), 1.0, Op.is_equal, HOLD - 1, Op.mult)
-    tt(v("pat", 0, 32), v("pat", 32, 64), v("pat", 64, 96), Op.add)
+    ts(v("ci", 0, 2), v("pc", 1, 3), 15, Op.bitwise_and)
+    cp(v("cf", 0, 2), v("ci", 0, 2), "v")
+    for i, (c, sh, m) in enumerate([(0, 1, 7), (0, 0, 1), (1, 0, 7), (1, 3, 1), (1, 2, 3), (3, 2, 3), (1, 0, 3)]):
+        ts(v("ci", i + 2, i + 3), v("pc", c, c + 1), sh, Op.logical_shift_right, m, Op.bitwise_and)
+    cp(v("cf", 2, 9), v("ci", 2, 9), "v")
+    for a, at, nxt in ((0, q_, q1), (16, kq, kq1)):
+        ts(v("pat", 32 + a, 48 + a), v("r32", 0, 16), at, Op.not_equal)
+        ts(v("pat", 64 + a, 80 + a), v("r32", 0, 16), nxt, Op.is_equal, HOLD - 1, Op.mult)
+        tt(v("pat", a, a + 16), v("pat", 32 + a, 48 + a), v("pat", 64 + a, 80 + a), Op.add)
     ts(Lq, v("r32", 0, 14), 0.0, Op.mult, q_, Op.add)
     ts(Lh, v("r32", 0, 14), 0.0, Op.mult, hh, Op.add)
     cp(v("c16"), by(v("pat", 0, 16), Lq))
@@ -227,36 +243,48 @@ def rank_program(g, core, T, topo):
     lin(m16, v("pat", 47, 48), 1 / HOLD - 1, 1.0)
     lin(m4, v("pat", 51, 52), 4 / HOLD - 4, 4.0)
     lin(off4, hh, 1.0, -4.0)
-    ts(k32, k_, 32.0, Op.mult, 192.0, Op.min)
-    lin(nk32, k32, -1.0, -1.0)
-    lin(c1b, k32, 1.0, 100.0)
+    lin(nk32, k_, -32.0, -1.0)
+    lin(c1b, k_, 32.0, 100.0)
     lin(c1, h_, float(C), c1b)
+    ts(z0, q_, 0.0, Op.is_equal)
+    lin(c6, v("r32", 0, 6), z0, c1)
+    lin(nq, q_, SLOPE, 80 * SLOPE + HALF)
+    for t in (1, 2):
+        fill(v("uw%d" % t, 454), 0.0)
+        lin(v("uw%d" % t, 448, 454), v("r32", 0, 6), -16 * SLOPE, nq)
+    fill(v("aw", 448), 0.0)
+    fill(v("dd", C), 0.0)
+    for a, s, x in ((1, 2, BIG), (0, 2, 1 / BIG), (0, 16, 1.0), (15, 16, 0.0)):
+        fill(v("mz", a, A, s), x)
+    iota(v("r1"), [[-64, 7], [0, 32]], -1000)
+    iota(ltr, [[2, 7], [0, 2]], 1)
+    cp(Ltree, ltr, "v")
+    lin(k8, v("r32", 0, 8), 64 / SLOPE, 0.0)
     lin(nb, bit, -1.0, 1.0)
     lin(y224, s8, float(C), -1.0)
     call({"s": (190, lambda: S.activation(ap(v("ta")), ap(ident), Act.Relu, bias=ap(nk32)))}, [ident, nk32], [v("ta")])
-    lin(v("tp"), v("ta"), -1.0, 100.0)
+    ts(v("cg", 40, 41), k_, 4.0, Op.is_lt)
+    ts(v("cg", 41, 42), k_, 4.0, Op.is_ge)
+    lin(v("cg", 42, 44), v("cg", 40, 42), -1.0, 0.0)
+    lin(v("cg", 44, 46), v("cg", 40, 42), 100.0, 0.0)
+    lin(later, v("cg", 40, 41), 4 * HUGE, -3 * HUGE)
+    for h, (a, z) in enumerate(HALVES):
+        lin(v("tp", a, z), v("ta", a, z), v("cg", 42 + h, 43 + h), v("cg", 44 + h, 45 + h))
+    for t in range(R + 1):
+        fill(v("xy%d" % t, 896, 1024), 0.0)
     lin(v("idb"), ident, nb, y224)
     fill(v("cs1"), 0.0)
     ts(v("cs1", 0, C, 32), v("r32", 0, 7), k_, Op.is_equal, -3 * HUGE, Op.mult)
     ts(v("cs1", 31, C, 32), v("r32", 0, 7), k_, Op.is_equal, HUGE, Op.mult)
     fill(v("rr", 0, 8), 0.0)
-    fill(v("ab"), 0.0)
-    fill(v("ee"), 0.0)
-    fill(v("sr"), 0.0)
+    fill(v("sr", 8, 16), 0.0)
     iota(v("ul_i"), [[1, 3], [16, 8]], 0)
     cp(v("ul"), v("ul_i"), "v")
-    iota(i48a, [[16, 6], [0, 8]], 0)
-    iota(i48b, [[0, 6], [-64, 8]], 448)
-    lin(n48, i48a, 1.0, q_)
-    lin(nt, n48, -SLOPE, 0.0)
-    lin(i48a, i48b, 1.0, HALF)
-    tt(nv, i48a, nt, Op.subtract)
+    iota(n48, [[16, 6], [0, 8]], 0)
+    lin(n48, n48, 1.0, q_)
     lin(nm, n48, -1.0, -1.0)
-    lin(v("k48", 240, 288, 8), v("k48", 192, 240, 8), 1.0, float(A))
-    lin(la, s8, -2.0, 14.0)
+    lin(v("k48", 48, 96, 8), v("k48", 0, 48, 8), 1.0, float(A))
     lin(lk, s8, -1.0, 7.0)
-    ts(LA, v("r32", 0, 3), 0.0, Op.mult, la, Op.add)
-    ts(LB, LA, -1.0, Op.add)
     ts(LK, v("r32", 0, 3), 0.0, Op.mult, lk, Op.add)
     iota(nv0, [[32, 6], [2, 8]], -14)
     iota(nt0, [[-32, 6], [-66, 8]], 462)
@@ -265,7 +293,7 @@ def rank_program(g, core, T, topo):
     ts(nt0, nt0, q2, Op.subtract)
     lin(lc, lk, 32.0, 15.0)
     ts(LC, v("r32", 0, 3), 0.0, Op.mult, lc, Op.add)
-    lin(v("gu", 0, 8), v("r32", 0, 8), 33.0, 0.0)
+    lin(k33, v("r32", 0, 8), 33.0, 0.0)
     fill(v("cum", 0, 16), 0.0)
     iota(lrf, [[64, 7], [-32, 2]], 62)
     iota(k64, [[64, 7], [0, 2]], 0)
@@ -274,7 +302,7 @@ def rank_program(g, core, T, topo):
     fill(v("rs0", 448), C + 1.0)
     fill(v("rs1", 448), C + 1.0)
     iota(v("fr", A), [[2, A]], C + 2)
-    iota(v("slot"), [[1, A]], C + 1)
+    iota(v("slot"), [[1, A]], 257)
     fill(v("dx", 896), 0.0)
     fill(v("pt", 384), 0.0)
     fill(v("ht", 384), 0.0)
@@ -289,7 +317,6 @@ def rank_program(g, core, T, topo):
     gather(tbl(1), ident, 0, SPLIT)
     gather(tbl(2), tbl(1), 0, SPLIT)
     wrap16(wl(1), v("sc"), tbl(2), -1.0, Op.add)
-    ts(e2, v("sc", 15, C, 16), m16, Op.mult, -1.0, Op.add)
     gather(tbl(4), tbl(2), 1, SPLIT)
     wrap16(wl(2), v("sc"), tbl(4), -1.0, Op.add)
     gather(v("p8"), tbl(4), 2, SPLIT)
@@ -299,34 +326,25 @@ def rank_program(g, core, T, topo):
     gather(tbl(6), tbl(4), 1)
     gather(tbl(7), tbl(3), 2)
     lin(v("t4b"), tbl(4), bit, 0.0)
-    level(v("aw", 0, C), v("t4b"), 2, v("idb"))
+    for a, z in ((0, 8), (8, 14)):
+        tt(v("aw", 16 * a, 16 * z), by(v("t4b"), wl(2, a, z)), v("idb", 16 * a, 16 * z), Op.add)
     gather(v("awm"), v("aw", 0, C), 3, SPLIT)
-    gather(v("aw", C), v("awm"), 3, SPLIT)
+    gather(v("aw", C, 2 * C), v("awm"), 3, SPLIT)
     gather(v("p16"), v("p8"), 3)
     wrap16(wl(4), v("sc"), v("p16"), -1.0, Op.add)
     tt(v("un"), tbl(1), ident, Op.not_equal)
+    lin(v("ff", 0, C), v("un"), 65.0, 0.0)
     fill(v("un", 0, C, 32), 0.0)
     lin(v("ca"), ident, -1.0, 256.0)
     scan(v("cb"), v("un"), v("ca"), 0.0, Op.mult, Op.max)
     iota(lend, [[32, 7], [0, 2]], 31)
     cp(v("ml", 0, 14), lend, "v")
     lin(v("top"), by(v("cb"), v("ml", 0, 14)), -1.0, 256.0)
-    d1, d2, d4, d8, d16, d24, d32, d2x = [piece("dd", i, C) for i in range(8)]
-    ts(idw, v("r32", 0, 14), 16.0, Op.mult, q_, Op.add)
-    tt(e1, v("par_i"), idw, Op.not_equal)
-    tt(e2, e2, v("par_i"), Op.not_equal)
-    tt(e2, e1, e2, Op.add)
-    cp(v("ml", 14, 28), e2, "v")
-    o = BASE if "s" in DEPTH else 0.0
-    lin(d2, by(ident, v("ml", 14, 28)), 1.0, o - 1, "s")
-    o4 = level(d4, d2, 1, None, DEPTH[0], o, o)
-    o8 = level(d8, d4, 2, None, DEPTH[1], o4, o4)
-    o16 = level(d16, d8, 3, None, DEPTH[2], o8, o8)
-    o32 = level(d32, d16, 4, None, DEPTH[3], o16, o16)
-    lin(d2x, d32, 2.0, 2.0 - 2 * o32)
-    lin(v("nd"), d32, -1.0, A + o32)
-    wrap16(dw, v("sc2"), d2x, -1.0, Op.mult)
-    tt(cw3, dw, k64, Op.add)
+    lin(q225, q_, 1.0, C + 1.0)
+    lin(spare, v("r32", 0, 14), 16.0, q225)
+    fill(v("t64"), 64.0)
+    fill(v("ee"), 0.0)
+    lin(v("r2"), v("r1"), -BIG, FAR - 936 * BIG)
 
     quant(v("uq"), v("us"), v("ut"))
     for t in range(R):
@@ -337,55 +355,53 @@ def rank_program(g, core, T, topo):
 
     for t in range(R):
         n = str(t)
-        xy, xq, xsc, rs, uw = "xy" + n, v("xq" + n), v("xsc" + n), "rs" + str(t % 2), t and v("uw" + n)
-        pq, psc, hq, hsc = "pq" + n, "psc" + n, "hq" + n, "hsc" + n
+        xy, xq, xsc, rs, uw = "xy" + n, "xq" + n, "xsc" + n, "rs" + str(t % 2), t and v("uw" + n)
+        hq, hsc = "hq" + n, "hsc" + n
         fo, fi = piece("fout", t, 24), piece("fin", t, 24)
-        quant(xq, xsc, v(xy, 0, 896))
-        mm(7, piece("upq", t), piece("ups", t), xq, xsc)
-        if not HOME[t]:
-            send(t, "ax" + n, [(v("aq" + n), xq), (v("asc" + n), xsc)])
-            xq, xsc = v("aq" + n), v("asc" + n)
-        for b in range(4):
-            mm(b, piece("eq", b), piece("es", b), xq, xsc)
-            cp(v("dx", b, 896, 4), bank(b, 0, C))
-        scan(v("rr", 8), v("cs1"), bank(7, 0, C), -3 * HUGE, Op.add, Op.max)
-        tt(v("nn"), bank(7, 0, C), v("rr", 7, 7 + C), Op.is_le)
-        scan(v("sel"), v("nn"), v("tp"), 0.0, Op.mult, Op.max)
-        ts(v("l1", 0, 1), v("sel", C - 1), -1.0, Op.mult, c1, Op.add)
-        cp(v("l2"), by(v("aw"), v("l1", 0, 1)), "v")
-        cp(v(rs, 0, 448, 2), by(v("tb"), v("l2", 0, 14)), "s")
+        aq, asc = "aq" + n, "asc" + n
+        for h, (a, z) in enumerate(HALVES):
+            quant(piece(xq, h), piece(xsc, h), piece(xy, h, 512))
+            mm(6 + h, piece("upq", t), piece("ups", t), piece(xq, h), piece(xsc, h))
+            scan(v("rr", 8 + a, 8 + z), v("cs1", a, z), bank(6 + h, 0, z - a), later if h else -3 * HUGE, Op.add, Op.max)
+            tt(v("nn", a, z), bank(6 + h, 0, z - a), v("rr", 7 + a, 7 + z), Op.is_le)
+            scan(v("sel", a, z), v("nn", a, z), v("tp", a, z), 0.0, Op.mult, Op.max)
+        ts(v("l1", 0, 6), c6, v("sel", 127, 128), Op.subtract, v("sel", C - 1), Op.subtract)
+        send(t, "ax" + n, [(v(aq, 0, 128), v(xq, 0, 128)), (v(asc), v(xsc, 0, C))])
+        send(t, "ay" + n, [(v(aq, 128), v(xq, 128, C))])
+        cp(v("l2", 1, 17), by(v("aw"), v("l1", 0, 1)), "v")
+        cp(v(rs, 0, 448, 2), by(v("tb"), v("l2", 2, 16)), "s")
         if t:
-            cp(v("gu"), by(uw, v("l1", 0, 1)), "v")
-            scan(v("ab", 1, 15), v("gu", 0, 14), v("ee", 0, 14), 0.0, Op.add, Op.add)
-            tt(v("vv"), by(v("ab"), LA), nv, Op.add)
-            tt(v("fa"), by(v("ab"), LB), nt, Op.is_ge)
-            ts(v("sr", 16, 24), v("ab", 0, 16, 2), -1 / SLOPE, Op.mult, WHOLE, Op.add)
-            ts(v("sr", 0, 8), v("sr", 16, 24), WHOLE, Op.subtract)
+            cp(v("gu"), by(uw, v("l1", 0, 6)), "v")
+            scan(v("ab"), v("gu"), v("mz"), 0.0, Op.add, Op.mult)
+            scan(v("cs"), v("ab", 0, A, 2), v("ab", 1, A, 2), BIG, Op.min, Op.max)
+            ts(v("cw", 5, -1, -1), v("cs", 7, 48, 8), WHOLE, Op.add, WHOLE, Op.subtract)
+            ts(v("sr", 16, 24), v("ab", 0, 16, 2), nq, Op.subtract, -1 / SLOPE, Op.mult)
+            tt(v("sr", 16, 24), v("sr", 16, 24), k8, Op.add)
+            ts(v("sr", 0, 8), v("sr", 16, 24), WHOLE, Op.add, WHOLE, Op.subtract)
         else:
-            tt(v("nn"), by(v("tb"), v("l2", 0, 14)), v("top"), Op.is_equal)
+            tt(v("nn"), by(v("tb"), v("l2", 2, 16)), v("top"), Op.is_equal)
             scan(v("cum", 16), v("nn"), v("nn"), 0.0, Op.add, Op.add)
             tt(v("vv"), by(v("cum"), LC), nv0, Op.add)
             tt(v("fa"), by(v("cum"), LC), nt0, Op.is_ge)
+            scan(v("cs"), v("vv"), v("fa"), 0.0, Op.max, Op.mult)
+            cp(v("cw"), v("cs", 7, 48, 8), "v")
             lin(v("sr", 16, 24), v("cum", 15, 240, 32), -0.5, 0.0)
-            tt(v("sr", 0, 8), v("sr", 16, 24), v("gu", 0, 8), Op.add)
-        scan(v("cs"), v("vv"), v("fa"), 0.0, Op.max, Op.mult)
-        ts(v("cw"), v("cs", 7, 48, 8), WHOLE, Op.add, WHOLE, Op.subtract)
+            tt(v("sr", 0, 8), v("sr", 16, 24), k33, Op.add)
         cp(v("fr", 0, A), by(v(rs), v("cw")), "v")
         wrap4(fo, v("f4"), v("fr", 0, A))
-        if HOME[t]:
-            fi = fo
-        else:
-            send(t, "al" + n, [(fi, fo)])
+        listed = len(calls) - 1
+        send(t, "al" + n, [(fi, fo)])
+        for h, (a, z) in enumerate(HALVES):
+            for b in range(4):
+                mm(4 * h + b, piece("eq", b), piece("es", b), v(aq, z - 128, z), v(asc, z - 128, z))
+                cp(v("dx", 4 * a + b, 4 * z, 4), bank(4 * h + b, 128 + a - z, 128), DXQ)
+                calls[-1]["soft"] = listed
         cp(v("pt", 0, 192), by(v("dx"), part(fi, 0, 12)), "v")
         cp(v("pt", 192, 384), by(v("dx"), part(fi, 12, 24)), "s")
-        quant(v(pq, 0, 128), v(psc, 0, 128), v("pt"))
-        o = 0
-        if HOME[t]:
-            send(t, "al" + n, [(v(pq, 128), v(pq, 0, A)), (v(psc, 128), v(psc, 0, A))])
-            o = 128 - A
+        quant(v("pq"), v("psc"), v("pt"))
         for b in range(4):
-            mm(4 + b, piece("wq", b), piece("wsc", b), v(pq, 3 * o, 3 * o + 128), v(psc, 3 * o, 3 * o + 128))
-            relu(v("ht", b, 384, 4), bank(4 + b, o, o + A), 0.03125, "vs"[b % 2])
+            mm(4 + b, piece("wq", b), piece("wsc", b), v("pq"), v("psc"))
+            relu(v("ht", b, 384, 4), bank(4 + b, 0, A), 0.03125, "vs"[b % 2])
         quant(v(hq, 0, 128), v(hsc, 0, 128), v("ht"))
         send(t, "ah" + n, [(v(hq, 128), v(hq, 0, A)), (v(hsc, 128), v(hsc, 0, A))])
         ts(v("sr", 24, 31), v("sr", 1, 8), float(A), Op.min)
@@ -402,23 +418,46 @@ def rank_program(g, core, T, topo):
         cp(v("hr", 0, C), ident)
         cp(by(v("hr"), v("m16")), v("slot"), "v")
         wrap4(v("hw"), v("sch"), v("hr", 0, C))
-        ts(v("l1", 2, 3), v("sel", C - 1), -1.0, Op.mult, c1b, Op.add)
-        cp(v("gd"), by(d2x, v("l1", 2, 3)))
-        tt(v("mlf", 0, 14), v("gd", 0, 14), cw3, Op.add)
-        cp(v("ml", 0, 14), v("mlf", 0, 14), "v")
+        if t:
+            ts(v("l1", 6, 7), c1b, v("sel", 127, 128), Op.subtract, v("sel", C - 1), Op.subtract)
+            lin(v("gd"), by(v("dd"), v("l1", 6, 7)), 2.0, 0.0)
+            tt(cw3, v("gd", 1, 15), k64, Op.add)
+            tt(v("mlf", 0, 14), cw3, dw, Op.add)
+            cp(v("ml", 0, 14), v("mlf", 0, 14), "v")
+        if t == 0:
+            wrap16(e1, v("sc2"), v(rs, 0, 448, 2), 0.0, Op.add)
+            tt(e2, e1, v("top", 0, C, 16), Op.is_equal)
+            tt(e2, e2, spare, Op.mult)
+            tt(e1, e1, e2, Op.max)
+            ts(v("ml", 0, 14), e1, -1.0, Op.add)
+            cp(by(v("ff", 0, 2 * C), v("ml", 0, 14)), v("t64"), "v")
+            fa, fb, fc, fd = [piece("ff", i, C) for i in (2, 3, 4, 5)]
+            lin(fb, v("ff", 0, C), 1.0, DEEP)
+            o = doubled([fa, fb, fa, fb, fa], fc, fd, v("ff", 0, C), fb, DEEP)
+            ts(fb, fa, 64 * WHOLE, Op.add, 64 * WHOLE, Op.subtract)
+            scan(v("ca"), fa, fb, 0.0, Op.max, Op.subtract)
+            lin(v("dd", 0, C), fb, 1 / 64, 1 - (o + 16) / 64)
+            wrap16(dw, v("sc2"), v("dd", 0, C), -2.0, Op.mult)
+            tt(v("gd", 0, 7), v("sr", 1, 8), v("sr", 0, 7), Op.subtract)
+            lin(v("ee", 1, 15, 2), v("gd", 0, 7), -SLOPE * BIG, 0.0)
+            tt(v("yo"), by(v("ee"), Ltree), v("r2"), Op.add)
+            lin(fc, fb, SLOPE * BIG / 64, -FAR - SLOPE * BIG * (o + 16) / 64)
+            scan(v("oa"), fc, v("yo"), 0.0, Op.min, Op.add)
+            scan(v("nd"), fc, v("r2"), 0.0, Op.min, Op.add)
+            o = -16.0
+        if t == 1:
+            for a, z in PARTS:
+                tt(v("un", 16 * a, 16 * z), by(v(rs), v("ml", a, z)), part(ident, 16 * a, 16 * z), Op.not_equal)
+            lin(v("cb"), v("un"), 1.0, BASE)
+            o = doubled([v(x) for x in ("ca", "cb", "ca", "cb", "ca")], v("cc"), v("dg"), v("un"), v("cb"), BASE)
+            lin(v("ee"), v("gd"), -SLOPE * BIG / 2, 0.0)
+            tt(v("oa"), by(v("ee"), Ltree), v("nd"), Op.add)
         if t < R - 1:
             nxt = "uw" + str(t + 1)
-            tt(v("un"), by(v(rs), v("ml", 0, 14)), ident, Op.not_equal)
-            o = BASE if "s" in LEVEL else 0.0
-            if o:
-                lin(v("cc"), v("un"), 1.0, o)
-            o = level(v("ca"), v("un"), 0, v("cc" if o else "un"), LEVEL[0], 0.0, o)
-            for i in range(1, 5):
-                o = level(v(("ca", "cb")[i % 2]), v(("cb", "ca")[i % 2]), i, None, LEVEL[i], o, o)
-            lin(v(nxt, 0, C), v("ca"), -SLOPE, o * SLOPE)
-            scan(v("cb"), v("ca"), v("nd"), 1000.0, Op.min, Op.add)
-            lin(v(nxt, C), v("cb"), -SLOPE, (o + A) * SLOPE)
-            lin(v("ee", 1, 14, 2), v("gd", 0, 14, 2), -SLOPE / 2, 0.0)
+            lin(v("idb"), v("ca"), -SLOPE, o * SLOPE + 1000)
+            scan(v(nxt, 0, C), v("idb"), v("r1"), 0.0, Op.max, Op.add)
+            lin(v("awm"), v("ca"), -SLOPE * BIG, o * SLOPE * BIG)
+            scan(v(nxt, C, 2 * C), v("awm"), v("oa"), 0.0, Op.min, Op.add)
             cp(v("rs" + str(1 - t % 2), 1, 448, 2), by(v(rs), Lrev))
         else:
             ts(v("mlf", 14, 28), v("mlf", 0, 14), -2.0, Op.add)
@@ -432,16 +471,17 @@ def rank_program(g, core, T, topo):
             store("y", T.op[:], T.oa[0:128:16, :], v("oa"))
         for b in range(4):
             mm(b, piece("eq", b), piece("es", b), v(hq, A), v(hsc, A))
-            tt(v(xy, 896 + b, 1280, 4), bank(b, 128 - A, 128), v("xs", b, 384, 4), Op.add)
-        cp(v("xy" + str(t + 1), 0, 448), by(v(xy), v("hw", 0, 28)), "v")
-        cp(v("xy" + str(t + 1), 448, 896), by(v(xy), v("hw", 28, 56)), "s")
+            tt(v(xy, 1024 + b, 1408, 4), bank(b, 128 - A, 128), v("xs", b, 384, 4), Op.add)
+        for (a, z), q in zip(CUTS, "vsvs"):
+            cp(v("xy" + str(t + 1), 16 * a, 16 * z), by(v(xy), v("hw", a, z)), q)
 
-    quant(v("xq3"), v("xsc3"), v("xy3"))
-    mm(7, v("vq"), v("vs"), v("xq3"), v("xsc3"))
-    store("s", T.oc[:], ap(v("xq3"), dt.uint8), v("xq3"))
+    for h, (a, z) in enumerate(HALVES):
+        quant(piece("xq3", h), piece("xsc3", h), piece("xy3", h, 512))
+        mm(6 + h, v("vq"), v("vs"), piece("xq3", h), piece("xsc3", h))
+        cp(v("yo", a, z), bank(6 + h, 0, z - a), "sv"[h])
+    store("s", T.oc[:], ap(v("xq3", 0, C), dt.uint8), v("xq3"))
     for k in range(4):
-        store("ys"[k % 2], T.osc[4 * k:4 * k + 4, :], T.xsc3[32 * k:32 * k + 4, :], v("xsc3"))
-    cp(v("yo"), bank(7, 0, C), "v")
+        store("ys"[k % 2], T.osc[4 * k:4 * k + 4, :], T.xsc3[32 * k:32 * k + 4, 0:C], v("xsc3"))
     store("y", T.y[:], T.yo[:], v("yo"))
 
     def place(rank_of, before):
@@ -462,7 +502,7 @@ def rank_program(g, core, T, topo):
             busy[best[3]] = sorted(busy[best[3]] + [best[1:3]])
         return plan
 
-    ahead = [[(d, calls[d]["lag"]) for d in c["deps"]] for c in calls]
+    ahead = [[(d, calls[d]["lag"]) for d in c["deps"]] + ([(c["soft"], SOFT)] if "soft" in c else []) for c in calls]
     behind = [[] for c in calls]
     tail = [0.0] * len(calls)
     for i in reversed(range(len(calls))):
@@ -470,10 +510,17 @@ def rank_program(g, core, T, topo):
         for d, lag in ahead[i]:
             tail[d] = max(tail[d], tail[i])
             behind[d].append((i, lag))
-    plans = [place(tail, ahead)]
+    def early(rank):
+        rank = [r + SOON * ("g" in c["ways"] and c["sem"] is not None) for r, c in zip(rank, calls)]
+        for i in reversed(range(len(calls))):
+            for d, lag in ahead[i]:
+                rank[d] = max(rank[d], rank[i] + 1)
+        return rank
+
+    plans = [place(early(tail), ahead)]
     for turn in range(TURNS):
         back = place([plans[-1][i][1] for i in range(len(calls))], behind)
-        plans.append(place([back[i][1] for i in range(len(calls))], ahead))
+        plans.append(place(early([back[i][1] for i in range(len(calls))]), ahead))
     plan = min(plans, key=lambda p: max(e[1] for e in p.values()))
 
     count = {q: 0 for q in "vspg"}

@@ -1,40 +1,54 @@
+from concourse.bass import DstId, RemoteDMATransfer
 from concourse.mybir import dt, AluOpType as Op, ActivationFunctionType as Act
 
 C, A, R = 224, 96, 3
 STEP = [1, 2, 4]
 SOFT = 0
-LAZY = 1.0
-SPLIT = True
-TURNS = 3
+LAZY = (0.25, 0.5, 1.0, 2.0)
+OVER = 700
+SIDE = "www"
+SHARE = "vs"
+SLOW = 1.0
+LATE, RSH, XSH, YQ = False, False, False, "vv"
+URGE = 0
+AHEAD = 2
+CLEAR = (0,)
+HRG = False
+LATER = 0
+SPEEDS = ((1.0, 1.0, 1.0, 0), (1.25, 1.1, 2.0, 20), (1.25, 1.5, 1.5, 0), (1.4, 1.4, 2.0, 40), (1.1, 1.3, 3.0, 0))
+TURNS = 2
 DXQ = "s"
 GFILL = True
-SOON = 0
-PARTS = ((0, 14),)
-PARTS2 = ((0, 14),)
+FUSE = False
 HALVES = ((0, 128), (128, C))
-CUTS = ((0, 16), (16, 32), (32, 42), (42, 56))
+RELU = ("vsvs", "vsvs", "vsvs")
+M = 128
+Y = M + 128
+PARTS = ((0, M, M), (M, C, Y))
+CUTS = ((0, 16), (16, 32), (32, 44), (44, 56))
 F32, BF, I32, U16, MX, U8 = "float32", "bfloat16", "int32", "uint16", "float8_e4m3fn_x4", "uint8"
 HUGE = 1.0e29
 HOLD = 512.0
 SLOPE, HALF = 127.0 / 64, 63.0 / 128
 WHOLE = 12582912.0
 BIG = 2048.0
-BASE, DEEP, FAR = 16.0, 1052.0, 262144.0
-WAIT, ISSUE, START, WAKE, ROWNS, BYTENS, LOAD = 220, 700, 200, 300, 5, 0.04, 2100
+BASE, DEEP, NEAR, FAR = 16.0, 4208.0, 16384.0, 33554432.0
+LEVELS = ("sssss", "sssss", "sssss")
+WAIT, ISSUE, START, WAKE, ROWNS, BYTENS, LOAD = 220, 700, 200, 300, 5, 0.04, 1350
 
 SCRATCH = {"ps": ("psum", [128, 4096], F32)}
 for _d, _l in (
-        (I32, "par_i 14 ci 10 pc 6 ul_i 24"),
-        (BF, "ut 512 vt 512 ez 520 eone 128 xy0 1408 xy1 1408 xy2 1408 xy3 1024 dx 912 pt 512 ht 512 xs 384 tp 224 nn 224 sel 224 "
-             "tb 1792 p8 224 p16 224 t4b 224 pat 96 c16 224 c4 224 sc 224 sc2 224 ta 224 rs0 640 rs1 640 fr 192 f4 96 "
-             "mr 96 mr4 96 scm 96 scn 96 dd 240 t64 224 un 224 ca 224 cb 224 cc 224 dg 224 top 224 cum 240"),
-        (MX, "wq 512 uq 128 upq 384 vq 128 eq 512 pq 128 xq0 256 xq1 256 xq2 256 xq3 256 aq0 224 aq1 224 aq2 224 "
+        (I32, "par_i 14 ci 10 pc 9 ul_i 24"),
+        (BF, "ut 512 vt 512 ez 520 eone 128 xy0 1536 xy1 1536 xy2 1536 xy3 1152 dx 912 pt 512 ht 512 xs 384 tp 224 nn 224 sel 224 "
+             "tb 1792 p8 224 p16 224 t4b 224 pat 96 c16 224 c4 224 sc 224 sc2 224 cs1 224 rs0 640 rs1 640 fr 192 f4 96 "
+             "mr 96 mr4 96 scm 96 scn 96 dd 240 de 896 mk 448 t64 224 un 224 ca 224 cb 224 cc 224 dg 224 top 224 cum 128"),
+        (MX, "wq 512 uq 128 upq 384 vq 128 eq 512 pq 128 xq0 288 xq1 288 xq2 288 xq3 288 aq0 224 aq1 224 aq2 224 "
              "hq0 224 hq1 224 hq2 224"),
-        (U8, "wsc 512 us 128 ups 384 vs 128 es 512 psc 128 xsc0 256 xsc1 256 xsc2 256 xsc3 256 "
-             "asc0 224 asc1 224 asc2 224 hsc0 224 hsc1 224 hsc2 224"),
-        (U16, "fout 72 fin 72 wl 80 cl 64 ul 24 l1 8 l2 18 cw 6 mw 6 m16 6 m4 24 hw 56 ml 28"),
-        (F32, "cf 10 cg 48 r32 32 idb 224 aw 456 awm 224 uw1 456 uw2 456 cs1 224 rr 232 gu 96 mz 96 ab 96 ee 16 gd 16 "
-              "nd 224 r1 224 r2 224 ff 1344 k48 192 vv 48 fa 48 cs 48 vm 48 fl 48 cm 48 sr 32 hr 424 slot 96 sch 224 k14 126 mlf 28 oa 224 yo 224")):
+        (U8, "wsc 512 us 128 ups 384 vs 128 es 512 psc 128 xsc0 288 xsc1 288 xsc2 288 xsc3 288 "
+             "asc0 224 asc1 224 asc2 224 hsc0 256 hsc1 256 hsc2 256"),
+        (U16, "fout 72 fin 72 wl 80 cl 64 ul 24 l1 8 l2 68 cw 6 mw 6 m16 6 m4 24 hw 56 ml 28"),
+        (F32, "cf 10 cg 64 r32 32 aw 464 awm 224 uw1 464 uw2 464 rr 232 gu 96 mz 96 ab 96 ee 16 gd 16 "
+              "nd 224 gs 96 gt 96 k48 192 vv 48 fa 48 cs 48 vm 48 fl 48 cm 48 sr 32 hr 424 slot 96 sch 224 k14 126 mlf 28 oa 224 yo 224")):
     _w = _l.split()
     for _i in range(0, len(_w), 2):
         SCRATCH[_w[_i]] = ("sbuf", [128, int(_w[_i + 1])], _d)
@@ -84,7 +98,7 @@ def rank_program(g, core, T, topo):
                 cols, w = {x[1] // 512}, True
             deps |= {o for c, ow, o in seen.setdefault(x[0], []) if (w or ow) and o != me and c & cols}
             seen[x[0]].append((cols, w, me))
-        calls.append({"ways": ways, "deps": deps, "lag": lag, "sem": sem})
+        calls.append({"ways": ways, "deps": deps, "lag": lag, "sem": sem, "list": any(len(x) > 4 for x in rd + wr)})
         return me
 
     def ns(out, ins, q="v", both=False):
@@ -158,8 +172,23 @@ def rank_program(g, core, T, topo):
             ids.append(call({"g": (ISSUE, lambda out=out, a=a, cast=cast: g.remote_dma(
                 ap(out, cast), ap(a, cast), T.sem[sem], T.sem.sent, pid, rid, topo.mask(core, peer)))}, [a], [], START, sem=("sent", 0)))
             nsent[0] += len(topo.engines(core, peer))
-            time += 16 * (ROWNS + BYTENS * width(a) * {MX: 4, U8: 1, U16: 2}[SCRATCH[a[0]][2]])
+            time = max(0, time - OVER * (sem[1] == "h")) + 16 * (ROWNS + BYTENS * width(a) * {MX: 4, U8: 1, U16: 2}[SCRATCH[a[0]][2]])
         call({"link": (time, None)}, [], [o for o, a in pairs], WAKE, ids, (sem, len(pairs) * len(topo.engines(peer, core))))
+
+    def send_one(t, sem, pairs):
+        peer = T.cores[rank ^ STEP[t]]
+        rid, pid, se = topo.addr(peer)
+        eng = topo.engines(core, peer)
+        k = len(eng) // len(pairs)
+
+        def go():
+            return g.remote_dma_fused([RemoteDMATransfer(
+                dst_ids=[DstId(rid=rid, pnc=pid)], dma_engine_mask=sum(1 << e for e in eng[k * i:k * i + k]), remote_sem=T.sem[sem],
+                src=ap(a, dt.uint8 if SCRATCH[a[0]][2] == MX else None), dst=ap(out, dt.uint8 if SCRATCH[a[0]][2] == MX else None))
+                for i, (out, a) in enumerate(pairs)], local_sem=T.sem.sent)
+        me = call({"g": (ISSUE, go)}, [a for o, a in pairs], [], START, sem=("sent", 0))
+        nsent[0] += k * len(pairs)
+        call({"link": (128 // k * (ROWNS + BYTENS * 128), None)}, [], [o for o, a in pairs], WAKE, [me], (sem, k * len(pairs)))
 
     Q = {"v": V, "s": S, "p": P, "g": g, "y": g.sync}
 
@@ -172,137 +201,130 @@ def rank_program(g, core, T, topo):
     def part(x, a, z):
         return (x[0], x[1] + a * x[3], x[1] + z * x[3], x[3])
 
-    def gather(out, win, i, split=False):
-        if split:
-            cp(part(out, 0, 128), by(win, wl(i, 0, 8)), "v")
-            cp(part(out, 128, C), by(win, wl(i, 8, 14)), "s")
-        else:
-            cp(out, by(win, wl(i)))
+    def shared(out, win, i):
+        for (a, z), q in zip(HALVES, SHARE):
+            cp(part(out, a, z), by(win, wl(i, a // 16, z // 16)), q)
 
     ident = tbl(0)
-    q_, q1, k_, h_, s8, bit, kq, kq1, hh = [v("cf", i, i + 1) for i in range(9)]
-    m16, m4, off4, z0, nk32, c1, c1b, nb, y224, q2, nq, lk, lc, q225, later = [v("cg", i, i + 1) for i in range(15)]
-    c6, k8, k33 = v("cg", 16, 22), v("cg", 24, 32), v("cg", 32, 40)
+    q_, q1, bit, nb, s8, k_, h_, kq, kq1, hh = [v("cf", i, i + 1) for i in range(10)]
+    m16, m4, off4, z0, nk32, c1, c1b, y224, nq, lk, lc, q225, later = [v("cg", i, i + 1) for i in range(13)]
+    c6, k8, k33, ktree = v("cg", 16, 22), v("cg", 24, 32), v("cg", 32, 40), v("cg", 48, 64)
     Lq, Lh, Lrev, Ltree = [v("cl", 14 * i, 14 * i + 14) for i in range(4)]
     LC, LK = v("cl", 56, 59), v("cl", 60, 63)
-    n48, nm, nv0, nt0 = [v("k48", 48 * i, 48 * i + 48) for i in range(4)]
+    n48, nv0, nt0, nm = [v("k48", 48 * i, 48 * i + 48) for i in range(4)]
     lrf, k64, dw, cw3, spare, e1, e2, lend, ltr = [v("k14", 14 * i, 14 * i + 14) for i in range(9)]
 
     def wrap16(out, buf, src, s2, o1):
         n = width(src)
         scan(part(buf, 0, n), v("c16", 0, n), src, 0.0, Op.mult, Op.max)
-        ts(out, (buf[0], 15, n, 16), m16, Op.mult, s2, o1)
+        ts(out, (buf[0], buf[1] + 15, buf[1] + n, 16), m16, Op.mult, s2, o1)
 
     def wrap4(out, buf, src):
         n = width(src)
         scan(part(buf, 0, n), v("c4", 0, n), src, 0.0, Op.mult, Op.max)
         ts(out, (buf[0], 3, n, 4), m4, Op.mult, off4, Op.add)
 
-    def doubled(outs, twin, far, src, own, base):
-        lift = 0.0
+    def plus(out, a, b):
+        scan(out, a, b, FAR, Op.min, Op.add)
+
+    def doubled(outs, far, src, own=None):
         for i, out in enumerate(outs):
-            if i % 2:
-                for a, z in PARTS:
-                    tt(part(out, 16 * a, 16 * z), by(src, wl(i, a, z)), part(twin, 16 * a, 16 * z), Op.add)
-                lift *= 2
-            else:
-                for a, z in PARTS2:
-                    lin(part(far, 16 * a, 16 * z), by(src, wl(i, a, z)), 1.0, -lift, "s")
-                for o in [out, twin][:len(outs) - i]:
-                    scan(o, far, own, FAR, Op.min, Op.add)
-                lift = max(lift, base)
-            src = own = out
-        return lift
+            lin(far, by(src, wl(i)), 1.0, 0.0 if own else -BASE, "s")
+            plus(out, far, own or src)
+            src, own = out, None
 
     def piece(name, b, n=128):
         return v(name, n * b, n * b + n)
 
     load("y", v("par_i"), T.par[:], "ld_par", LOAD)
-    load("s", v("xy0", 0, 896), T.x[:], "ld_x", LOAD)
-    load("y", v("ut"), T.u[:], "ld_u", LOAD + 500)
+    load("y", v("ut"), T.u[:], "ld_u", LOAD + 450)
+    load("y", v("xy0", 0, 896), T.x[:], "ld_x", LOAD + 1200)
     load("y", v("wq"), T.wc[:], "ld_w", LOAD + 2000, dt.uint8)
     load("y", v("wsc"), T.ws[:], "ld_s", LOAD + 2000)
     load("y", v("vt"), T.v[:], "ld_v", LOAD + 2000)
+    for i in range(1, 6):
+        calls[i]["soft"] = i - 1
 
-    iota(v("pc"), [[5, 2], [1, 3]], 15, 1)
+    iota(v("pc"), [[4, 3], [1, 3]], 15, 1)
     iota(v("r32"), [[1, 32]], 0)
     iota(ident, [[1, C]], 1)
+    calls[-1]["soft"] = len(calls) - 2
+    calls[-2]["soft"] = len(calls) - 3
     ts(v("ci", 0, 2), v("pc", 1, 3), 15, Op.bitwise_and)
     cp(v("cf", 0, 2), v("ci", 0, 2), "v")
-    for i, (c, sh, m) in enumerate([(0, 1, 7), (0, 0, 1), (1, 0, 7), (1, 3, 1), (1, 2, 3), (3, 2, 3), (1, 0, 3)]):
-        ts(v("ci", i + 2, i + 3), v("pc", c, c + 1), sh, Op.logical_shift_right, m, Op.bitwise_and)
-    cp(v("cf", 2, 9), v("ci", 2, 9), "v")
+    for a, z, src, sh, m in [(2, 4, (1, 8, 6), 3, 1), (4, 5, (1, 2), 0, 7), (5, 6, (0, 1), 1, 7), (6, 7, (0, 1), 0, 1),
+                             (7, 9, (1, 5, 3), 2, 3), (9, 10, (1, 2), 0, 3)]:
+        ts(v("ci", a, z), v("pc", *src), sh, Op.logical_shift_right, m, Op.bitwise_and)
+        if a >= 5:
+            calls[-1]["not before"] = LATER
+    cp(v("cf", 2, 5), v("ci", 2, 5), "v")
+    cp(v("cf", 5, 10), v("ci", 5, 10), "v")
     for a, at, nxt in ((0, q_, q1), (16, kq, kq1)):
         ts(v("pat", 32 + a, 48 + a), v("r32", 0, 16), at, Op.not_equal)
         ts(v("pat", 64 + a, 80 + a), v("r32", 0, 16), nxt, Op.is_equal, HOLD - 1, Op.mult)
         tt(v("pat", a, a + 16), v("pat", 32 + a, 48 + a), v("pat", 64 + a, 80 + a), Op.add)
     ts(Lq, v("r32", 0, 14), 0.0, Op.mult, q_, Op.add)
     ts(Lh, v("r32", 0, 14), 0.0, Op.mult, hh, Op.add)
-    cp(v("c16"), by(v("pat", 0, 16), Lq))
+    for a, z in HALVES:
+        cp(v("c16", a, z), by(v("pat", 0, 16), part(Lq, 0, (z - a) // 16)))
     cp(v("c4"), by(v("pat", 16, 32), Lh))
     lin(m16, v("pat", 47, 48), 1 / HOLD - 1, 1.0)
     lin(m4, v("pat", 51, 52), 4 / HOLD - 4, 4.0)
     lin(off4, hh, 1.0, -4.0)
-    lin(nk32, k_, -32.0, -1.0)
-    lin(c1b, k_, 32.0, 100.0)
-    lin(c1, h_, float(C), c1b)
-    ts(z0, q_, 0.0, Op.is_equal)
-    lin(c6, v("r32", 0, 6), z0, c1)
+    lin(c1, k_, 32.0, 100.0)
+    lin(c1, h_, C + 8.0, c1)
+    lin(c6, v("r32", 0, 6), 0.0, c1)
     lin(nq, q_, SLOPE, 80 * SLOPE + HALF)
-    for t in (1, 2):
-        fill(v("uw%d" % t, 454), 0.0)
-        lin(v("uw%d" % t, 448, 454), v("r32", 0, 6), -16 * SLOPE, nq)
-    fill(v("aw", 448), 0.0)
+    iota(v("gt"), [[0, 6], [1, 16]], 0)
+    lin(v("gs", 1, A, 2), v("gt", 1, A, 2), -32.0, 32.0)
+    lin(v("gs", 0, A, 2), v("gt", 0, A, 2), 32 * BIG, 0.0)
+    lin(v("gs", 0, A, 16), v("r32", 0, 6), -16 * SLOPE, nq)
+    for h in range(2):
+        fill(v("aw", C + 232 * h, 232 + 232 * h), 0.0)
     fill(v("dd", C), 0.0)
     for a, s, x in ((1, 2, BIG), (0, 2, 1 / BIG), (0, 16, 1.0), (15, 16, 0.0)):
         fill(v("mz", a, A, s), x)
-    iota(v("r1"), [[-64, 7], [0, 32]], -1000)
-    iota(ltr, [[2, 7], [0, 2]], 1)
-    cp(Ltree, ltr, "v")
     lin(k8, v("r32", 0, 8), 64 / SLOPE, 0.0)
-    lin(nb, bit, -1.0, 1.0)
     lin(y224, s8, float(C), -1.0)
-    call({"s": (190, lambda: S.activation(ap(v("ta")), ap(ident), Act.Relu, bias=ap(nk32)))}, [ident, nk32], [v("ta")])
-    ts(v("cg", 40, 41), k_, 4.0, Op.is_lt)
-    ts(v("cg", 41, 42), k_, 4.0, Op.is_ge)
-    lin(v("cg", 42, 44), v("cg", 40, 42), -1.0, 0.0)
-    lin(v("cg", 44, 46), v("cg", 40, 42), 100.0, 0.0)
-    lin(later, v("cg", 40, 41), 4 * HUGE, -3 * HUGE)
-    for h, (a, z) in enumerate(HALVES):
-        lin(v("tp", a, z), v("ta", a, z), v("cg", 42 + h, 43 + h), v("cg", 44 + h, 45 + h))
-    for t in range(R + 1):
-        fill(v("xy%d" % t, 896, 1024), 0.0)
-    lin(v("idb"), ident, nb, y224)
+    lin(v("cc"), ident, nb, 0.0)
     fill(v("cs1"), 0.0)
-    ts(v("cs1", 0, C, 32), v("r32", 0, 7), k_, Op.is_equal, -3 * HUGE, Op.mult)
-    ts(v("cs1", 31, C, 32), v("r32", 0, 7), k_, Op.is_equal, HUGE, Op.mult)
+
+    def own_tree(k):
+        lin(nk32, k, 32.0, 101.0)
+        lin(c1b, k, 32.0, 100.0)
+        ts(v("cg", 40, 41), k, M / 32, Op.is_lt, -100.0, Op.mult)
+        ts(v("cg", 41, 42), k, M / 32, Op.is_ge, -100.0, Op.mult)
+        lin(later, v("cg", 40, 41), -HUGE / 25, -3 * HUGE)
+        for h, (a, z, y) in enumerate(PARTS):
+            ts(v("tp", a, z), part(ident, a, z), nk32, Op.subtract, v("cg", 40 + h, 41 + h), Op.max)
+        ts(v("cs1", 0, C, 32), v("r32", 0, 7), k, Op.is_equal, -3 * HUGE, Op.mult)
+        ts(v("cs1", 31, C, 32), v("r32", 0, 7), k, Op.is_equal, HUGE, Op.mult)
+
+    own_tree(s8)
     fill(v("rr", 0, 8), 0.0)
     fill(v("sr", 8, 16), 0.0)
     iota(v("ul_i"), [[1, 3], [16, 8]], 0)
     cp(v("ul"), v("ul_i"), "v")
     iota(n48, [[16, 6], [0, 8]], 0)
-    lin(n48, n48, 1.0, q_)
-    lin(nm, n48, -1.0, -1.0)
-    lin(v("k48", 48, 96, 8), v("k48", 0, 48, 8), 1.0, float(A))
-    lin(lk, s8, -1.0, 7.0)
-    ts(LK, v("r32", 0, 3), 0.0, Op.mult, lk, Op.add)
-    iota(nv0, [[32, 6], [2, 8]], -14)
-    iota(nt0, [[-32, 6], [-66, 8]], 462)
-    lin(q2, q_, 2.0, 0.0)
-    lin(nv0, nv0, 1.0, q2)
-    ts(nt0, nt0, q2, Op.subtract)
-    lin(lc, lk, 32.0, 15.0)
-    ts(LC, v("r32", 0, 3), 0.0, Op.mult, lc, Op.add)
-    lin(k33, v("r32", 0, 8), 33.0, 0.0)
+    iota(nv0, [[16, 6], [1, 8]], -7)
+    iota(nt0, [[-16, 6], [-33, 8]], 231)
+    iota(nm, [[-16, 6], [0, 8]], -1)
+    lin(v("k48", 0, 96), v("k48", 0, 96), 1.0, q_)
+    ts(v("k48", 96), v("k48", 96), q_, Op.subtract)
+    lin(v("k48", 144, 192, 8), v("k48", 0, 48, 8), 1.0, float(A))
+    lin(v("cg", 44, 47), v("r32", 0, 3), 0.0, s8)
+    ts(LK, v("cg", 44, 47), -1.0, Op.mult, 7.0, Op.add)
+    ts(LC, v("cg", 44, 47), -16.0, Op.mult, 127.0, Op.add)
+    iota(k33, [[33, 8]], 0)
     fill(v("cum", 0, 16), 0.0)
     iota(lrf, [[64, 7], [-32, 2]], 62)
     iota(k64, [[64, 7], [0, 2]], 0)
-    ts(Lrev, lrf, q2, Op.subtract)
+    ts(Lrev, lrf, q_, Op.subtract, q_, Op.subtract)
     fill(v("rs0", 1, 448, 2), C + 1.0)
     fill(v("rs0", 448), C + 1.0)
     fill(v("rs1", 448), C + 1.0)
     iota(v("fr", A), [[2, A]], C + 2)
-    iota(v("slot"), [[1, A]], 257)
+    iota(v("slot"), [[1, A]], Y + 1)
     fill(v("dx", 896), 0.0)
     fill(v("pt", 384), 0.0)
     fill(v("ht", 384), 0.0)
@@ -314,44 +336,56 @@ def rank_program(g, core, T, topo):
         quant(piece("eq", b), piece("es", b), v("ez", 3 - b, 515 - b))
 
     cp(wl(0), v("par_i"), "v")
-    gather(tbl(1), ident, 0, SPLIT)
-    gather(tbl(2), tbl(1), 0, SPLIT)
-    wrap16(wl(1), v("sc"), tbl(2), -1.0, Op.add)
-    gather(tbl(4), tbl(2), 1, SPLIT)
+    calls[-1]["clear"] = 0
+    for i in range(4):
+        shared(tbl(i + 1), tbl(i), 0)
+    calls[-7]["clear"] = 100
     wrap16(wl(2), v("sc"), tbl(4), -1.0, Op.add)
-    gather(v("p8"), tbl(4), 2, SPLIT)
+    cp(v("p8"), by(tbl(4), wl(2)), "s")
     wrap16(wl(3), v("sc"), v("p8"), -1.0, Op.add)
-    gather(tbl(3), tbl(2), 0)
-    gather(tbl(5), tbl(4), 0)
-    gather(tbl(6), tbl(4), 1)
-    gather(tbl(7), tbl(3), 2)
     lin(v("t4b"), tbl(4), bit, 0.0)
-    for a, z in ((0, 8), (8, 14)):
-        tt(v("aw", 16 * a, 16 * z), by(v("t4b"), wl(2, a, z)), v("idb", 16 * a, 16 * z), Op.add)
-    gather(v("awm"), v("aw", 0, C), 3, SPLIT)
-    gather(v("aw", C, 2 * C), v("awm"), 3, SPLIT)
-    gather(v("p16"), v("p8"), 3)
-    wrap16(wl(4), v("sc"), v("p16"), -1.0, Op.add)
-    tt(v("un"), tbl(1), ident, Op.not_equal)
-    lin(v("ff", 0, C), v("un"), 65.0, 0.0)
-    fill(v("un", 0, C, 32), 0.0)
-    lin(v("ca"), ident, -1.0, 256.0)
-    scan(v("cb"), v("un"), v("ca"), 0.0, Op.mult, Op.max)
-    iota(lend, [[32, 7], [0, 2]], 31)
-    cp(v("ml", 0, 14), lend, "v")
-    lin(v("top"), by(v("cb"), v("ml", 0, 14)), -1.0, 256.0)
-    lin(q225, q_, 1.0, C + 1.0)
-    lin(spare, v("r32", 0, 14), 16.0, q225)
-    fill(v("t64"), 64.0)
+    tt(v("aw", 0, C), by(v("t4b"), wl(2)), v("cc"), Op.add)
+    shared(v("awm"), v("aw", 0, C), 3)
+    shared(v("aw", 232, 232 + C), v("awm"), 3)
+    wrap16(wl(1), v("sc2"), tbl(2), -1.0, Op.add)
+    for i, src, lst in ((5, 4, 0), (6, 2, 2), (7, 3, 2)):
+        cp(tbl(i), by(tbl(src), wl(lst)))
+    cp(v("p16"), by(v("p8"), wl(3)))
+    wrap16(wl(4), v("sc2"), v("p16"), -1.0, Op.add)
+    for a, z in ((0, 96), (96, 160), (160, C)):
+        tt(v("un", a, z), part(tbl(1), a, z), part(ident, a, z), Op.not_equal)
+    ts(v("un", 31, C, 32), v("un", 31, C, 32), 0.0, Op.mult)
+    scan(v("cb", C - 1, -1, -1), v("un", C - 1, -1, -1), v("tb", C - 1, -1, -1), 0.0, Op.mult, Op.max)
+    fill(v("ca"), 0.0)
+    fill(v("ca", 0, C, 32), 256.0)
+    scan(v("top"), v("ca"), v("cb"), 0.0, Op.add, Op.min)
+    tt(v("un", 31, C, 32), v("tb", C + 31, 2 * C, 32), v("tb", 31, C, 32), Op.not_equal)
+    lin(v("mk", 0, C), v("un"), 1.0, BASE)
+    iota(spare, [[16, 14]], C + 1)
+    lin(spare, spare, 1.0, q_)
+    fill(v("t64"), BASE)
     fill(v("ee"), 0.0)
-    lin(v("r2"), v("r1"), -BIG, FAR - 936 * BIG)
+    da, db, de = [piece("de", i, C) for i in range(3)]
+    lin(db, v("un"), 1.0, BASE)
+    doubled([da, db, da, db, v("dd", 0, C)], de, v("un"), db)
+    deep = BASE
+    lin(v("nd"), v("dd", 0, C), SLOPE * BIG, FAR - SLOPE * BIG * deep)
+    wrap16(dw, v("sc2"), v("dd", 0, C), -2.0, Op.mult)
 
     quant(v("uq"), v("us"), v("ut"))
-    for t in range(R):
+
+    def ahead_of(t):
+        fill(v("xy%d" % t, 4 * C, 4 * Y), 0.0)
+        if t == R:
+            return quant(v("vq"), v("vs"), v("vt"))
         lst, oq = piece("ul", t, 8), piece("upq", t)
-        call({"v": (216, lambda oq=oq, lst=lst: V.tensor_copy(ap(oq, dt.uint32), ap(by(v("uq"), lst), dt.uint32)))}, [by(v("uq"), lst)], [oq])
+        call({"v": (216, lambda: V.tensor_copy(ap(oq, dt.uint32), ap(by(v("uq"), lst), dt.uint32)))}, [by(v("uq"), lst)], [oq])
         cp(piece("ups", t), by(v("us"), lst))
-    quant(v("vq"), v("vs"), v("vt"))
+        if t:
+            for h in range(2):
+                fill(v("uw%d" % t, C + 232 * h, 232 + 232 * h), 0.0)
+
+    ahead_of(0)
 
     for t in range(R):
         n = str(t)
@@ -359,19 +393,20 @@ def rank_program(g, core, T, topo):
         hq, hsc = "hq" + n, "hsc" + n
         fo, fi = piece("fout", t, 24), piece("fin", t, 24)
         aq, asc = "aq" + n, "asc" + n
-        for h, (a, z) in enumerate(HALVES):
-            quant(piece(xq, h), piece(xsc, h), piece(xy, h, 512))
-            mm(6 + h, piece("upq", t), piece("ups", t), piece(xq, h), piece(xsc, h))
+        for h, (a, z, y) in enumerate(PARTS):
+            quant(v(xq, a, y), v(xsc, a, y), v(xy, 4 * a, 4 * y))
+            mm(6 + h, piece("upq", t), piece("ups", t), v(xq, a, y), v(xsc, a, y))
             scan(v("rr", 8 + a, 8 + z), v("cs1", a, z), bank(6 + h, 0, z - a), later if h else -3 * HUGE, Op.add, Op.max)
             tt(v("nn", a, z), bank(6 + h, 0, z - a), v("rr", 7 + a, 7 + z), Op.is_le)
-            scan(v("sel", a, z), v("nn", a, z), v("tp", a, z), 0.0, Op.mult, Op.max)
-        ts(v("l1", 0, 6), c6, v("sel", 127, 128), Op.subtract, v("sel", C - 1), Op.subtract)
-        send(t, "ax" + n, [(v(aq, 0, 128), v(xq, 0, 128)), (v(asc), v(xsc, 0, C))])
-        send(t, "ay" + n, [(v(aq, 128), v(xq, 128, C))])
-        cp(v("l2", 1, 17), by(v("aw"), v("l1", 0, 1)), "v")
-        cp(v(rs, 0, 448, 2), by(v("tb"), v("l2", 2, 16)), "s")
+            scan(v("sel", a, z), v("nn", a, z), v("tp", a, z), 0.0, Op.mult, Op.min)
+        send(t, "ax" + n, [(v(aq, 0, M), v(xq, 0, M)), (v(asc), v(xsc, 0, C))])
+        send(t, "ay" + n, [(v(aq, M), v(xq, M, C))])
         if t:
-            cp(v("gu"), by(uw, v("l1", 0, 6)), "v")
+            ts(v("l1", 0, 6), c6, v("sel", M - 1, M), Op.add, v("sel", C - 1), Op.add)
+            ts(v("l2", 1, 17), by(v("aw"), v("l1", 0, 1)), y224, Op.add)
+            for (a, z), q in zip(HALVES, "sv") if RSH else [((0, C), "s")]:
+                cp(v(rs, 2 * a, 2 * z, 2), by(v("tb"), v("l2", 2 + a // 16, 2 + z // 16)), q)
+            tt(v("gu"), by(uw, v("l1", 0, 6)), v("gt"), Op.add)
             scan(v("ab"), v("gu"), v("mz"), 0.0, Op.add, Op.mult)
             scan(v("cs"), v("ab", 0, A, 2), v("ab", 1, A, 2), BIG, Op.min, Op.max)
             ts(v("cw", 5, -1, -1), v("cs", 7, 48, 8), WHOLE, Op.add, WHOLE, Op.subtract)
@@ -379,31 +414,43 @@ def rank_program(g, core, T, topo):
             tt(v("sr", 16, 24), v("sr", 16, 24), k8, Op.add)
             ts(v("sr", 0, 8), v("sr", 16, 24), WHOLE, Op.add, WHOLE, Op.subtract)
         else:
-            tt(v("nn"), by(v("tb"), v("l2", 2, 16)), v("top"), Op.is_equal)
-            scan(v("cum", 16), v("nn"), v("nn"), 0.0, Op.add, Op.add)
+            ts(v("l1", 0, 1), c1b, v("sel", M - 1, M), Op.add, v("sel", C - 1), Op.add)
+            for h in range(2):
+                ts(v("l2", 36 + 16 * h, 52 + 16 * h), by(piece("aw", h, 232), v("l1", 0, 1)), y224, Op.add)
+                tt(piece("nn", h, 112), by(v("tb"), v("l2", 36 + 16 * h, 43 + 16 * h)), v("top", 0, C, 2), Op.is_equal)
+                ts(v("l2", h, 32 + h, 2), by(piece("aw", h, 232), v("l1", 0, 1)), y224, Op.add)
+            cp(v(rs, 0, 448, 2), by(v("tb"), v("l2", 0, 14)), "s")
+            scan(v("cum", 16), piece("nn", 0, 112), piece("nn", 1, 112), 0.0, Op.add, Op.add)
             tt(v("vv"), by(v("cum"), LC), nv0, Op.add)
             tt(v("fa"), by(v("cum"), LC), nt0, Op.is_ge)
             scan(v("cs"), v("vv"), v("fa"), 0.0, Op.max, Op.mult)
-            cp(v("cw"), v("cs", 7, 48, 8), "v")
-            lin(v("sr", 16, 24), v("cum", 15, 240, 32), -0.5, 0.0)
-            tt(v("sr", 0, 8), v("sr", 16, 24), k33, Op.add)
-        cp(v("fr", 0, A), by(v(rs), v("cw")), "v")
+            ts(v("cw"), v("cs", 7, 48, 8), 2.0, Op.mult)
+            tt(v("sr", 0, 8), k33, v("cum", 15, 128, 16), Op.subtract)
+            own_tree(k_)
+        cp(v("fr", 0, 64), by(v(rs), v("cw", 0, 4)), "v")
+        cp(v("fr", 64, A), by(v(rs), v("cw", 4, 6)), "s")
         wrap4(fo, v("f4"), v("fr", 0, A))
         listed = len(calls) - 1
         send(t, "al" + n, [(fi, fo)])
-        for h, (a, z) in enumerate(HALVES):
+        for h, (a, z, y) in enumerate(PARTS):
+            o = min(a, z - 128)
             for b in range(4):
-                mm(4 * h + b, piece("eq", b), piece("es", b), v(aq, z - 128, z), v(asc, z - 128, z))
-                cp(v("dx", 4 * a + b, 4 * z, 4), bank(4 * h + b, 128 + a - z, 128), DXQ)
+                mm(4 * h + b, piece("eq", b), piece("es", b), v(aq, o, z), v(asc, o, z))
+                cp(v("dx", 4 * a + b, 4 * z, 4), bank(4 * h + b, a - o, z - o), DXQ)
                 calls[-1]["soft"] = listed
         cp(v("pt", 0, 192), by(v("dx"), part(fi, 0, 12)), "v")
         cp(v("pt", 192, 384), by(v("dx"), part(fi, 12, 24)), "s")
+        gathered = len(calls) - 1
         quant(v("pq"), v("psc"), v("pt"))
         for b in range(4):
             mm(4 + b, piece("wq", b), piece("wsc", b), v("pq"), v("psc"))
-            relu(v("ht", b, 384, 4), bank(4 + b, 0, A), 0.03125, "vs"[b % 2])
+            relu(v("ht", b, 384, 4), bank(4 + b, 0, A), 0.03125, RELU[t][b])
         quant(v(hq, 0, 128), v(hsc, 0, 128), v("ht"))
-        send(t, "ah" + n, [(v(hq, 128), v(hq, 0, A)), (v(hsc, 128), v(hsc, 0, A))])
+        send(t, "ah" + n, [(v(hq, 128), v(hq, 0, A)), (v(hsc, 128, C), v(hsc, 0, A))])
+        made = len(calls)
+        ahead_of(t + 1)
+        for c in calls[made:]:
+            c["soft"] = {0: listed, 1: gathered, 2: made - 4}[AHEAD]
         ts(v("sr", 24, 31), v("sr", 1, 8), float(A), Op.min)
         tt(v("sr", 8, 15), v("sr", 0, 7), v("sr", 24, 31), Op.add)
         tt(v("vm"), by(v("sr", 8, 16), LK), nm, Op.add)
@@ -413,52 +460,47 @@ def rank_program(g, core, T, topo):
         cp(v("mr"), by(v("fr"), v("mw")))
         ts(v("mr4"), v("mr"), float(C), Op.min)
         wrap4(v("m4"), v("scn"), v("mr4"))
-        cp(v("xs"), by(v(xy, 0, 896), v("m4")))
+        for a, z in ((0, 12), (12, 24)) if XSH else [(0, 24)]:
+            cp(v("xs", 16 * a, 16 * z), by(v(xy, 0, 896), v("m4", a, z)))
         wrap16(v("m16"), v("scm"), v("mr"), -1.0, Op.add)
-        cp(v("hr", 0, C), ident)
+        if HRG:
+            iota(v("hr", 0, C), [[1, C]], 1)
+        else:
+            cp(v("hr", 0, C), ident)
         cp(by(v("hr"), v("m16")), v("slot"), "v")
         wrap4(v("hw"), v("sch"), v("hr", 0, C))
         if t:
-            ts(v("l1", 6, 7), c1b, v("sel", 127, 128), Op.subtract, v("sel", C - 1), Op.subtract)
+            ts(v("l1", 6, 7), c1b, v("sel", M - 1, M), Op.add, v("sel", C - 1), Op.add)
             lin(v("gd"), by(v("dd"), v("l1", 6, 7)), 2.0, 0.0)
             tt(cw3, v("gd", 1, 15), k64, Op.add)
             tt(v("mlf", 0, 14), cw3, dw, Op.add)
             cp(v("ml", 0, 14), v("mlf", 0, 14), "v")
         if t == 0:
-            wrap16(e1, v("sc2"), v(rs, 0, 448, 2), 0.0, Op.add)
+            wrap16(e1, v("sc"), v(rs, 0, 448, 2), 0.0, Op.add)
             tt(e2, e1, v("top", 0, C, 16), Op.is_equal)
             tt(e2, e2, spare, Op.mult)
             tt(e1, e1, e2, Op.max)
             ts(v("ml", 0, 14), e1, -1.0, Op.add)
-            cp(by(v("ff", 0, 2 * C), v("ml", 0, 14)), v("t64"), "v")
-            fa, fb, fc, fd = [piece("ff", i, C) for i in (2, 3, 4, 5)]
-            lin(fb, v("ff", 0, C), 1.0, DEEP)
-            o = doubled([fa, fb, fa, fb, fa], fc, fd, v("ff", 0, C), fb, DEEP)
-            ts(fb, fa, 64 * WHOLE, Op.add, 64 * WHOLE, Op.subtract)
-            scan(v("ca"), fa, fb, 0.0, Op.max, Op.subtract)
-            lin(v("dd", 0, C), fb, 1 / 64, 1 - (o + 16) / 64)
-            wrap16(dw, v("sc2"), v("dd", 0, C), -2.0, Op.mult)
+            cp(by(v("mk"), v("ml", 0, 14)), v("t64"), "v")
+            calls[-1]["urge"] = URGE
             tt(v("gd", 0, 7), v("sr", 1, 8), v("sr", 0, 7), Op.subtract)
-            lin(v("ee", 1, 15, 2), v("gd", 0, 7), -SLOPE * BIG, 0.0)
-            tt(v("yo"), by(v("ee"), Ltree), v("r2"), Op.add)
-            lin(fc, fb, SLOPE * BIG / 64, -FAR - SLOPE * BIG * (o + 16) / 64)
-            scan(v("oa"), fc, v("yo"), 0.0, Op.min, Op.add)
-            scan(v("nd"), fc, v("r2"), 0.0, Op.min, Op.add)
-            o = -16.0
+            lin(v("ee", 2, 16, 2), v("gd", 0, 7), -SLOPE * BIG, 0.0)
         if t == 1:
-            for a, z in PARTS:
-                tt(v("un", 16 * a, 16 * z), by(v(rs), v("ml", a, z)), part(ident, 16 * a, 16 * z), Op.not_equal)
-            lin(v("cb"), v("un"), 1.0, BASE)
-            o = doubled([v(x) for x in ("ca", "cb", "ca", "cb", "ca")], v("cc"), v("dg"), v("un"), v("cb"), BASE)
-            lin(v("ee"), v("gd"), -SLOPE * BIG / 2, 0.0)
-            tt(v("oa"), by(v("ee"), Ltree), v("nd"), Op.add)
+            tt(v("mk", 0, C), by(v(rs), v("ml", 0, 14)), ident, Op.not_equal)
+            lin(v("ee", 2, 16, 2), v("gd", 2, 16, 2), -SLOPE * BIG / 2, SLOPE * BIG * (deep - 1))
         if t < R - 1:
             nxt = "uw" + str(t + 1)
-            lin(v("idb"), v("ca"), -SLOPE, o * SLOPE + 1000)
-            scan(v(nxt, 0, C), v("idb"), v("r1"), 0.0, Op.max, Op.add)
-            lin(v("awm"), v("ca"), -SLOPE * BIG, o * SLOPE * BIG)
-            scan(v(nxt, C, 2 * C), v("awm"), v("oa"), 0.0, Op.min, Op.add)
+            if t:
+                lin(v("cb"), v("mk", 0, C), 1.0, BASE)
+            doubled([v(x) for x in ("ca", "cb", "ca", "cb", "ca")], v("dg"), v("mk", 0, C), v("cb") if t else None)
+            o = BASE
+            lin(v(nxt, 0, C), v("ca"), -SLOPE, o * SLOPE)
+            lin(v("awm"), v("ca"), -SLOPE * BIG, o * SLOPE * BIG - FAR)
+            plus(v(nxt, 232, 232 + C), v("awm"), v("nd"))
+            tt(v("gt"), by(v("ee"), part(Lq, 0, 6)), v("gs"), Op.add)
             cp(v("rs" + str(1 - t % 2), 1, 448, 2), by(v(rs), Lrev))
+            if LATE:
+                calls[-1]["soft"] = gathered
         else:
             ts(v("mlf", 14, 28), v("mlf", 0, 14), -2.0, Op.add)
             tt(v("mlf", 14, 28), v("mlf", 14, 28), k64, Op.max)
@@ -470,24 +512,29 @@ def rank_program(g, core, T, topo):
             lin(v("oa"), v("ca"), 1.0, -1.0)
             store("y", T.op[:], T.oa[0:128:16, :], v("oa"))
         for b in range(4):
-            mm(b, piece("eq", b), piece("es", b), v(hq, A), v(hsc, A))
-            tt(v(xy, 1024 + b, 1408, 4), bank(b, 128 - A, 128), v("xs", b, 384, 4), Op.add)
+            mm(b, piece("eq", b), piece("es", b), v(hq, A), v(hsc, A, C))
+            tt(v(xy, 4 * Y + b, 4 * (Y + A), 4), bank(b, 128 - A, 128), v("xs", b, 384, 4), Op.add)
         for (a, z), q in zip(CUTS, "vsvs"):
-            cp(v("xy" + str(t + 1), 16 * a, 16 * z), by(v(xy), v("hw", a, z)), q)
+            cp(v("xy" + str(t + 1), 16 * a, 16 * z), by(v(xy, 0, 4 * (Y + A)), v("hw", a, z)), q)
 
-    for h, (a, z) in enumerate(HALVES):
-        quant(piece("xq3", h), piece("xsc3", h), piece("xy3", h, 512))
-        mm(6 + h, v("vq"), v("vs"), piece("xq3", h), piece("xsc3", h))
-        cp(v("yo", a, z), bank(6 + h, 0, z - a), "sv"[h])
-    store("s", T.oc[:], ap(v("xq3", 0, C), dt.uint8), v("xq3"))
+    for h, (a, z, y) in enumerate(PARTS):
+        quant(v("xq3", a, y), v("xsc3", a, y), v("xy3", 4 * a, 4 * y))
+        mm(6 + h, v("vq"), v("vs"), v("xq3", a, y), v("xsc3", a, y))
+        cp(v("yo", a, z), bank(6 + h, 0, z - a), YQ[h])
+        store("s", T.oc[:, 4 * a:4 * z], ap(v("xq3", a, z), dt.uint8), v("xq3", a, z))
+        store("y", T.y[:, a:z], ap(v("yo", a, z)), v("yo", a, z))
     for k in range(4):
-        store("ys"[k % 2], T.osc[4 * k:4 * k + 4, :], T.xsc3[32 * k:32 * k + 4, 0:C], v("xsc3"))
-    store("y", T.y[:], T.yo[:], v("yo"))
+        store("ysss"[k], T.osc[4 * k:4 * k + 4, :], T.xsc3[32 * k:32 * k + 4, 0:C], v("xsc3", 0, C))
 
-    def place(rank_of, before):
+    def place(rank_of, before, spare_v):
         busy, plan = {}, {}
+        if before is ahead:
+            rank_of = [r + c.get("urge", 0) for r, c in zip(rank_of, calls)]
+            for i in reversed(range(len(calls))):
+                for d, lag in ahead[i]:
+                    rank_of[d] = max(rank_of[d], rank_of[i] + 1)
         for i in sorted(range(len(calls)), key=lambda i: -rank_of[i]):
-            ready = max([plan[d][1] + lag for d, lag in before[i]] + [0])
+            ready = max([plan[d][1] + lag for d, lag in before[i]] + [calls[i].get("not before", 0) * (before is ahead)])
             best = None
             for q, (time, f) in calls[i]["ways"].items():
                 at = ready
@@ -495,11 +542,11 @@ def rank_program(g, core, T, topo):
                     if at + time <= a:
                         break
                     at = max(at, z)
-                worth = at + time * (1 + LAZY * (q == "v"))
+                worth = at + time * (1 + spare_v * (q == "v"))
                 if best is None or worth < best[0]:
                     best = (worth, at, at + time, q)
             plan[i] = best[1:]
-            busy[best[3]] = sorted(busy[best[3]] + [best[1:3]])
+            busy[best[3]] = sorted(busy[best[3]] + [(best[1] - calls[i].get("clear", 0) * (before is ahead), best[2])])
         return plan
 
     ahead = [[(d, calls[d]["lag"]) for d in c["deps"]] + ([(c["soft"], SOFT)] if "soft" in c else []) for c in calls]
@@ -510,18 +557,26 @@ def rank_program(g, core, T, topo):
         for d, lag in ahead[i]:
             tail[d] = max(tail[d], tail[i])
             behind[d].append((i, lag))
-    def early(rank):
-        rank = [r + SOON * ("g" in c["ways"] and c["sem"] is not None) for r, c in zip(rank, calls)]
-        for i in reversed(range(len(calls))):
-            for d, lag in ahead[i]:
-                rank[d] = max(rank[d], rank[i] + 1)
-        return rank
+    plans = []
+    first = [c for c in calls if "clear" in c][0]
+    for first["clear"] in CLEAR:
+        for spare_v in LAZY:
+            plans.append(place(tail, ahead, spare_v))
+            for turn in range(TURNS):
+                back = place([plans[-1][i][1] for i in range(len(calls))], behind, spare_v)
+                plans.append(place([back[i][1] for i in range(len(calls))], ahead, spare_v))
+    def span(p):
+        order, total = sorted(p, key=lambda i: p[i][0]), 0
+        for slow, lists, link, more in SPEEDS:
+            free, end = {}, {}
+            for i in order:
+                c, q = calls[i], p[i][2]
+                at = max([end[d] + lag + more for d, lag in ahead[i]] + [free.get(q, 0)])
+                free[q] = end[i] = at + c["ways"][q][0] * (link if q == "link" else 1 if c["sem"] else lists if c["list"] else slow)
+            total += max(end.values()) / slow
+        return total
 
-    plans = [place(early(tail), ahead)]
-    for turn in range(TURNS):
-        back = place([plans[-1][i][1] for i in range(len(calls))], behind)
-        plans.append(place(early([back[i][1] for i in range(len(calls))]), ahead))
-    plan = min(plans, key=lambda p: max(e[1] for e in p.values()))
+    plan = min(plans, key=span)
 
     count = {q: 0 for q in "vspg"}
     clock = {q: {} for q in Q}
@@ -544,7 +599,7 @@ def rank_program(g, core, T, topo):
             if q != "g":
                 done.then_inc(T.sem[c["sem"][0]], 16)
             c["ev"] = c["sem"] + (dict(clock[q]),)
-    g.sync.wait_ge(T.sem.stored, 16 * 7)
+    g.sync.wait_ge(T.sem.stored, 16 * 9)
     g.wait_ge(T.sem.sent, nsent[0])
     for q in count:
         Q[q].wait_ge(T.sem["n" + q], count[q])

from concourse.bass import DstId, RemoteDMATransfer
from concourse.mybir import dt, AluOpType as Op, ActivationFunctionType as Act

C, A, R = 224, 96, 3
STEP = [1, 2, 4]
SOFT = 0
LAZY = (0.25, 0.5, 1.0, 2.0)
OVER = 700
SIDE = "www"
SHARE = "vs"
SLOW = 1.0
LATE, RSH, XSH, YQ = False, False, False, "vv"
URGE = 0
AHEAD = 2
CLEAR = (0,)
HRG = False
LATER = 0
SPEEDS = ((1.0, 1.0, 1.0, 0), (1.25, 1.1, 2.0, 20), (1.25, 1.5, 1.5, 0), (1.4, 1.4, 2.0, 40), (1.1, 1.3, 3.0, 0))
TURNS = 2
DXQ = "s"
GFILL = True
FUSE = False
HALVES = ((0, 128), (128, C))
RELU = ("vsvs", "vsvs", "vsvs")
M = 128
Y = M + 128
PARTS = ((0, M, M), (M, C, Y))
CUTS = ((0, 16), (16, 32), (32, 44), (44, 56))
F32, BF, I32, U16, MX, U8 = "float32", "bfloat16", "int32", "uint16", "float8_e4m3fn_x4", "uint8"
HUGE = 1.0e29
HOLD = 512.0
SLOPE, HALF = 127.0 / 64, 63.0 / 128
WHOLE = 12582912.0
BIG = 2048.0
BASE, DEEP, NEAR, FAR = 16.0, 4208.0, 16384.0, 33554432.0
LEVELS = ("sssss", "sssss", "sssss")
WAIT, ISSUE, START, WAKE, ROWNS, BYTENS, LOAD = 220, 700, 200, 300, 5, 0.04, 1350

SCRATCH = {"ps": ("psum", [128, 4096], F32)}
for _d, _l in (
        (I32, "par_i 14 ci 10 pc 9 ul_i 24"),
        (BF, "ut 512 vt 512 ez 520 eone 128 xy0 1536 xy1 1536 xy2 1536 xy3 1152 dx 912 pt 512 ht 512 xs 384 tp 224 nn 224 sel 224 "
             "tb 1792 p8 224 p16 224 t4b 224 pat 96 c16 224 c4 224 sc 224 sc2 224 cs1 224 rs0 640 rs1 640 fr 192 f4 96 "
             "mr 96 mr4 96 scm 96 scn 96 dd 240 de 896 mk 448 t64 224 un 224 ca 224 cb 224 cc 224 dg 224 top 224 cum 128"),
        (MX, "wq 512 uq 128 upq 384 vq 128 eq 512 pq 128 xq0 288 xq1 288 xq2 288 xq3 288 aq0 224 aq1 224 aq2 224 "
             "hq0 224 hq1 224 hq2 224"),
        (U8, "wsc 512 us 128 ups 384 vs 128 es 512 psc 128 xsc0 288 xsc1 288 xsc2 288 xsc3 288 "
             "asc0 224 asc1 224 asc2 224 hsc0 256 hsc1 256 hsc2 256"),
        (U16, "fout 72 fin 72 wl 80 cl 64 ul 24 l1 8 l2 68 cw 6 mw 6 m16 6 m4 24 hw 56 ml 28"),
        (F32, "cf 10 cg 64 r32 32 aw 464 awm 224 uw1 464 uw2 464 rr 232 gu 96 mz 96 ab 96 ee 16 gd 16 "
              "nd 224 gs 96 gt 96 k48 192 vv 48 fa 48 cs 48 vm 48 fl 48 cm 48 sr 32 hr 424 slot 96 sch 224 k14 126 mlf 28 oa 224 yo 224")):
    _w = _l.split()
    for _i in range(0, len(_w), 2):
        SCRATCH[_w[_i]] = ("sbuf", [128, int(_w[_i + 1])], _d)

SEMAPHORES = (["nv", "ns", "np", "ng", "ld_par", "ld_x", "ld_u", "ld_w", "ld_s", "ld_v", "stored", "sent"]
              + [n + str(t) for n in ("ax", "ay", "al", "ah") for t in range(R)])


def v(name, a=0, z=None, s=1):
    return (name, a, SCRATCH[name][1][1] if z is None else z, s)


def by(win, lst):
    return win + (lst,)


def width(x):
    return 16 * width(x[4]) if len(x) > 4 else len(range(*x[1:4]))


def bank(b, a, z):
    return ("ps", 512 * b + a, 512 * b + z, 1)


def rank_program(g, core, T, topo):
    rank = T.rank_of(core)
    if rank is None:
        return
    V, S, P = g.vector, g.scalar, g.tensor
    calls, seen = [], {}

    def ap(x, cast=None):
        if not isinstance(x, tuple):
            return x
        a = T[x[0]][:, x[1]:(x[2] if x[2] >= 0 else None):x[3]] if x[3] != 1 else T[x[0]][:, x[1]:x[2]]
        if cast:
            a = a.bitcast(cast)
        return a.indirect(ap(x[4])) if len(x) > 4 else a

    def call(ways, rd, wr, lag=WAIT, after=(), sem=None):
        me, deps = len(calls), set(after)
        rd = [x for x in rd if isinstance(x, tuple)]
        rd += [x[4] for x in rd + wr if len(x) > 4]
        for x, w in [(x, False) for x in rd] + [(x, True) for x in wr]:
            cols = set(range(*x[1:4]))
            if x[0] == "ps":
                cols, w = {x[1] // 512}, True
            deps |= {o for c, ow, o in seen.setdefault(x[0], []) if (w or ow) and o != me and c & cols}
            seen[x[0]].append((cols, w, me))
        calls.append({"ways": ways, "deps": deps, "lag": lag, "sem": sem, "list": any(len(x) > 4 for x in rd + wr)})
        return me

    def ns(out, ins, q="v", both=False):
        n = width(out)
        if len(out) > 4:
            return 50 + 3.2 * n
        if any(len(x) > 4 for x in ins):
            return (50 if q == "v" else 65) + 1.3 * n
        if q == "v" and all(x[0] != "ps" and SCRATCH[x[0]][2] in (BF, U16) for x in [out] + ins):
            n = n / 2
        return 0.83 * max(64, n * (2 if both else 1))

    def ts(out, a, s1, o0, s2=None, o1=None):
        f = (lambda: V.tensor_scalar(ap(out), ap(a), ap(s1), None, o0)) if o1 is None else (
            lambda: V.tensor_scalar(ap(out), ap(a), ap(s1), ap(s2), o0, o1))
        call({"v": (ns(out, [a]), f)}, [a, s1, s2], [out])

    def tt(out, a, b, o):
        call({"v": (ns(out, [a, b], both=a[0] != "ps"), lambda: V.tensor_tensor(ap(out), ap(a), ap(b), o))}, [a, b], [out])

    def scan(out, a, b, init, o0, o1):
        call({"v": (ns(out, [a, b]), lambda: V.tensor_tensor_scan(ap(out), ap(a), ap(b), ap(init), o0, o1))}, [a, b, init], [out])

    def cp(out, a, qs="vs"):
        ways = {"v": (ns(out, [a]), lambda: V.tensor_copy(ap(out), ap(a))),
                "s": (ns(out, [a], "s"), lambda: S.activation(ap(out), ap(a), Act.Copy))}
        call({q: ways[q] for q in qs}, [a], [out])

    def lin(out, a, scale, bias, qs="vs"):
        ways = {"v": (ns(out, [a]), lambda: V.tensor_scalar(ap(out), ap(a), ap(scale), ap(bias), Op.mult, Op.add)),
                "s": (ns(out, [a], "s"), lambda: S.activation(ap(out), ap(a), Act.Identity, bias=ap(bias), scale=ap(scale)))}
        call({q: ways[q] for q in qs}, [a, scale, bias], [out])

    def relu(out, a, scale, qs="vs"):
        ways = {"v": (ns(out, [a]), lambda: V.tensor_scalar(ap(out), ap(a), 0.0, scale, Op.max, Op.mult)),
                "s": (ns(out, [a], "s"), lambda: S.activation(ap(out), ap(a), Act.Relu, scale=scale))}
        call({q: ways[q] for q in qs}, [a], [out])

    def iota(out, pat, base, cm=0):
        kw = {} if SCRATCH[out[0]][2] == I32 else {"allow_small_or_imprecise_dtypes": True}
        call({"g": (180 + 2.3 * width(out), lambda: g.iota(ap(out), pat, base, cm, **kw))}, [], [out])

    def fill(out, x):
        ways = {"v": (ns(out, []), lambda: V.memset(ap(out), x))}
        if x == int(x) and GFILL:
            ways["g"] = (180 + 2.3 * width(out), lambda: g.iota(ap(out), [[0, width(out)]], int(x), 0, allow_small_or_imprecise_dtypes=True))
        call(ways, [], [out])

    def quant(q, s, a):
        call({"v": (12 + 0.22 * width(a), lambda: V.quantize_mx(ap(q), ap(s), ap(a)))}, [a], [q, s])

    def mm(b, lq, ls, rq, rs):
        out = bank(b, 0, width(rq))
        call({"p": (0.6 * (width(rq) + 16), lambda: P.matmul_mx(ap(out), ap(lq), ap(ls), ap(rq), ap(rs), True, True))},
             [lq, ls, rq, rs], [out])

    def load(q, out, src, sem, lag, cast=None):
        call({q: (60, lambda: Q[q].dma_start(ap(out, cast), src))}, [], [out], lag, sem=(sem, 16))

    def store(q, dst, src, rd):
        call({q: (60, lambda: Q[q].dma_start(dst, src))}, [rd], [], LOAD, sem=("stored", 0))

    nsent = [0]

    def send(t, sem, pairs):
        peer = T.cores[rank ^ STEP[t]]
        rid, pid, se = topo.addr(peer)
        ids, time = [], 0
        for out, a in pairs:
            cast = dt.uint8 if SCRATCH[a[0]][2] == MX else None
            ids.append(call({"g": (ISSUE, lambda out=out, a=a, cast=cast: g.remote_dma(
                ap(out, cast), ap(a, cast), T.sem[sem], T.sem.sent, pid, rid, topo.mask(core, peer)))}, [a], [], START, sem=("sent", 0)))
            nsent[0] += len(topo.engines(core, peer))
            time = max(0, time - OVER * (sem[1] == "h")) + 16 * (ROWNS + BYTENS * width(a) * {MX: 4, U8: 1, U16: 2}[SCRATCH[a[0]][2]])
        call({"link": (time, None)}, [], [o for o, a in pairs], WAKE, ids, (sem, len(pairs) * len(topo.engines(peer, core))))

    def send_one(t, sem, pairs):
        peer = T.cores[rank ^ STEP[t]]
        rid, pid, se = topo.addr(peer)
        eng = topo.engines(core, peer)
        k = len(eng) // len(pairs)

        def go():
            return g.remote_dma_fused([RemoteDMATransfer(
                dst_ids=[DstId(rid=rid, pnc=pid)], dma_engine_mask=sum(1 << e for e in eng[k * i:k * i + k]), remote_sem=T.sem[sem],
                src=ap(a, dt.uint8 if SCRATCH[a[0]][2] == MX else None), dst=ap(out, dt.uint8 if SCRATCH[a[0]][2] == MX else None))
                for i, (out, a) in enumerate(pairs)], local_sem=T.sem.sent)
        me = call({"g": (ISSUE, go)}, [a for o, a in pairs], [], START, sem=("sent", 0))
        nsent[0] += k * len(pairs)
        call({"link": (128 // k * (ROWNS + BYTENS * 128), None)}, [], [o for o, a in pairs], WAKE, [me], (sem, k * len(pairs)))

    Q = {"v": V, "s": S, "p": P, "g": g, "y": g.sync}

    def tbl(i):
        return v("tb", C * i, C * i + C)

    def wl(i, a=0, z=14):
        return v("wl", 16 * i + a, 16 * i + z)

    def part(x, a, z):
        return (x[0], x[1] + a * x[3], x[1] + z * x[3], x[3])

    def shared(out, win, i):
        for (a, z), q in zip(HALVES, SHARE):
            cp(part(out, a, z), by(win, wl(i, a // 16, z // 16)), q)

    ident = tbl(0)
    q_, q1, bit, nb, s8, k_, h_, kq, kq1, hh = [v("cf", i, i + 1) for i in range(10)]
    m16, m4, off4, z0, nk32, c1, c1b, y224, nq, lk, lc, q225, later = [v("cg", i, i + 1) for i in range(13)]
    c6, k8, k33, ktree = v("cg", 16, 22), v("cg", 24, 32), v("cg", 32, 40), v("cg", 48, 64)
    Lq, Lh, Lrev, Ltree = [v("cl", 14 * i, 14 * i + 14) for i in range(4)]
    LC, LK = v("cl", 56, 59), v("cl", 60, 63)
    n48, nv0, nt0, nm = [v("k48", 48 * i, 48 * i + 48) for i in range(4)]
    lrf, k64, dw, cw3, spare, e1, e2, lend, ltr = [v("k14", 14 * i, 14 * i + 14) for i in range(9)]

    def wrap16(out, buf, src, s2, o1):
        n = width(src)
        scan(part(buf, 0, n), v("c16", 0, n), src, 0.0, Op.mult, Op.max)
        ts(out, (buf[0], buf[1] + 15, buf[1] + n, 16), m16, Op.mult, s2, o1)

    def wrap4(out, buf, src):
        n = width(src)
        scan(part(buf, 0, n), v("c4", 0, n), src, 0.0, Op.mult, Op.max)
        ts(out, (buf[0], 3, n, 4), m4, Op.mult, off4, Op.add)

    def plus(out, a, b):
        scan(out, a, b, FAR, Op.min, Op.add)

    def doubled(outs, far, src, own=None):
        for i, out in enumerate(outs):
            lin(far, by(src, wl(i)), 1.0, 0.0 if own else -BASE, "s")
            plus(out, far, own or src)
            src, own = out, None

    def piece(name, b, n=128):
        return v(name, n * b, n * b + n)

    load("y", v("par_i"), T.par[:], "ld_par", LOAD)
    load("y", v("ut"), T.u[:], "ld_u", LOAD + 450)
    load("y", v("xy0", 0, 896), T.x[:], "ld_x", LOAD + 1200)
    load("y", v("wq"), T.wc[:], "ld_w", LOAD + 2000, dt.uint8)
    load("y", v("wsc"), T.ws[:], "ld_s", LOAD + 2000)
    load("y", v("vt"), T.v[:], "ld_v", LOAD + 2000)
    for i in range(1, 6):
        calls[i]["soft"] = i - 1

    iota(v("pc"), [[4, 3], [1, 3]], 15, 1)
    iota(v("r32"), [[1, 32]], 0)
    iota(ident, [[1, C]], 1)
    calls[-1]["soft"] = len(calls) - 2
    calls[-2]["soft"] = len(calls) - 3
    ts(v("ci", 0, 2), v("pc", 1, 3), 15, Op.bitwise_and)
    cp(v("cf", 0, 2), v("ci", 0, 2), "v")
    for a, z, src, sh, m in [(2, 4, (1, 8, 6), 3, 1), (4, 5, (1, 2), 0, 7), (5, 6, (0, 1), 1, 7), (6, 7, (0, 1), 0, 1),
                             (7, 9, (1, 5, 3), 2, 3), (9, 10, (1, 2), 0, 3)]:
        ts(v("ci", a, z), v("pc", *src), sh, Op.logical_shift_right, m, Op.bitwise_and)
        if a >= 5:
            calls[-1]["not before"] = LATER
    cp(v("cf", 2, 5), v("ci", 2, 5), "v")
    cp(v("cf", 5, 10), v("ci", 5, 10), "v")
    for a, at, nxt in ((0, q_, q1), (16, kq, kq1)):
        ts(v("pat", 32 + a, 48 + a), v("r32", 0, 16), at, Op.not_equal)
        ts(v("pat", 64 + a, 80 + a), v("r32", 0, 16), nxt, Op.is_equal, HOLD - 1, Op.mult)
        tt(v("pat", a, a + 16), v("pat", 32 + a, 48 + a), v("pat", 64 + a, 80 + a), Op.add)
    ts(Lq, v("r32", 0, 14), 0.0, Op.mult, q_, Op.add)
    ts(Lh, v("r32", 0, 14), 0.0, Op.mult, hh, Op.add)
    for a, z in HALVES:
        cp(v("c16", a, z), by(v("pat", 0, 16), part(Lq, 0, (z - a) // 16)))
    cp(v("c4"), by(v("pat", 16, 32), Lh))
    lin(m16, v("pat", 47, 48), 1 / HOLD - 1, 1.0)
    lin(m4, v("pat", 51, 52), 4 / HOLD - 4, 4.0)
    lin(off4, hh, 1.0, -4.0)
    lin(c1, k_, 32.0, 100.0)
    lin(c1, h_, C + 8.0, c1)
    lin(c6, v("r32", 0, 6), 0.0, c1)
    lin(nq, q_, SLOPE, 80 * SLOPE + HALF)
    iota(v("gt"), [[0, 6], [1, 16]], 0)
    lin(v("gs", 1, A, 2), v("gt", 1, A, 2), -32.0, 32.0)
    lin(v("gs", 0, A, 2), v("gt", 0, A, 2), 32 * BIG, 0.0)
    lin(v("gs", 0, A, 16), v("r32", 0, 6), -16 * SLOPE, nq)
    for h in range(2):
        fill(v("aw", C + 232 * h, 232 + 232 * h), 0.0)
    fill(v("dd", C), 0.0)
    for a, s, x in ((1, 2, BIG), (0, 2, 1 / BIG), (0, 16, 1.0), (15, 16, 0.0)):
        fill(v("mz", a, A, s), x)
    lin(k8, v("r32", 0, 8), 64 / SLOPE, 0.0)
    lin(y224, s8, float(C), -1.0)
    lin(v("cc"), ident, nb, 0.0)
    fill(v("cs1"), 0.0)

    def own_tree(k):
        lin(nk32, k, 32.0, 101.0)
        lin(c1b, k, 32.0, 100.0)
        ts(v("cg", 40, 41), k, M / 32, Op.is_lt, -100.0, Op.mult)
        ts(v("cg", 41, 42), k, M / 32, Op.is_ge, -100.0, Op.mult)
        lin(later, v("cg", 40, 41), -HUGE / 25, -3 * HUGE)
        for h, (a, z, y) in enumerate(PARTS):
            ts(v("tp", a, z), part(ident, a, z), nk32, Op.subtract, v("cg", 40 + h, 41 + h), Op.max)
        ts(v("cs1", 0, C, 32), v("r32", 0, 7), k, Op.is_equal, -3 * HUGE, Op.mult)
        ts(v("cs1", 31, C, 32), v("r32", 0, 7), k, Op.is_equal, HUGE, Op.mult)

    own_tree(s8)
    fill(v("rr", 0, 8), 0.0)
    fill(v("sr", 8, 16), 0.0)
    iota(v("ul_i"), [[1, 3], [16, 8]], 0)
    cp(v("ul"), v("ul_i"), "v")
    iota(n48, [[16, 6], [0, 8]], 0)
    iota(nv0, [[16, 6], [1, 8]], -7)
    iota(nt0, [[-16, 6], [-33, 8]], 231)
    iota(nm, [[-16, 6], [0, 8]], -1)
    lin(v("k48", 0, 96), v("k48", 0, 96), 1.0, q_)
    ts(v("k48", 96), v("k48", 96), q_, Op.subtract)
    lin(v("k48", 144, 192, 8), v("k48", 0, 48, 8), 1.0, float(A))
    lin(v("cg", 44, 47), v("r32", 0, 3), 0.0, s8)
    ts(LK, v("cg", 44, 47), -1.0, Op.mult, 7.0, Op.add)
    ts(LC, v("cg", 44, 47), -16.0, Op.mult, 127.0, Op.add)
    iota(k33, [[33, 8]], 0)
    fill(v("cum", 0, 16), 0.0)
    iota(lrf, [[64, 7], [-32, 2]], 62)
    iota(k64, [[64, 7], [0, 2]], 0)
    ts(Lrev, lrf, q_, Op.subtract, q_, Op.subtract)
    fill(v("rs0", 1, 448, 2), C + 1.0)
    fill(v("rs0", 448), C + 1.0)
    fill(v("rs1", 448), C + 1.0)
    iota(v("fr", A), [[2, A]], C + 2)
    iota(v("slot"), [[1, A]], Y + 1)
    fill(v("dx", 896), 0.0)
    fill(v("pt", 384), 0.0)
    fill(v("ht", 384), 0.0)
    fill(v("eone"), 1.0)
    fill(v("ez"), 0.0)
    call({"g": (385, lambda: g.affine_select(ap(v("ez", 3, 515, 4)), ap(v("eone")), [[-1, 128]], Op.is_equal, 0.0, 0, 1))},
         [v("eone")], [v("ez", 3, 515, 4)])
    for b in range(4):
        quant(piece("eq", b), piece("es", b), v("ez", 3 - b, 515 - b))

    cp(wl(0), v("par_i"), "v")
    calls[-1]["clear"] = 0
    for i in range(4):
        shared(tbl(i + 1), tbl(i), 0)
    calls[-7]["clear"] = 100
    wrap16(wl(2), v("sc"), tbl(4), -1.0, Op.add)
    cp(v("p8"), by(tbl(4), wl(2)), "s")
    wrap16(wl(3), v("sc"), v("p8"), -1.0, Op.add)
    lin(v("t4b"), tbl(4), bit, 0.0)
    tt(v("aw", 0, C), by(v("t4b"), wl(2)), v("cc"), Op.add)
    shared(v("awm"), v("aw", 0, C), 3)
    shared(v("aw", 232, 232 + C), v("awm"), 3)
    wrap16(wl(1), v("sc2"), tbl(2), -1.0, Op.add)
    for i, src, lst in ((5, 4, 0), (6, 2, 2), (7, 3, 2)):
        cp(tbl(i), by(tbl(src), wl(lst)))
    cp(v("p16"), by(v("p8"), wl(3)))
    wrap16(wl(4), v("sc2"), v("p16"), -1.0, Op.add)
    for a, z in ((0, 96), (96, 160), (160, C)):
        tt(v("un", a, z), part(tbl(1), a, z), part(ident, a, z), Op.not_equal)
    ts(v("un", 31, C, 32), v("un", 31, C, 32), 0.0, Op.mult)
    scan(v("cb", C - 1, -1, -1), v("un", C - 1, -1, -1), v("tb", C - 1, -1, -1), 0.0, Op.mult, Op.max)
    fill(v("ca"), 0.0)
    fill(v("ca", 0, C, 32), 256.0)
    scan(v("top"), v("ca"), v("cb"), 0.0, Op.add, Op.min)
    tt(v("un", 31, C, 32), v("tb", C + 31, 2 * C, 32), v("tb", 31, C, 32), Op.not_equal)
    lin(v("mk", 0, C), v("un"), 1.0, BASE)
    iota(spare, [[16, 14]], C + 1)
    lin(spare, spare, 1.0, q_)
    fill(v("t64"), BASE)
    fill(v("ee"), 0.0)
    da, db, de = [piece("de", i, C) for i in range(3)]
    lin(db, v("un"), 1.0, BASE)
    doubled([da, db, da, db, v("dd", 0, C)], de, v("un"), db)
    deep = BASE
    lin(v("nd"), v("dd", 0, C), SLOPE * BIG, FAR - SLOPE * BIG * deep)
    wrap16(dw, v("sc2"), v("dd", 0, C), -2.0, Op.mult)

    quant(v("uq"), v("us"), v("ut"))

    def ahead_of(t):
        fill(v("xy%d" % t, 4 * C, 4 * Y), 0.0)
        if t == R:
            return quant(v("vq"), v("vs"), v("vt"))
        lst, oq = piece("ul", t, 8), piece("upq", t)
        call({"v": (216, lambda: V.tensor_copy(ap(oq, dt.uint32), ap(by(v("uq"), lst), dt.uint32)))}, [by(v("uq"), lst)], [oq])
        cp(piece("ups", t), by(v("us"), lst))
        if t:
            for h in range(2):
                fill(v("uw%d" % t, C + 232 * h, 232 + 232 * h), 0.0)

    ahead_of(0)

    for t in range(R):
        n = str(t)
        xy, xq, xsc, rs, uw = "xy" + n, "xq" + n, "xsc" + n, "rs" + str(t % 2), t and v("uw" + n)
        hq, hsc = "hq" + n, "hsc" + n
        fo, fi = piece("fout", t, 24), piece("fin", t, 24)
        aq, asc = "aq" + n, "asc" + n
        for h, (a, z, y) in enumerate(PARTS):
            quant(v(xq, a, y), v(xsc, a, y), v(xy, 4 * a, 4 * y))
            mm(6 + h, piece("upq", t), piece("ups", t), v(xq, a, y), v(xsc, a, y))
            scan(v("rr", 8 + a, 8 + z), v("cs1", a, z), bank(6 + h, 0, z - a), later if h else -3 * HUGE, Op.add, Op.max)
            tt(v("nn", a, z), bank(6 + h, 0, z - a), v("rr", 7 + a, 7 + z), Op.is_le)
            scan(v("sel", a, z), v("nn", a, z), v("tp", a, z), 0.0, Op.mult, Op.min)
        send(t, "ax" + n, [(v(aq, 0, M), v(xq, 0, M)), (v(asc), v(xsc, 0, C))])
        send(t, "ay" + n, [(v(aq, M), v(xq, M, C))])
        if t:
            ts(v("l1", 0, 6), c6, v("sel", M - 1, M), Op.add, v("sel", C - 1), Op.add)
            ts(v("l2", 1, 17), by(v("aw"), v("l1", 0, 1)), y224, Op.add)
            for (a, z), q in zip(HALVES, "sv") if RSH else [((0, C), "s")]:
                cp(v(rs, 2 * a, 2 * z, 2), by(v("tb"), v("l2", 2 + a // 16, 2 + z // 16)), q)
            tt(v("gu"), by(uw, v("l1", 0, 6)), v("gt"), Op.add)
            scan(v("ab"), v("gu"), v("mz"), 0.0, Op.add, Op.mult)
            scan(v("cs"), v("ab", 0, A, 2), v("ab", 1, A, 2), BIG, Op.min, Op.max)
            ts(v("cw", 5, -1, -1), v("cs", 7, 48, 8), WHOLE, Op.add, WHOLE, Op.subtract)
            ts(v("sr", 16, 24), v("ab", 0, 16, 2), nq, Op.subtract, -1 / SLOPE, Op.mult)
            tt(v("sr", 16, 24), v("sr", 16, 24), k8, Op.add)
            ts(v("sr", 0, 8), v("sr", 16, 24), WHOLE, Op.add, WHOLE, Op.subtract)
        else:
            ts(v("l1", 0, 1), c1b, v("sel", M - 1, M), Op.add, v("sel", C - 1), Op.add)
            for h in range(2):
                ts(v("l2", 36 + 16 * h, 52 + 16 * h), by(piece("aw", h, 232), v("l1", 0, 1)), y224, Op.add)
                tt(piece("nn", h, 112), by(v("tb"), v("l2", 36 + 16 * h, 43 + 16 * h)), v("top", 0, C, 2), Op.is_equal)
                ts(v("l2", h, 32 + h, 2), by(piece("aw", h, 232), v("l1", 0, 1)), y224, Op.add)
            cp(v(rs, 0, 448, 2), by(v("tb"), v("l2", 0, 14)), "s")
            scan(v("cum", 16), piece("nn", 0, 112), piece("nn", 1, 112), 0.0, Op.add, Op.add)
            tt(v("vv"), by(v("cum"), LC), nv0, Op.add)
            tt(v("fa"), by(v("cum"), LC), nt0, Op.is_ge)
            scan(v("cs"), v("vv"), v("fa"), 0.0, Op.max, Op.mult)
            ts(v("cw"), v("cs", 7, 48, 8), 2.0, Op.mult)
            tt(v("sr", 0, 8), k33, v("cum", 15, 128, 16), Op.subtract)
            own_tree(k_)
        cp(v("fr", 0, 64), by(v(rs), v("cw", 0, 4)), "v")
        cp(v("fr", 64, A), by(v(rs), v("cw", 4, 6)), "s")
        wrap4(fo, v("f4"), v("fr", 0, A))
        listed = len(calls) - 1
        send(t, "al" + n, [(fi, fo)])
        for h, (a, z, y) in enumerate(PARTS):
            o = min(a, z - 128)
            for b in range(4):
                mm(4 * h + b, piece("eq", b), piece("es", b), v(aq, o, z), v(asc, o, z))
                cp(v("dx", 4 * a + b, 4 * z, 4), bank(4 * h + b, a - o, z - o), DXQ)
                calls[-1]["soft"] = listed
        cp(v("pt", 0, 192), by(v("dx"), part(fi, 0, 12)), "v")
        cp(v("pt", 192, 384), by(v("dx"), part(fi, 12, 24)), "s")
        gathered = len(calls) - 1
        quant(v("pq"), v("psc"), v("pt"))
        for b in range(4):
            mm(4 + b, piece("wq", b), piece("wsc", b), v("pq"), v("psc"))
            relu(v("ht", b, 384, 4), bank(4 + b, 0, A), 0.03125, RELU[t][b])
        quant(v(hq, 0, 128), v(hsc, 0, 128), v("ht"))
        send(t, "ah" + n, [(v(hq, 128), v(hq, 0, A)), (v(hsc, 128, C), v(hsc, 0, A))])
        made = len(calls)
        ahead_of(t + 1)
        for c in calls[made:]:
            c["soft"] = {0: listed, 1: gathered, 2: made - 4}[AHEAD]
        ts(v("sr", 24, 31), v("sr", 1, 8), float(A), Op.min)
        tt(v("sr", 8, 15), v("sr", 0, 7), v("sr", 24, 31), Op.add)
        tt(v("vm"), by(v("sr", 8, 16), LK), nm, Op.add)
        tt(v("fl"), by(v("sr", 0, 8), LK), n48, Op.is_le)
        scan(v("cm"), v("vm"), v("fl"), 0.0, Op.max, Op.mult)
        cp(v("mw"), v("cm", 7, 48, 8), "v")
        cp(v("mr"), by(v("fr"), v("mw")))
        ts(v("mr4"), v("mr"), float(C), Op.min)
        wrap4(v("m4"), v("scn"), v("mr4"))
        for a, z in ((0, 12), (12, 24)) if XSH else [(0, 24)]:
            cp(v("xs", 16 * a, 16 * z), by(v(xy, 0, 896), v("m4", a, z)))
        wrap16(v("m16"), v("scm"), v("mr"), -1.0, Op.add)
        if HRG:
            iota(v("hr", 0, C), [[1, C]], 1)
        else:
            cp(v("hr", 0, C), ident)
        cp(by(v("hr"), v("m16")), v("slot"), "v")
        wrap4(v("hw"), v("sch"), v("hr", 0, C))
        if t:
            ts(v("l1", 6, 7), c1b, v("sel", M - 1, M), Op.add, v("sel", C - 1), Op.add)
            lin(v("gd"), by(v("dd"), v("l1", 6, 7)), 2.0, 0.0)
            tt(cw3, v("gd", 1, 15), k64, Op.add)
            tt(v("mlf", 0, 14), cw3, dw, Op.add)
            cp(v("ml", 0, 14), v("mlf", 0, 14), "v")
        if t == 0:
            wrap16(e1, v("sc"), v(rs, 0, 448, 2), 0.0, Op.add)
            tt(e2, e1, v("top", 0, C, 16), Op.is_equal)
            tt(e2, e2, spare, Op.mult)
            tt(e1, e1, e2, Op.max)
            ts(v("ml", 0, 14), e1, -1.0, Op.add)
            cp(by(v("mk"), v("ml", 0, 14)), v("t64"), "v")
            calls[-1]["urge"] = URGE
            tt(v("gd", 0, 7), v("sr", 1, 8), v("sr", 0, 7), Op.subtract)
            lin(v("ee", 2, 16, 2), v("gd", 0, 7), -SLOPE * BIG, 0.0)
        if t == 1:
            tt(v("mk", 0, C), by(v(rs), v("ml", 0, 14)), ident, Op.not_equal)
            lin(v("ee", 2, 16, 2), v("gd", 2, 16, 2), -SLOPE * BIG / 2, SLOPE * BIG * (deep - 1))
        if t < R - 1:
            nxt = "uw" + str(t + 1)
            if t:
                lin(v("cb"), v("mk", 0, C), 1.0, BASE)
            doubled([v(x) for x in ("ca", "cb", "ca", "cb", "ca")], v("dg"), v("mk", 0, C), v("cb") if t else None)
            o = BASE
            lin(v(nxt, 0, C), v("ca"), -SLOPE, o * SLOPE)
            lin(v("awm"), v("ca"), -SLOPE * BIG, o * SLOPE * BIG - FAR)
            plus(v(nxt, 232, 232 + C), v("awm"), v("nd"))
            tt(v("gt"), by(v("ee"), part(Lq, 0, 6)), v("gs"), Op.add)
            cp(v("rs" + str(1 - t % 2), 1, 448, 2), by(v(rs), Lrev))
            if LATE:
                calls[-1]["soft"] = gathered
        else:
            ts(v("mlf", 14, 28), v("mlf", 0, 14), -2.0, Op.add)
            tt(v("mlf", 14, 28), v("mlf", 14, 28), k64, Op.max)
            cp(v("ml", 14, 28), v("mlf", 14, 28), "v")
            tt(v("un"), by(v(rs), v("ml", 0, 14)), ident, Op.is_equal)
            tt(v("ca"), by(v(rs), v("ml", 14, 28)), tbl(1), Op.subtract)
            tt(v("cb"), v("ca"), v("un"), Op.mult)
            tt(v("ca"), v("cb"), tbl(1), Op.add)
            lin(v("oa"), v("ca"), 1.0, -1.0)
            store("y", T.op[:], T.oa[0:128:16, :], v("oa"))
        for b in range(4):
            mm(b, piece("eq", b), piece("es", b), v(hq, A), v(hsc, A, C))
            tt(v(xy, 4 * Y + b, 4 * (Y + A), 4), bank(b, 128 - A, 128), v("xs", b, 384, 4), Op.add)
        for (a, z), q in zip(CUTS, "vsvs"):
            cp(v("xy" + str(t + 1), 16 * a, 16 * z), by(v(xy, 0, 4 * (Y + A)), v("hw", a, z)), q)

    for h, (a, z, y) in enumerate(PARTS):
        quant(v("xq3", a, y), v("xsc3", a, y), v("xy3", 4 * a, 4 * y))
        mm(6 + h, v("vq"), v("vs"), v("xq3", a, y), v("xsc3", a, y))
        cp(v("yo", a, z), bank(6 + h, 0, z - a), YQ[h])
        store("s", T.oc[:, 4 * a:4 * z], ap(v("xq3", a, z), dt.uint8), v("xq3", a, z))
        store("y", T.y[:, a:z], ap(v("yo", a, z)), v("yo", a, z))
    for k in range(4):
        store("ysss"[k], T.osc[4 * k:4 * k + 4, :], T.xsc3[32 * k:32 * k + 4, 0:C], v("xsc3", 0, C))

    def place(rank_of, before, spare_v):
        busy, plan = {}, {}
        if before is ahead:
            rank_of = [r + c.get("urge", 0) for r, c in zip(rank_of, calls)]
            for i in reversed(range(len(calls))):
                for d, lag in ahead[i]:
                    rank_of[d] = max(rank_of[d], rank_of[i] + 1)
        for i in sorted(range(len(calls)), key=lambda i: -rank_of[i]):
            ready = max([plan[d][1] + lag for d, lag in before[i]] + [calls[i].get("not before", 0) * (before is ahead)])
            best = None
            for q, (time, f) in calls[i]["ways"].items():
                at = ready
                for a, z in busy.setdefault(q, []):
                    if at + time <= a:
                        break
                    at = max(at, z)
                worth = at + time * (1 + spare_v * (q == "v"))
                if best is None or worth < best[0]:
                    best = (worth, at, at + time, q)
            plan[i] = best[1:]
            busy[best[3]] = sorted(busy[best[3]] + [(best[1] - calls[i].get("clear", 0) * (before is ahead), best[2])])
        return plan

    ahead = [[(d, calls[d]["lag"]) for d in c["deps"]] + ([(c["soft"], SOFT)] if "soft" in c else []) for c in calls]
    behind = [[] for c in calls]
    tail = [0.0] * len(calls)
    for i in reversed(range(len(calls))):
        tail[i] += min(w[0] for w in calls[i]["ways"].values()) + calls[i]["lag"]
        for d, lag in ahead[i]:
            tail[d] = max(tail[d], tail[i])
            behind[d].append((i, lag))
    plans = []
    first = [c for c in calls if "clear" in c][0]
    for first["clear"] in CLEAR:
        for spare_v in LAZY:
            plans.append(place(tail, ahead, spare_v))
            for turn in range(TURNS):
                back = place([plans[-1][i][1] for i in range(len(calls))], behind, spare_v)
                plans.append(place([back[i][1] for i in range(len(calls))], ahead, spare_v))
    def span(p):
        order, total = sorted(p, key=lambda i: p[i][0]), 0
        for slow, lists, link, more in SPEEDS:
            free, end = {}, {}
            for i in order:
                c, q = calls[i], p[i][2]
                at = max([end[d] + lag + more for d, lag in ahead[i]] + [free.get(q, 0)])
                free[q] = end[i] = at + c["ways"][q][0] * (link if q == "link" else 1 if c["sem"] else lists if c["list"] else slow)
            total += max(end.values()) / slow
        return total

    plan = min(plans, key=span)

    count = {q: 0 for q in "vspg"}
    clock = {q: {} for q in Q}
    for i in sorted(plan, key=lambda i: plan[i][0]):
        c, q = calls[i], plan[i][2]
        if q == "link":
            c["ev"] = c["sem"] + ({},)
            continue
        for sem, val, known in sorted([calls[d]["ev"] for d in c["deps"]], key=lambda e: (-len(e[2]), e[0], -e[1])):
            if clock[q].get(sem, 0) < val:
                Q[q].wait_ge(T.sem[sem], val)
                for k, x in list(known.items()) + [(sem, val)]:
                    clock[q][k] = max(clock[q].get(k, 0), x)
        done = c["ways"][q][1]()
        if c["sem"] is None:
            count[q] += 1
            done.then_inc(T.sem["n" + q], 1)
            c["ev"] = ("n" + q, count[q], dict(clock[q]))
        else:
            if q != "g":
                done.then_inc(T.sem[c["sem"][0]], 16)
            c["ev"] = c["sem"] + (dict(clock[q]),)
    g.sync.wait_ge(T.sem.stored, 16 * 9)
    g.wait_ge(T.sem.sent, nsent[0])
    for q in count:
        Q[q].wait_ge(T.sem["n" + q], count[q])
